import numpy as np, ml_dtypes
CORES = [48,51,52,55]
N = 4
BF = ml_dtypes.bfloat16
def gentries(a):
    return np.ascontiguousarray(a.reshape(8, 16, -1).transpose(0, 2, 1)).reshape(8, -1)
def gtable(e):
    e = np.asarray(e); return np.ascontiguousarray(e.reshape(8, -1, 16).transpose(0, 2, 1)).reshape(128, -1).astype(np.int32)
V, E, R, B = 1024, 512, 4, 4
W = N * V
def parts(rng):
    m = np.floor(rng.random((8, 16, W)) * rng.choice(np.array([2, 3, 6, 16]), (8, 1, W))).astype(np.int64)
    ring = rng.integers(0, W, (N, 8, R, V)); u = np.ascontiguousarray(np.argsort(rng.random((N, 8, B, V)), axis=-1)[..., :E])
    return m, ring, u, rng.integers(0, W, (N, 8, B, E))
def pack(m, ring, u, v):
    return {"m0": np.repeat(m.reshape(1, 128, W), N, axis=0).astype(BF), "ring0": np.ascontiguousarray(ring.reshape(N, 8 * R, V)).astype(np.int32),
            "eu": np.stack([gtable(a.reshape(8, -1)) for a in u]), "ev": np.stack([gtable(a.reshape(8, -1)) for a in v])}
def setup_inputs(rng):
    return pack(*parts(rng))
def setup_inputs_ties(rng):
    m, ring, u, v = parts(rng)
    for g in range(8):
        if g % 4 == 0:
            for k in range(R): ring[:, g, k] = ring[:, g, k // 2 * 2]
        if g % 4 == 1: ring[:, g] = ring[:, g, :1]
        if g % 4 == 2: m[g] = rng.integers(0, 16, (16, 3))[:, rng.integers(0, 3, W)]
        if g % 4 == 3: m[g] = rng.integers(0, 2, (16, W)) * rng.integers(0, 2, (1, W))
    return pack(m, ring, u, v)
def setup_inputs_after(rng):
    m, ring, u, v = parts(rng)
    u[:, 4:6] = np.take_along_axis(np.repeat(u[:, 4:6, :1], B, axis=2), np.argsort(rng.random((N, 2, B, E)), axis=-1), axis=-1)
    nodes = u + np.arange(N).reshape(N, 1, 1, 1) * V
    for q in range(N):
        o = (q + int(rng.integers(1, N))) % N
        v[q, ::2, 1:] = nodes[o, ::2, :-1]; v[q, 1::2] = nodes[o, 1::2]
    return pack(m, ring, u, v)
def setup_inputs_alike(rng):
    m, ring, u, v = parts(rng); own = np.arange(N).reshape(N, 1, 1) * V
    v[:, :2] = rng.integers(0, W, (N, 2, B, 1))
    for q in range(N): ring[q, 1] = rng.integers(0, V, (R, V)) + (q + int(rng.integers(1, N))) % N * V
    v[:, 2] = u[:, 2] + own
    ring[:, 3] = np.arange(V) + own
    hot = int(rng.integers(0, W)); ring[:, 4] = hot; m[4, :, hot] = rng.integers(1, 16, 16)
    ring[:, 5] = rng.integers(0, V, (N, R, V)) + own; v[:, 5] = rng.integers(0, V, (N, B, E)) + own
    ring[:, 6] = (rng.integers(V, W, (N, R, V)) + own) % W; v[:, 6] = (rng.integers(V, W, (N, B, E)) + own) % W
    u[:, 7] = np.arange(E); u[:, 7, 1] = np.arange(V - E, V)
    first = int(rng.integers(0, N)) * V; ring[:, 7] = rng.integers(0, V, (N, R, V)) + first; v[:, 7] = rng.integers(0, V, (N, B, E)) + first
    return pack(m, ring, u, v)
def setup_inputs_ends(rng):
    m, ring, u, v = parts(rng)
    m = 15 * (rng.random((8, 16, W)) < rng.choice(np.array([0.1, 0.5, 1.0]), (8, 1, W))).astype(np.int64); m[0] = 15; m[1] = 0
    m[2:4] = rng.integers(12, 15, (2, 16, 1)) + rng.integers(-1, 2, (2, 16, W)) * (rng.random((2, 16, W)) < np.array([1.0, 0.125]).reshape(2, 1, 1))
    mid = np.argsort(rng.random((N, 8, B, V - 2)), axis=-1)[..., :E - 2] + 1
    u = np.concatenate([np.full((N, 8, B, 1), V - 1), mid, np.zeros((N, 8, B, 1), np.int64)], axis=3)
    ends = np.concatenate([np.arange(N) * V, np.arange(N) * V + V - 1])
    ring[:, 5:] = rng.choice(ends, (N, 3, R, V)); v[:, 5:] = rng.choice(ends, (N, 3, B, E))
    return pack(m, ring, u, v)
def setup_inputs_spread(rng):
    m, ring, u, v = parts(rng)
    m = np.floor(16 * rng.random((8, 16, W)) * np.exp2(-rng.integers(0, 5, (8, 1, W)))).astype(np.int64)
    o = np.argsort(rng.random((8, W)), axis=-1)
    for g in range(8):
        ring[:, g] = o[g][np.minimum((W * rng.random((N, R, V)) ** 4).astype(np.int64), W - 1)]
        v[:, g] = o[g][np.minimum((W * rng.random((N, B, E)) ** 4).astype(np.int64), W - 1)]
    u = np.ascontiguousarray(np.argsort(rng.random((N, 8, B, V)) * np.exp2(3 * rng.random((N, 8, 1, V))), axis=-1)[..., :E])
    return pack(m, ring, u, v)
def check_inputs(d):
    bad = []; a = np.asarray(d["m0"]).astype(np.float32)
    if not np.all((a >= 0) & (a <= 15) & (a == np.floor(a))): bad.append("range of m0")
    if not np.all(a == a[:1]): bad.append("m0 alike on all ranks")
    for k, hi in (("ring0", W - 1), ("eu", V - 1), ("ev", W - 1)):
        if np.min(d[k]) < 0 or np.max(d[k]) > hi: bad.append("range of " + k)
    s = np.sort(np.stack([gentries(x) for x in d["eu"]]).reshape(N, 8, B, E), axis=-1)
    if np.any(s[..., 1:] == s[..., :-1]): bad.append("u distinct in a batch")
    return bad
def reference(m0, ring0, eu, ev):
    m = m0[0].astype(np.int64).reshape(8, 16, W); ring = ring0.astype(np.int64).reshape(N, 8, R, V).copy(); gi = np.arange(8)[:, None]
    us = np.stack([gentries(a) for a in eu]).astype(np.int64).reshape(N, 8, B, E); vs = np.stack([gentries(a) for a in ev]).astype(np.int64).reshape(N, 8, B, E)
    for b in range(B):
        new = m.copy()
        for q in range(N):
            u, v = us[q, :, b], vs[q, :, b]
            ids = np.take_along_axis(ring[q], np.broadcast_to(u[:, None, :], (8, R, E)), 2)
            mi = np.take_along_axis(m, ids.reshape(8, 1, R * E), 2).reshape(8, 16, R, E)
            mu = np.take_along_axis(m, u[:, None, :] + q * V, 2); mv = np.take_along_axis(m, v[:, None, :], 2)
            c = np.sum(mi * mv[:, :, None, :], axis=1)
            k = np.argmin(c, axis=1)
            np.put_along_axis(new, np.broadcast_to(u[:, None, :] + q * V, (8, 16, E)), np.clip(mu + mv - np.max(mi, axis=2), 0, 15), 2)
            ring[q][gi, k, u] = v
        m = new
    full = m.reshape(128, W)
    return {"ym": np.stack([full[:, q * V:(q + 1) * V] for q in range(N)]).astype(BF), "yr": ring.reshape(N, 8 * R, V).astype(np.float32)}

@@ -1,0 +1,602 @@
+from concourse.bass import DstId, RemoteDMATransfer
+from concourse.mybir import AluOpType as A, ActivationFunctionType as F
+
+NB, V, E, R = 4, 1024, 512, 4
+BF, F32, I32, U16 = "bfloat16", "float32", "int32", "uint16"
+LAG, FAR, SLACK = 0.12, 3.7, 0.03
+
+SCRATCH = {
+    "OB": ("sbuf", [128, V + NB * E], BF),
+    "RW": ("sbuf", [128, V + NB * E], F32),
+    "RI": ("sbuf", [128, V], I32),
+    "EUI": ("sbuf", [128, 128], I32), "EVI": ("sbuf", [128, 128], I32),
+    "EU16": ("sbuf", [128, 128], U16), "EV16": ("sbuf", [128, 128], U16), "EVF": ("sbuf", [128, 128], F32),
+    "MX": ("sbuf", [128, 2048], BF), "PR": ("sbuf", [128, 1536], BF),
+    "SG": ("sbuf", [128, 512], BF), "ON": ("sbuf", [128, 128], F32),
+    "GR": ("sbuf", [128, 512], F32), "DF": ("sbuf", [128, 128], F32),
+    "VW": ("sbuf", [128, 512], F32),
+    "YB": ("sbuf", [128, V], BF), "YR": ("sbuf", [128, V], F32),
+    "ONE": ("sbuf", [128, 144], BF), "ID": ("sbuf", [128, 128], BF), "NI": ("sbuf", [128, 128], BF), "IF": ("sbuf", [128, 128], F32),
+    "ZL": ("sbuf", [128, 144], BF), "ZB": ("sbuf", [128, 144], BF), "RQ": ("sbuf", [128, 16], F32), "QH": ("sbuf", [128, 16], F32),
+    "LO": ("sbuf", [128, 256], BF), "PZ": ("sbuf", [128, NB * E], BF),
+    "LE": ("sbuf", [128, 4, 128], F32), "LV": ("sbuf", [128, 4, 128], F32), "RD": ("sbuf", [128, 4, 128], F32),
+    "BO": ("sbuf", [128, 128], BF), "B1": ("sbuf", [128, 128], BF),
+    "LD": ("sbuf", [128, 3, 128], BF), "LS": ("sbuf", [128, 4, 128], BF), "CD": ("sbuf", [128, 3, 128], BF),
+    "C4": ("sbuf", [128, 12], F32), "CK": ("sbuf", [128, 4], F32),
+    "RS": ("sbuf", [128, 1024], BF),
+    "PC": ("sbuf", [128, 8], I32), "CF": ("sbuf", [128, 8], F32),
+    "W0": ("psum", [128, 512], F32), "W1": ("psum", [128, 512], F32), "LX": ("psum", [128, 512], F32), "LN": ("psum", [128, 512], F32),
+    "DA0": ("psum", [128, 512], F32), "DA1": ("psum", [128, 512], F32), "CX0": ("psum", [128, 512], F32), "CX1": ("psum", [128, 512], F32),
+}
+for _c in range(4):
+    SCRATCH["TB%d" % _c] = ("sbuf", [128, 4 * V], BF)
+    SCRATCH["OF%d" % _c] = ("sbuf", [128, 128], U16)
+    SCRATCH["LW%d" % _c] = ("sbuf", [128, 96], U16)
+    SCRATCH["LL%d" % _c] = ("sbuf", [128, V + E], BF)
+for _c in range(2):
+    SCRATCH["MU%d" % _c] = ("sbuf", [128, 512], BF)
+    SCRATCH["MV%d" % _c] = ("sbuf", [128, 512], BF)
+    SCRATCH["MT%d" % _c] = ("sbuf", [128, 2048], BF)
+NDMA = 20
+SEMAPHORES = ["cv", "cs", "cp", "cg", "sent"] + ["arr%d" % b for b in range(NB)] + ["d%d" % i for i in range(NDMA)]
+
+
+def rank_program(g, core, T, topo):
+    rank = T.rank_of(core)
+    if rank is None:
+        return
+    peers = [c for c in T.cores if c != core]
+    own = rank * V
+    QU = {"v": g.vector, "s": g.scalar, "p": g.tensor, "g": g, "y": g.sync}
+    known = {q: {} for q in QU}
+    hold, marks, prog = [None], {}, []
+    total, waited, acc, ndma, clks = {}, {}, {}, [0], {}
+    psum = {n for n in SCRATCH if SCRATCH[n][0] == "psum"}
+
+    def wait(q, rec):
+        sem, val, clk = rec
+        if known[q].get(sem, 0) >= val:
+            return
+        QU[q].wait_ge(T.sem[sem], val)
+        waited[sem] = max(waited.get(sem, 0), val)
+        for s, x in clk.items():
+            known[q][s] = max(known[q].get(s, 0), x)
+        known[q][sem] = max(known[q].get(sem, 0), val)
+
+    def order(q, reads, writes, dma=False, waw=False):
+        deps = []
+        for mode, regs in ((0, reads), (1, writes)):
+            for (b, c0, c1) in regs:
+                for (aq, aw, a0, a1, rec) in acc.get(b, []):
+                    ps = b in psum
+                    hit = a1 > c0 and c1 > a0
+                    if not ps and not hit:
+                        continue
+                    same = aq == q and not dma
+                    if mode == 0 and ((aw and hit) or (ps and not same)):
+                        deps.append(rec)
+                    elif mode == 1 and (not same or (aw and waw)):
+                        deps.append(rec)
+        for rec in sorted(deps, key=lambda x: -sum(x[2].values()) - x[1]):
+            wait(q, rec)
+
+    def note(q, rec, reads, writes):
+        for w, regs in ((False, reads), (True, writes)):
+            for (b, c0, c1) in regs:
+                lst = acc.setdefault(b, [])
+                if w and b not in psum:
+                    lst[:] = [x for x in lst if not (c0 <= x[2] and x[3] <= c1)]
+                lst.append((q, w, c0, c1, rec))
+
+    def emit(k):
+        q, reads, writes = k["q"], k["reads"], k["writes"]
+        if k["kind"] == "op":
+            order(q, reads, writes, waw=k["waw"])
+            sem = "c" + q
+            k["fn"](QU[q]).then_inc(T.sem[sem], 1)
+            total[sem] = total.get(sem, 0) + 1
+            note(q, (sem, total[sem], dict(known[q])), reads, writes)
+        elif k["kind"] == "dma":
+            order(q, reads, writes, dma=True)
+            QU[q].dma_start(*k["fn"]).then_inc(T.sem[k["sem"]], 16)
+            total[k["sem"]] = 16 * k["n"]
+            clk = clks.setdefault(k["sem"], [0, {}])
+            for s, x in known[q].items():
+                clk[1][s] = max(clk[1].get(s, 0), x)
+            clk[0] += 1
+            if clk[0] == k["n"]:
+                note("dma" + k["sem"], (k["sem"], total[k["sem"]], clk[1]), reads, writes)
+        else:
+            if k["kind"] == "send":
+                order("g", reads, [])
+            k["fn"]()
+
+    def item(**k):
+        k["hold"] = hold[0]
+        prog.append(k)
+
+    def here():
+        return len(prog) - 1
+
+    def op(q, fn, reads, writes, waw=False, n=128, t=None):
+        item(q=q, kind="op", fn=fn, reads=reads, writes=writes, waw=waw, time=t or (0.38 if q == "g" else 0.055 + 0.00083 * max(n, 64)), lag=LAG)
+
+    def dmas(parts, reads, writes, lag=2.2):
+        sem = "d%d" % ndma[0]
+        ndma[0] += 1
+        for q, out, in_ in parts:
+            item(q=q, kind="dma", fn=(out, in_), reads=reads, writes=writes, time=0.06, lag=lag, sem=sem, n=len(parts))
+
+    def plan():
+        n = len(prog)
+        after, then = [set() for _ in range(n)], [[] for _ in range(n)]
+        seen, bank = {}, {}
+        for j, k in enumerate(prog):
+            regs = [(0,) + r for r in k["reads"]] + [(1,) + r for r in k["writes"]]
+            if k["hold"] is not None and prog[k["hold"]]["q"] == k["q"]:
+                after[j].add(k["hold"])
+            for w, b, c0, c1 in regs:
+                if b in psum:
+                    if bank.get(b, j) != j:
+                        after[j].add(bank[b])
+                    continue
+                for (i, w2, a0, a1) in seen.get(b, []):
+                    together = k["kind"] == prog[i]["kind"] == "dma" and k["sem"] == prog[i]["sem"]
+                    if i != j and (w or w2) and a1 > c0 and c1 > a0 and not together:
+                        after[j].add(i)
+            for w, b, c0, c1 in regs:
+                if b in psum:
+                    bank[b] = j
+                else:
+                    seen.setdefault(b, []).append((j, w, c0, c1))
+        for j in range(n):
+            for i in after[j]:
+                then[i].append(j)
+        near = lambda i, j: prog[i]["q"] == prog[j]["q"] == "p"
+        way = [0.0] * n
+        for j in range(n - 1, -1, -1):
+            k = prog[j]
+            for i in then[j]:
+                way[j] = max(way[j], way[i] - (k["lag"] if near(i, j) else 0))
+            way[j] += k["time"] + k["lag"]
+        for j in range(n):
+            way[j] += 1000.0 - j if prog[j]["kind"] == "dma" else 0.0
+        left = [len(after[j]) for j in range(n)]
+        ready = {j for j in range(n) if not left[j]}
+        at, start, free = [0.0] * n, {}, {}
+        while ready:
+            best = None
+            for j in ready:
+                t = max(at[j], free.get(prog[j]["q"], 0.0))
+                c = (t - SLACK * way[j], -way[j], j, t)
+                if best is None or c < best:
+                    best = c
+            j, t = best[2], best[3]
+            k = prog[j]
+            start[j] = t
+            free[k["q"]] = t + k["time"]
+            ready.discard(j)
+            for i in then[j]:
+                at[i] = max(at[i], t + k["time"] + (0 if near(i, j) else k["lag"]))
+                left[i] -= 1
+                if not left[i]:
+                    ready.add(i)
+        return sorted(range(n), key=lambda j: (start[j], j))
+
+    def full(n):
+        c = 1
+        for d in SCRATCH[n][1][1:]:
+            c *= d
+        return (n, 0, c)
+
+    def mm(out, lhsT, rhs, start, stop, reads, writes, n=128):
+        op("p", lambda e: e.matmul(out, lhsT, rhs, start, stop), reads, writes, t=0.04 + 0.000417 * max(n, 64))
+
+    def cp(out, in_, reads, writes, scale=1.0, n=128):
+        op("s", lambda e: e.activation(out, in_, F.Copy, scale=scale), reads, writes, n=n)
+
+    def gath(q, out, win, off, reads, writes):
+        t = 0.06 + 0.0014 * (writes[0][2] - writes[0][1])
+        if q == "v":
+            return op(q, lambda e: e.tensor_copy(out, win.indirect(off)), reads, writes, t=t)
+        return op(q, lambda e: e.activation(out, win.indirect(off), F.Copy), reads, writes, t=t)
+
+    def sel(out, in_, pat, cmp, base, cm, fill=0.0):
+        return lambda e: e.affine_select(out, in_, pat, cmp, fill, base, cm)
+
+    def ts(out, in_, s1, s2, o0, o1, reads, writes, n=64):
+        if o1 is None:
+            op("v", lambda e: e.tensor_scalar(out, in_, s1, None, o0), reads, writes, n=n)
+        else:
+            op("v", lambda e: e.tensor_scalar(out, in_, s1, s2, o0, o1), reads, writes, n=n)
+
+    def tt(out, x, y, o, reads, writes, n=64):
+        op("v", lambda e: e.tensor_tensor(out, x, y, o), reads, writes, n=n)
+
+    def tc(out, in_, reads, writes, n=64):
+        op("v", lambda e: e.tensor_copy(out, in_), reads, writes, n=n)
+
+    dmas([("y", T.EUI[:], T.eu[:])], [], [full("EUI")], 2.0)
+    dmas([("s", T.EVI[:], T.ev[:])], [], [full("EVI")], 2.0)
+    dmas([("sy"[i % 2], T.RI[i::16, :], T.ring0[i % 4::4, :]) for i in range(16)], [], [full("RI")], 3.7)
+    dmas([("y", T.TB0[:, own:own + V], T.m0[:, own:own + V])], [], [("TB0", own, own + V)], 4.8)
+    rest = [T.rank_of(p) * V for p in peers]
+    dmas([("s", T.TB0[:, o:o + V], T.m0[:, o:o + V]) for o in rest], [], [("TB0", o, o + V) for o in rest], 6.6)
+
+    one = T.ONE[:, 0:128]
+    op("v", lambda e: e.memset(T.ONE[:], 1.0), [], [full("ONE")])
+    op("g", lambda e: e.iota(T.PC[:, 0:1], [[0, 1]], 0, 1), [], [("PC", 0, 1)])
+    op("g", lambda e: e.iota(T.RQ[:], [[1, 16]], 0, 0, allow_small_or_imprecise_dtypes=True), [], [full("RQ")])
+    op("g", lambda e: e.iota(T.LO[:], [[1, 256]], 0, 0, allow_small_or_imprecise_dtypes=True), [], [full("LO")])
+    op("g", sel(T.ID[:], one, [[-1, 128]], A.is_equal, 0, 1), [full("ONE")], [full("ID")])
+    op("g", sel(T.ZL[:], T.ONE[:], [[-16, 9], [1000, 16]], A.is_equal, -15000, 1), [full("ONE")], [full("ZL")])
+    op("g", sel(T.ZB[:], T.ZL[:], [[-16, 9], [1000, 16]], A.not_equal, -15001, 1, 256.0), [full("ZL")], [full("ZB")])
+    op("g", sel(T.B1[:], one, [[-16, 8], [0, 16]], A.is_ge, 0, 1), [full("ONE")], [full("B1")])
+    op("g", sel(T.BO[:], T.B1[:], [[16, 8], [0, 16]], A.is_ge, 15, -1), [full("B1")], [full("BO")])
+    for z in range(4):
+        op("g", sel(T.LV[:, z, :], one, [[-16, 8], [-1, 4], [0, 4]], A.is_equal, -4 * z, 1), [full("ONE")], [("LV", 128 * z, 128 * z + 128)])
+    for a in range(4):
+        op("g", sel(T.LE[:, a, :], one, [[-16, 8], [0, 4], [-1, 4]], A.is_equal, -4 * a, 1), [full("ONE")], [("LE", 128 * a, 128 * a + 128)])
+
+    P0 = [("PC", 0, 1)]
+    ts(T.PC[:, 3:4], T.PC[:, 0:1], 1, None, A.bitwise_and, None, P0, [("PC", 3, 4)])
+    ts(T.PC[:, 2:3], T.PC[:, 0:1], 2, 3, A.logical_shift_right, A.bitwise_and, P0, [("PC", 2, 3)])
+    ts(T.PC[:, 1:2], T.PC[:, 0:1], 3, None, A.bitwise_and, None, P0, [("PC", 1, 2)])
+    tc(T.CF[:, 3:4], T.PC[:, 3:4], [("PC", 3, 4)], [("CF", 3, 4)])
+    tc(T.CF[:, 0:1], T.PC[:, 2:3], [("PC", 2, 3)], [("CF", 0, 1)])
+    tc(T.C4[:, 11:12], T.PC[:, 1:2], [("PC", 1, 2)], [("C4", 11, 12)])
+    ts(T.CF[:, 4:5], T.CF[:, 3:4], -1.0, 1.0, A.mult, A.add, [("CF", 3, 4)], [("CF", 4, 5)])
+    ts(T.QH[:], T.RQ[:], T.CF[:, 3:4], None, A.mult, None, [full("RQ"), ("CF", 3, 4)], [full("QH")])
+    ts(T.C4[:, 0:4], T.RQ[:, 0:4], T.CF[:, 0:1], None, A.is_equal, None, [full("RQ"), ("CF", 0, 1)], [("C4", 0, 4)])
+    ts(T.C4[:, 4:8], T.RQ[:, 0:4], T.C4[:, 11:12], None, A.is_equal, None, [full("RQ"), ("C4", 11, 12)], [("C4", 4, 8)])
+    tt(T.CF[:, 1:2], T.PC[:, 2:3], T.PC[:, 1:2], A.is_ge, [("PC", 1, 3)], [("CF", 1, 2)])
+    tt(T.CK[:], T.C4[:, 0:4], T.C4[:, 4:8], A.subtract, [("C4", 0, 8)], [full("CK")])
+    ts(T.CF[:, 2:3], T.CF[:, 1:2], -0.5, None, A.add, None, [("CF", 1, 2)], [("CF", 2, 3)])
+    hold[0] = here()
+
+    def digits(q, out, n, reg):
+        rd = [full("LO"), ("CF", 4, 5), ("QH", n, n + 1)]
+        if q == "v":
+            ts(out, T.LO[:], T.CF[:, 4:5], T.QH[:, n:n + 1], A.mult, A.add, rd, [reg], n=128)
+        else:
+            op("s", lambda e: e.activation(out, T.LO[:], F.Identity, bias=T.QH[:, n:n + 1], scale=T.CF[:, 4:5]), rd, [reg], n=256)
+
+    for n in range(4):
+        digits("v", T.LL0[:, 256 * n:256 * n + 256], n, ("LL0", 256 * n, 256 * n + 256))
+    hold[0] = None
+    for n in range(8):
+        digits("vs"[n > 1], T.PZ[:, 256 * n:256 * n + 256], n + 4, ("PZ", 256 * n, 256 * n + 256))
+    cp(T.IF[:], T.ID[:], [full("ID")], [full("IF")])
+    cp(T.NI[:], T.ID[:], [full("ID")], [full("NI")], scale=-1.0)
+    for a in range(4):
+        cp(T.RD[:, a, :], T.ID[:], [full("ID"), ("C4", 0, 4)], [("RD", 128 * a, 128 * a + 128)], scale=T.C4[:, a:a + 1])
+    tc(T.EU16[:], T.EUI[:], [full("EUI")], [full("EU16")], n=128)
+
+    def place_scatter(b, h0, h1):
+        ll = "LL%d" % b
+        for h in range(h0, h1):
+            src = T.PZ[:, E * b + 256 * h:E * b + 256 * h + 256]
+            dst = T[ll][:, 0:V].indirect(T.EU16[:, 32 * b + 16 * h:32 * b + 16 * h + 16])
+            op("v", lambda e, dst=dst, src=src: e.tensor_copy(dst, src), [("PZ", E * b, E * b + E), ("EU16", 0, 128)], [(ll, 0, V)], waw=True, t=0.80)
+        if h1 == 2 and b + 1 < NB:
+            dmas([("y", T["LL%d" % (b + 1)][:, 0:V], T[ll][:, 0:V])], [(ll, 0, V)], [("LL%d" % (b + 1), 0, V)])
+
+    def place_next(b):
+        ll = "LL%d" % b
+        gath("s", T[ll][:, V:V + E], T[ll][:, 0:V], T.EU16[:, 32 * b + 32:32 * b + 64], [(ll, 0, V), ("EU16", 0, 128)], [(ll, V, V + E)])
+
+    def place_mm(b, part):
+        ll, lx, c0, n = "LL%d" % b, ("LX", "LN", "LX")[part], (0, V, 0)[part], (64, 32, 96)[part]
+        for i in range(16):
+            mm(T[lx][:, 0:n], T.ZB[:, 15 - i:143 - i], T[ll][:, c0 + i:c0 + 16 * n:16], i == 0, i == 15, [full("ZB"), (ll, c0, c0 + 16 * n)], [(lx, 0, n)], n=n)
+
+    def place_out(b, part):
+        o, lx, n, c0 = "LW%d" % b, ("LX", "LN", "LX")[part], (64, 32, 96)[part], (0, 64, 0)[part]
+        tc(T[o][:, c0:c0 + n], T[lx][:, 0:n], [(lx, 0, n)], [(o, c0, c0 + n)], n=n)
+
+    def ring_gather(b, h):
+        g0 = 256 * h
+        if b == 0:
+            gath("s", T.GR[:, g0:g0 + 256], T.RW[:, 0:V], T.EU16[:, 16 * h:16 * h + 16], [("RW", 0, V), ("EU16", 0, 128)], [("GR", g0, g0 + 256)])
+        else:
+            n, lu = V + E * b, "LW%d" % (b - 1)
+            gath("s", T.GR[:, g0:g0 + 256], T.RW[:, 0:n], T[lu][:, 64 + 16 * h:80 + 16 * h], [("RW", 0, n), (lu, 64, 96)], [("GR", g0, g0 + 256)])
+
+    def ring_sum(h):
+        cx, g0 = "CX%d" % h, 256 * h
+        for a in range(4):
+            mm(T[cx][:, 0:64], T.RD[:, a, :], T.GR[:, g0 + a:g0 + 256:4], a == 0, a == 3, [("RD", 128 * a, 128 * a + 128), ("GR", g0, g0 + 256)], [(cx, 0, 64)], n=256)
+
+    def ring_out(b, h):
+        of, cx = "OF%d" % b, "CX%d" % h
+        tc(T[of][:, 64 * h:64 * h + 64], T[cx][:, 0:64], [(cx, 0, 64)], [(of, 64 * h, 64 * h + 64)])
+
+    def ring_diff(b, h):
+        c0 = 128 * b + 64 * h
+        tt(T.DF[:, 64 * h:64 * h + 64], T.VW[:, c0:c0 + 64], T["CX%d" % h][:, 0:64], A.subtract, [("VW", c0, c0 + 64), ("CX%d" % h, 0, 64)], [("DF", 64 * h, 64 * h + 64)])
+
+    def mem_u(b):
+        tb, mu = "TB%d" % b, "MU%d" % (b % 2)
+        gath("s", T[mu][:], T[tb][:, own:own + V], T.EU16[:, 32 * b:32 * b + 32], [(tb, own, own + V), ("EU16", 0, 128)], [full(mu)])
+
+    def mem_v(b):
+        tb, mv = "TB%d" % b, "MV%d" % (b % 2)
+        gath("s", T[mv][:], T[tb][:], T.EV16[:, 32 * b:32 * b + 32], [full(tb), ("EV16", 0, 128)], [full(mv)])
+        marks["mv"] = here()
+
+    def wadd(b, name, start):
+        src = name + "%d" % (b % 2)
+        for h in range(2):
+            mm(T["W%d" % h][:, 0:256], T.ID[:], T[src][:, 256 * h:256 * h + 256], start, False, [full("ID"), full(src)], [("W%d" % h, 0, 256)], n=256)
+
+    def block_half(b, h, dst, base):
+        n, c0 = V + E * (b + 1), base + 512 * h
+        op("s", lambda e: e.activation(T[dst][:, c0:c0 + 512], T.OB[:, 0:n].indirect(T["LW%d" % b][:, 32 * h:32 * h + 32]), F.Relu, bias=15.0, scale=-1.0),
+           [("OB", 0, n), ("LW%d" % b, 0, 64)], [(dst, c0, c0 + 512)], t=0.73)
+
+    def send_half(b, h):
+        tb = "TB%d" % (b + 1)
+        c0 = own + 512 * h
+        ap = T[tb][:, c0:c0 + 512]
+        mask = topo.mask(core, peers[0])
+        ids = []
+        for p in peers:
+            rid, pid, _ = topo.addr(p)
+            mask &= topo.mask(core, p)
+            ids.append(DstId(rid=rid, pnc=pid))
+        ne = bin(mask).count("1")
+
+        def send():
+            g.remote_dma_fused([RemoteDMATransfer(dst_ids=ids, dma_engine_mask=mask, remote_sem=T.sem["arr%d" % b],
+                                                  srcs=[ap], dsts=[ap] * len(ids))], local_sem=T.sem.sent)
+            total["sent"] = total.get("sent", 0) + ne
+
+        def arrive():
+            total["arr%d" % b] = 2 * ne * len(peers)
+            for p in peers:
+                o = T.rank_of(p) * V
+                note("far", ("arr%d" % b, total["arr%d" % b], {}), [], [(tb, o, o + V)])
+
+        item(q="g", kind="send", fn=send, reads=[(tb, c0, c0 + 512)], writes=[("sends%d" % b, h, h + 1)], time=0.5, lag=0.0)
+        if h == 1:
+            item(q="far", kind="far", fn=arrive, reads=[("sends%d" % b, 0, 2)], writes=[(tb, T.rank_of(p) * V, T.rank_of(p) * V + V) for p in peers], time=0.0, lag=FAR)
+
+    place_scatter(0, 0, 1)
+    tc(T.EVF[:], T.EVI[:], [full("EVI")], [full("EVF")], n=128)
+    hold[0] = here()
+    place_scatter(0, 1, 2)
+    hold[0] = None
+    for k in range(3):
+        cp(T.CD[:, k, :], T.ID[:], [full("ID"), full("CK")], [("CD", 128 * k, 128 * k + 128)], scale=T.CK[:, k + 1:k + 2])
+    mm(T.DA0[:, 0:384], T.BO[:], T.CD[:], True, True, [full("BO"), full("CD")], [("DA0", 0, 384)], n=384)
+    for z in range(4):
+        mm(T.DA1[:, z::4], T.LV[:, z, :], T.EVF[:], True, True, [("LV", 128 * z, 128 * z + 128), full("EVF")], [full("DA1")], n=512)
+    cp(T.LD[:], T.DA0[:, 0:384], [("DA0", 0, 384)], [full("LD")], n=384)
+    hold[0] = here()
+    cp(T.VW[:], T.DA1[:], [full("DA1")], [full("VW")], n=512)
+    hold[0] = None
+    vw = here()
+    place_mm(0, 0)
+    tc(T.RW[:, 0:V], T.RI[:], [full("RI")], [("RW", 0, V)], n=V)
+    hold[0] = vw
+    ring_gather(0, 0)
+    hold[0] = None
+    ring_gather(0, 1)
+    r0 = here()
+    ring_sum(0)
+    ring_sum(1)
+    tc(T.EV16[:], T.EVI[:], [full("EVI")], [full("EV16")], n=128)
+    op("v", lambda e: e.memset(T.RS[:], 1.0), [], [full("RS")], n=512)
+    op("v", lambda e: e.memset(T.RS[:, 0::4], 0.0), [], [full("RS")], waw=True, n=128)
+    ring_out(0, 0)
+    ring_out(0, 1)
+    hold[0] = r0
+    mem_u(0)
+    hold[0] = here()
+    mem_v(0)
+    hold[0] = None
+    ts(T.OB[:, 0:V], T.TB0[:, own:own + V], -1.0, 15.0, A.mult, A.add, [("TB0", own, own + V)], [("OB", 0, V)], n=V // 2)
+    wadd(0, "MU", True)
+    for a in range(4):
+        mm(T.LN[:, 128 * a:128 * a + 128], T.LE[:, a, :], T.IF[:], True, True, [("LE", 128 * a, 128 * a + 128), full("IF")], [full("LN")], n=512)
+    place_out(0, 0)
+
+    for b in range(NB):
+        last = b == NB - 1
+        tb, mt, mv, of = "TB%d" % b, "MT%d" % (b % 2), "MV%d" % (b % 2), "OF%d" % b
+
+        def slots(c, q):
+            s = 512 * c
+            gath(q, T[mt][:, s:s + 512], T[tb][:], T[of][:, 32 * c:32 * c + 32], [full(tb), (of, 32 * c, 32 * c + 32)], [(mt, s, s + 512)])
+
+        def scan(c0, c1):
+            s = (512 * c0, 512 * c1)
+            n = s[1] - s[0]
+            x = T[mt][:, s[0]:s[1]]
+            op("v", lambda e: e.tensor_tensor_scan(T.MX[:, s[0]:s[1]], T.RS[:, 0:n], x, 0.0, A.mult, A.max),
+               [full("RS"), (mt,) + s], [("MX",) + s], n=n // 2)
+
+        def wsub(h):
+            s = (1024 * h, 1024 * h + 1024)
+            mm(T["W%d" % h][:, 0:256], T.NI[:], T.MX[:, s[0] + 3:s[1]:4], False, True, [full("NI"), ("MX",) + s], [("W%d" % h, 0, 256)], n=256)
+
+        def clip(h):
+            o, w = V + E * b + 256 * h, "W%d" % h
+            op("s", lambda e: e.activation(T.OB[:, o:o + 256], T[w][:, 0:256], F.Relu, bias=15.0, scale=-1.0), [(w, 0, 256)], [("OB", o, o + 256)], n=256)
+
+        def where(h, j):
+            return (("DA%d" % h, 0), ("DA%d" % h, 256), ("CX%d" % h, 256))[j]
+
+        def diff(h):
+            s = (1024 * h, 1024 * h + 1024)
+            for j in range(3):
+                bk, d = where(h, j)
+                for w, k in (("ID", j + 1), ("NI", 0)):
+                    mm(T[bk][:, d:d + 256], T[w][:], T[mt][:, s[0] + k:s[1]:4], w == "ID", w == "NI", [full(w), (mt,) + s], [(bk, d, d + 256)], n=256)
+
+        def prod(h, j):
+            bk, d = where(h, j)
+            p = 256 * (3 * h + j)
+            tt(T.PR[:, p:p + 256], T[bk][:, d:d + 256], T[mv][:, 256 * h:256 * h + 256], A.mult, [(bk, d, d + 256), full(mv)], [("PR", p, p + 256)], n=256)
+
+        def cdiff(h):
+            bk = "DA%d" % h
+            for j in range(3):
+                p = 256 * (3 * h + j)
+                mm(T[bk][:, 0:256], T.LD[:, j, :], T.PR[:, p:p + 256], j == 0, j == 2, [full("LD"), ("PR", p, p + 256)], [(bk, 0, 256)], n=256)
+
+        def sign(h):
+            bk = "DA%d" % h
+            op("s", lambda e: e.activation(T.SG[:, 256 * h:256 * h + 256], T[bk][:, 0:256], F.Sign, bias=T.CF[:, 2:3]),
+               [(bk, 0, 256), ("CF", 2, 3)], [("SG", 256 * h, 256 * h + 256)], n=256)
+
+        def count(h):
+            cx, s = "CX%d" % h, 256 * h
+            for a in range(4):
+                mm(T[cx][:, 0:64], T.LS[:, a, :], T.SG[:, s + a:s + 256:4], a == 0, a == 3, [full("LS"), ("SG", s, s + 256)], [(cx, 0, 64)], n=64)
+
+        def pick(h):
+            cx, c0 = "CX%d" % h, 64 * h
+            ts(T[cx][:, 64:128], T[cx][:, 0:64], 3.0, None, A.is_ge, None, [(cx, 0, 64)], [(cx, 64, 128)])
+            tt(T.ON[:, c0:c0 + 64], T[cx][:, 64:128], T.DF[:, c0:c0 + 64], A.mult, [(cx, 64, 128), ("DF", c0, c0 + 64)], [("ON", c0, c0 + 64)])
+
+        def spread(h):
+            ex, c0 = "W%d" % h, 64 * h
+            for a in range(4):
+                mm(T[ex][:, a:256:4], T.LE[:, a, :], T.ON[:, c0:c0 + 64], True, True, [("LE", 128 * a, 128 * a + 128), ("ON", c0, c0 + 64)], [(ex, 0, 256)], n=256)
+
+        def renew(h):
+            ex, o, g0 = "W%d" % h, V + E * b + 256 * h, 256 * h
+            tt(T.RW[:, o:o + 256], T[ex][:, 0:256], T.GR[:, g0:g0 + 256], A.add, [(ex, 0, 256), ("GR", g0, g0 + 256)], [("RW", o, o + 256)], n=256)
+
+        if b:
+            hold[0] = marks["ring"]
+            mem_v(b)
+        hold[0] = marks["mv"]
+        slots(0, "v")
+        slots(1, "s")
+        slots(2, "s")
+        s2 = here()
+        slots(3, "v")
+        hold[0] = None
+        if b == 0:
+            hold[0] = s2
+            cp(T.LS[:], T.LN[:], [full("LN")], [full("LS")], n=512)
+            hold[0] = None
+        wadd(b, "MV", False)
+        if last:
+            diff(0)
+            scan(0, 2)
+            ring_diff(b, 0)
+            ring_diff(b, 1)
+            for j in (2, 0, 1):
+                prod(0, j)
+            p0 = here()
+            diff(1)
+            hold[0] = here()
+            cdiff(0)
+            c0 = here()
+            sign(0)
+            hold[0] = p0
+            for j in (2, 0, 1):
+                prod(1, j)
+            hold[0] = None
+            wsub(0)
+            count(0)
+            hold[0] = c0
+            cdiff(1)
+            hold[0] = None
+            sign(1)
+            scan(2, 4)
+            wsub(1)
+            count(1)
+            pick(0)
+            place_out(b, 0)
+            pick(1)
+            clip(0)
+            clip(1)
+            spread(0)
+            hold[0] = here()
+            spread(1)
+            hold[0] = None
+            renew(0)
+            renew(1)
+            n = V + E * NB
+            for h in range(2):
+                gath("sv"[h], T.YR[:, 512 * h:512 * h + 512], T.RW[:, 0:n], T.LW3[:, 32 * h:32 * h + 32], [("RW", 0, n), ("LW3", 0, 64)], [("YR", 512 * h, 512 * h + 512)])
+                dmas([("ys"[k % 2], T.yr[k::4, 512 * h:512 * h + 512], T.YR[k::16, 512 * h:512 * h + 512]) for k in range(4)], [("YR", 512 * h, 512 * h + 512)], [])
+            for h in range(2):
+                block_half(b, h, "YB", 0)
+                dmas([("y", T.ym[:, 512 * h:512 * h + 512], T.YB[:, 512 * h:512 * h + 512])], [("YB", 512 * h, 512 * h + 512)], [])
+            continue
+        diff(0)
+        scan(0, 2)
+        wsub(0)
+        ring_diff(b, 0)
+        ring_diff(b, 1)
+        if b:
+            place_out(b, 2)
+        scan(2, 3)
+        clip(0)
+        scan(3, 4)
+        wsub(1)
+        prod(0, 2)
+        clip(1)
+        diff(1)
+        for h in range(2):
+            block_half(b, h, "TB%d" % (b + 1), own)
+            blk = here()
+            send_half(b, h)
+        if b == 0:
+            hold[0] = blk
+            place_next(b)
+            place_mm(b, 1)
+            hold[0] = None
+            place_out(b, 1)
+        prod(0, 0)
+        prod(0, 1)
+        hold[0] = here()
+        cdiff(0)
+        c0 = here()
+        sign(0)
+        for j in range(3):
+            prod(1, j)
+        hold[0] = None
+        p1 = here()
+        count(0)
+        hold[0] = c0
+        cdiff(1)
+        hold[0] = None
+        mem_u(b + 1)
+        sign(1)
+        count(1)
+        hold[0] = p1
+        place_scatter(b + 1, 0, 1)
+        hold[0] = None
+        pick(0)
+        spread(0)
+        hold[0] = here()
+        pick(1)
+        spread(1)
+        hold[0] = None
+        renew(0)
+        renew(1)
+        hold[0] = here()
+        place_scatter(b + 1, 1, 2)
+        hold[0] = None
+        ring_gather(b + 1, 0)
+        ring_gather(b + 1, 1)
+        marks["ring"] = here()
+        ring_sum(0)
+        ring_sum(1)
+        wadd(b + 1, "MU", True)
+        if b + 2 < NB:
+            place_next(b + 1)
+        place_mm(b + 1, 2 if b + 2 < NB else 0)
+        ring_out(b + 1, 0)
+        ring_out(b + 1, 1)
+    for j in plan():
+        emit(prog[j])
+    for s in total:
+        if waited.get(s, 0) < total[s]:
+            g.wait_ge(T.sem[s], total[s])

@@ -3,28 +3,44 @@ from concourse.mybir import AluOpType as A, ActivationFunctionType as F
 
 NB, V, E, R = 4, 1024, 512, 4
 BF, F32, I32, U16 = "bfloat16", "float32", "int32", "uint16"
-LAG, FAR, SLACK = 0.12, 3.7, 0.03
+BIG = 128.0
+PIECES = (("s", 0, 512), ("s", 512, 1024))
+SENDS = ((0, 512), (512, 1024))
+START = {"v": "fill cols cols2 eu16 rdig scat0 scat1 ld ev16 ro0 ro1",
+         "s": "cols pz0 lldig cd ni rws rwv rg0 rg1 u",
+         "p": "rw ld rs0 rs1 pm0 wu0 wu1"}
+FIRST = {"v": "s0 s1 m0 m1 obinit m2 m3 po vdig p0 blk p1 pz1 lc scat0 rn0 rn1 pnout scat1 ro0 ro1 pz2",
+         "s": "v s2 s3 clip0 pn0 clip1 blk vw sg0 sg1 u rg0 rg1 pn",
+         "p": "wv d0 ws0 ws1 d1 vw cd0 cd1 of0 of1 ct0 ct1 pm1 wu0 rs0 wu1 rs1 pm0"}
+TURN = {"v": "s0 s1 m0 m1 m2 pnout m3 po p0 blk p1 scat0 rn0 rn1 scat1 ro0 ro1 pz3",
+        "s": "v s2 s3 clip0 clip1 blk sg0 sg1 u rg0 rg1 pn",
+        "p": "pm1 wv d0 ws0 ws1 d1 of0 cd0 cd1 of1 ct0 ct1 wu0 wu1 rs0 rs1 pm0"}
+LAST = {"v": "po s0 s1 m0 m1 m2 m3 p0 p1 rn0 rn1 yg yr",
+        "s": "v s2 s3 clip0 clip1 blk0 sg0 sg1 yg blk1",
+        "p": "of0 of1 wv d0 ws0 ws1 d1 cd0 cd1 ct0 ct1 yr"}
+WHO = {"pz0": "s", "pz1": "v", "pz2": "v", "pz3": "v", "cd": "s", "pn0": "s", "pn": "s", "obinit": "v", "lldig": "s", "rwv": "s", "ld": "v"}
 
 SCRATCH = {
     "OB": ("sbuf", [128, V + NB * E], BF),
-    "RW": ("sbuf", [128, V + NB * E], F32),
-    "RI": ("sbuf", [128, V], I32),
-    "EUI": ("sbuf", [128, 128], I32), "EVI": ("sbuf", [128, 128], I32),
-    "EU16": ("sbuf", [128, 128], U16), "EV16": ("sbuf", [128, 128], U16), "EVF": ("sbuf", [128, 128], F32),
+    "RW": ("sbuf", [128, V + NB * E], BF),
+    "RI": ("sbuf", [128, 256], I32), "RJ": ("sbuf", [128, 512], I32), "RD": ("sbuf", [128, 512], BF),
+    "EUI": ("sbuf", [128, 128], I32), "EVI": ("sbuf", [128, 128], I32), "EVJ": ("sbuf", [128, 256], I32), "EVD": ("sbuf", [128, 256], BF),
+    "EU16": ("sbuf", [128, 128], U16), "EV16": ("sbuf", [128, 128], U16),
     "MX": ("sbuf", [128, 2048], BF), "PR": ("sbuf", [128, 1536], BF),
-    "SG": ("sbuf", [128, 512], BF), "ON": ("sbuf", [128, 128], F32),
-    "GR": ("sbuf", [128, 512], F32), "DF": ("sbuf", [128, 128], F32),
-    "VW": ("sbuf", [128, 512], F32),
-    "YB": ("sbuf", [128, V], BF), "YR": ("sbuf", [128, V], F32),
-    "ONE": ("sbuf", [128, 144], BF), "ID": ("sbuf", [128, 128], BF), "NI": ("sbuf", [128, 128], BF), "IF": ("sbuf", [128, 128], F32),
+    "SG": ("sbuf", [128, 512], BF), "GR": ("sbuf", [128, 512], BF),
+    "VW": ("sbuf", [128, 512], BF),
+    "YB": ("sbuf", [128, V], BF), "YG": ("sbuf", [128, V], BF), "YR": ("sbuf", [128, 256], F32),
+    "ONE": ("sbuf", [128, 528], BF), "PM": ("sbuf", [128, 128], BF), "ZR": ("sbuf", [128, 144], BF),
+    "ID": ("sbuf", [128, 128], BF), "NI": ("sbuf", [128, 128], BF),
     "ZL": ("sbuf", [128, 144], BF), "ZB": ("sbuf", [128, 144], BF), "RQ": ("sbuf", [128, 16], F32), "QH": ("sbuf", [128, 16], F32),
-    "LO": ("sbuf", [128, 256], BF), "PZ": ("sbuf", [128, NB * E], BF),
-    "LE": ("sbuf", [128, 4, 128], F32), "LV": ("sbuf", [128, 4, 128], F32), "RD": ("sbuf", [128, 4, 128], F32),
+    "XL": ("sbuf", [128, 272], BF), "Q4": ("sbuf", [128, 128], BF), "PZ": ("sbuf", [128, NB * E], BF),
+    "ZA": ("sbuf", [128, 4, 132], BF), "LV": ("sbuf", [128, 4, 144], BF), "YL": ("sbuf", [128, 144], BF), "Y2": ("sbuf", [128, 144], BF),
+    "Y1": ("sbuf", [128, 144], BF), "LC": ("sbuf", [128, 32, 4], BF), "SV": ("sbuf", [128, 4, 128], BF),
     "BO": ("sbuf", [128, 128], BF), "B1": ("sbuf", [128, 128], BF),
-    "LD": ("sbuf", [128, 3, 128], BF), "LS": ("sbuf", [128, 4, 128], BF), "CD": ("sbuf", [128, 3, 128], BF),
-    "C4": ("sbuf", [128, 12], F32), "CK": ("sbuf", [128, 4], F32),
-    "RS": ("sbuf", [128, 1024], BF),
-    "PC": ("sbuf", [128, 8], I32), "CF": ("sbuf", [128, 8], F32),
+    "LD": ("sbuf", [128, 3, 128], BF), "CD": ("sbuf", [128, 3, 128], BF),
+    "CA": ("sbuf", [128, 4], F32), "CJ": ("sbuf", [128, 4], F32), "CK": ("sbuf", [128, 4], F32),
+    "RS": ("sbuf", [128, 512], BF), "LL": ("sbuf", [128, V + E], BF),
+    "PC": ("sbuf", [128, 8], I32), "CF": ("sbuf", [128, 24], F32),
     "W0": ("psum", [128, 512], F32), "W1": ("psum", [128, 512], F32), "LX": ("psum", [128, 512], F32), "LN": ("psum", [128, 512], F32),
     "DA0": ("psum", [128, 512], F32), "DA1": ("psum", [128, 512], F32), "CX0": ("psum", [128, 512], F32), "CX1": ("psum", [128, 512], F32),
 }
@@ -32,12 +48,11 @@ for _c in range(4):
     SCRATCH["TB%d" % _c] = ("sbuf", [128, 4 * V], BF)
     SCRATCH["OF%d" % _c] = ("sbuf", [128, 128], U16)
     SCRATCH["LW%d" % _c] = ("sbuf", [128, 96], U16)
-    SCRATCH["LL%d" % _c] = ("sbuf", [128, V + E], BF)
 for _c in range(2):
     SCRATCH["MU%d" % _c] = ("sbuf", [128, 512], BF)
     SCRATCH["MV%d" % _c] = ("sbuf", [128, 512], BF)
     SCRATCH["MT%d" % _c] = ("sbuf", [128, 2048], BF)
-NDMA = 20
+NDMA = 12
 SEMAPHORES = ["cv", "cs", "cp", "cg", "sent"] + ["arr%d" % b for b in range(NB)] + ["d%d" % i for i in range(NDMA)]
 
 
@@ -49,9 +64,10 @@ def rank_program(g, core, T, topo):
     own = rank * V
     QU = {"v": g.vector, "s": g.scalar, "p": g.tensor, "g": g, "y": g.sync}
     known = {q: {} for q in QU}
-    hold, marks, prog = [None], {}, []
+    stage, prog = [0, None, None], []
     total, waited, acc, ndma, clks = {}, {}, {}, [0], {}
     psum = {n for n in SCRATCH if SCRATCH[n][0] == "psum"}
+    turns = [START, FIRST] + [TURN] * (NB - 2) + [LAST]
 
     def wait(q, rec):
         sem, val, clk = rec
@@ -111,30 +127,38 @@ def rank_program(g, core, T, topo):
                 order("g", reads, [])
             k["fn"]()
 
+    def step(name, p=None, turn=None):
+        stage[1:] = [name, p or name]
+        if turn is not None:
+            stage[0] = turn
+
     def item(**k):
-        k["hold"] = hold[0]
+        turn, name, k["at"] = stage[0], stage[2 if k["q"] == "p" else 1], (0, 0)
+        if k["q"] in "vsp" and k["kind"] == "op":
+            while name not in turns[turn][k["q"]].split():
+                turn += 1
+            k["at"] = (turn, 1 + turns[turn][k["q"]].split().index(name))
         prog.append(k)
 
-    def here():
-        return len(prog) - 1
+    def op(q, fn, reads, writes, waw=False):
+        item(q=q, kind="op", fn=fn, reads=reads, writes=writes, waw=waw)
 
-    def op(q, fn, reads, writes, waw=False, n=128, t=None):
-        item(q=q, kind="op", fn=fn, reads=reads, writes=writes, waw=waw, time=t or (0.38 if q == "g" else 0.055 + 0.00083 * max(n, 64)), lag=LAG)
-
-    def dmas(parts, reads, writes, lag=2.2):
+    def dmas(parts, reads, writes):
         sem = "d%d" % ndma[0]
         ndma[0] += 1
         for q, out, in_ in parts:
-            item(q=q, kind="dma", fn=(out, in_), reads=reads, writes=writes, time=0.06, lag=lag, sem=sem, n=len(parts))
+            item(q=q, kind="dma", fn=(out, in_), reads=reads, writes=writes, sem=sem, n=len(parts))
 
     def plan():
         n = len(prog)
         after, then = [set() for _ in range(n)], [[] for _ in range(n)]
         seen, bank = {}, {}
+        for q in QU:
+            mine = sorted((j for j in range(n) if prog[j]["q"] == q), key=lambda j: (prog[j]["at"], j))
+            for i, j in zip(mine, mine[1:]):
+                after[j].add(i)
         for j, k in enumerate(prog):
             regs = [(0,) + r for r in k["reads"]] + [(1,) + r for r in k["writes"]]
-            if k["hold"] is not None and prog[k["hold"]]["q"] == k["q"]:
-                after[j].add(k["hold"])
             for w, b, c0, c1 in regs:
                 if b in psum:
                     if bank.get(b, j) != j:
@@ -152,36 +176,15 @@ def rank_program(g, core, T, topo):
         for j in range(n):
             for i in after[j]:
                 then[i].append(j)
-        near = lambda i, j: prog[i]["q"] == prog[j]["q"] == "p"
-        way = [0.0] * n
-        for j in range(n - 1, -1, -1):
-            k = prog[j]
-            for i in then[j]:
-                way[j] = max(way[j], way[i] - (k["lag"] if near(i, j) else 0))
-            way[j] += k["time"] + k["lag"]
-        for j in range(n):
-            way[j] += 1000.0 - j if prog[j]["kind"] == "dma" else 0.0
         left = [len(after[j]) for j in range(n)]
-        ready = {j for j in range(n) if not left[j]}
-        at, start, free = [0.0] * n, {}, {}
-        while ready:
-            best = None
-            for j in ready:
-                t = max(at[j], free.get(prog[j]["q"], 0.0))
-                c = (t - SLACK * way[j], -way[j], j, t)
-                if best is None or c < best:
-                    best = c
-            j, t = best[2], best[3]
-            k = prog[j]
-            start[j] = t
-            free[k["q"]] = t + k["time"]
-            ready.discard(j)
+        line = [j for j in range(n) if not left[j]]
+        for j in line:
             for i in then[j]:
-                at[i] = max(at[i], t + k["time"] + (0 if near(i, j) else k["lag"]))
                 left[i] -= 1
                 if not left[i]:
-                    ready.add(i)
-        return sorted(range(n), key=lambda j: (start[j], j))
+                    line.append(i)
+        assert len(line) == n, [(prog[j]["q"], prog[j]["at"]) for j in range(n) if left[j]][:9]
+        return line
 
     def full(n):
         c = 1
@@ -189,155 +192,176 @@ def rank_program(g, core, T, topo):
             c *= d
         return (n, 0, c)
 
-    def mm(out, lhsT, rhs, start, stop, reads, writes, n=128):
-        op("p", lambda e: e.matmul(out, lhsT, rhs, start, stop), reads, writes, t=0.04 + 0.000417 * max(n, 64))
+    def mm(out, lhsT, rhs, start, stop, reads, writes):
+        op("p", lambda e: e.matmul(out, lhsT, rhs, start, stop), reads, writes)
 
-    def cp(out, in_, reads, writes, scale=1.0, n=128):
-        op("s", lambda e: e.activation(out, in_, F.Copy, scale=scale), reads, writes, n=n)
+    def act(out, in_, reads, writes, f=F.Copy, **k):
+        op("s", lambda e: e.activation(out, in_, f, **k), reads, writes)
 
-    def gath(q, out, win, off, reads, writes):
-        t = 0.06 + 0.0014 * (writes[0][2] - writes[0][1])
-        if q == "v":
-            return op(q, lambda e: e.tensor_copy(out, win.indirect(off)), reads, writes, t=t)
-        return op(q, lambda e: e.activation(out, win.indirect(off), F.Copy), reads, writes, t=t)
+    def sel(out, in_, pat, cmp, base, reads, writes, fill=0.0, cm=1):
+        op("g", lambda e: e.affine_select(out, in_, pat, cmp, fill, base, cm), reads, writes)
 
-    def sel(out, in_, pat, cmp, base, cm, fill=0.0):
-        return lambda e: e.affine_select(out, in_, pat, cmp, fill, base, cm)
+    def iota(name, pat, base=0):
+        op("g", lambda e: e.iota(T[name][:], pat, base, 0, allow_small_or_imprecise_dtypes=True), [], [full(name)])
 
-    def ts(out, in_, s1, s2, o0, o1, reads, writes, n=64):
+    def ts(out, in_, s1, s2, o0, o1, reads, writes):
         if o1 is None:
-            op("v", lambda e: e.tensor_scalar(out, in_, s1, None, o0), reads, writes, n=n)
+            op("v", lambda e: e.tensor_scalar(out, in_, s1, None, o0), reads, writes)
         else:
-            op("v", lambda e: e.tensor_scalar(out, in_, s1, s2, o0, o1), reads, writes, n=n)
+            op("v", lambda e: e.tensor_scalar(out, in_, s1, s2, o0, o1), reads, writes)
 
-    def tt(out, x, y, o, reads, writes, n=64):
-        op("v", lambda e: e.tensor_tensor(out, x, y, o), reads, writes, n=n)
+    def tt(out, x, y, o, reads, writes):
+        op("v", lambda e: e.tensor_tensor(out, x, y, o), reads, writes)
 
-    def tc(out, in_, reads, writes, n=64):
-        op("v", lambda e: e.tensor_copy(out, in_), reads, writes, n=n)
+    def copy(q, out, in_, reads, writes):
+        if q == "v":
+            op("v", lambda e: e.tensor_copy(out, in_), reads, writes)
+        else:
+            act(out, in_, reads, writes)
 
-    dmas([("y", T.EUI[:], T.eu[:])], [], [full("EUI")], 2.0)
-    dmas([("s", T.EVI[:], T.ev[:])], [], [full("EVI")], 2.0)
-    dmas([("sy"[i % 2], T.RI[i::16, :], T.ring0[i % 4::4, :]) for i in range(16)], [], [full("RI")], 3.7)
-    dmas([("y", T.TB0[:, own:own + V], T.m0[:, own:own + V])], [], [("TB0", own, own + V)], 4.8)
-    rest = [T.rank_of(p) * V for p in peers]
-    dmas([("s", T.TB0[:, o:o + V], T.m0[:, o:o + V]) for o in rest], [], [("TB0", o, o + V) for o in rest], 6.6)
+    def affine(q, out, in_, scale, bias, reads, writes):
+        if q == "v":
+            ts(out, in_, scale, bias, A.mult, A.add, reads, writes)
+        else:
+            act(out, in_, reads, writes, F.Identity, scale=scale, bias=bias)
 
+    dmas([("y", T.RI[:], T.ring0[:])], [], [full("RI")])
+    dmas([("s", T.EUI[:], T.eu[:])], [], [full("EUI")])
+    dmas([("s", T.EVI[:], T.ev[:])], [], [full("EVI")])
+    dmas([("y", T.TB0[:, own:own + V], T.m0[:, own:own + V])], [], [("TB0", own, own + V)])
+    rest = [(a, b) for a, b in ((0, own), (own + V, 4 * V)) if a < b]
+    dmas([("y", T.TB0[:, a:b], T.m0[:, a:b]) for a, b in rest], [], [("TB0", a, b) for a, b in rest])
+
+    step("fill")
     one = T.ONE[:, 0:128]
     op("v", lambda e: e.memset(T.ONE[:], 1.0), [], [full("ONE")])
+    op("v", lambda e: e.memset(T.ZR[:], 0.0), [], [full("ZR")])
     op("g", lambda e: e.iota(T.PC[:, 0:1], [[0, 1]], 0, 1), [], [("PC", 0, 1)])
-    op("g", lambda e: e.iota(T.RQ[:], [[1, 16]], 0, 0, allow_small_or_imprecise_dtypes=True), [], [full("RQ")])
-    op("g", lambda e: e.iota(T.LO[:], [[1, 256]], 0, 0, allow_small_or_imprecise_dtypes=True), [], [full("LO")])
-    op("g", sel(T.ID[:], one, [[-1, 128]], A.is_equal, 0, 1), [full("ONE")], [full("ID")])
-    op("g", sel(T.ZL[:], T.ONE[:], [[-16, 9], [1000, 16]], A.is_equal, -15000, 1), [full("ONE")], [full("ZL")])
-    op("g", sel(T.ZB[:], T.ZL[:], [[-16, 9], [1000, 16]], A.not_equal, -15001, 1, 256.0), [full("ZL")], [full("ZB")])
-    op("g", sel(T.B1[:], one, [[-16, 8], [0, 16]], A.is_ge, 0, 1), [full("ONE")], [full("B1")])
-    op("g", sel(T.BO[:], T.B1[:], [[16, 8], [0, 16]], A.is_ge, 15, -1), [full("B1")], [full("BO")])
+    iota("RQ", [[1, 16]])
+    iota("XL", [[1, 272]], -16)
+    sel(T.ZA[:], T.ONE[:], [[-1, 4], [-4, 33], [1000, 4]], A.is_equal, -1000, [full("ONE")], [full("ZA")])
+    sel(T.ID[:], one, [[-1, 128]], A.is_equal, 0, [full("ONE")], [full("ID")])
+    sel(T.B1[:], one, [[-16, 8], [0, 16]], A.is_ge, 0, [full("ONE")], [full("B1")])
+    sel(T.BO[:], T.B1[:], [[16, 8], [0, 16]], A.is_ge, 15, [full("B1")], [full("BO")], cm=-1)
+    sel(T.YL[:], T.ZR[:], [[-16, 9], [1000, 4], [-4, 4]], A.not_equal, -3000, [full("ZR")], [full("YL")], 1.0)
+    sel(T.Y2[:], T.YL[:], [[-16, 9], [1000, 4], [-4, 4]], A.not_equal, -3001, [full("YL")], [full("Y2")], 32.0)
+    sel(T.ZL[:], T.ZR[:], [[-16, 9], [1000, 16]], A.not_equal, -15000, [full("ZR")], [full("ZL")], 1.0)
+    sel(T.ZB[:], T.ZL[:], [[-16, 9], [1000, 16]], A.not_equal, -15001, [full("ZL")], [full("ZB")], 256.0)
+    iota("RS", [[0, 128], [32, 4]], -16)
     for z in range(4):
-        op("g", sel(T.LV[:, z, :], one, [[-16, 8], [-1, 4], [0, 4]], A.is_equal, -4 * z, 1), [full("ONE")], [("LV", 128 * z, 128 * z + 128)])
+        sel(T.LV[:, z, :], T.ONE[:, 0:144], [[-16, 9], [-1, 4], [1000, 4]], A.is_equal, -1000 - 4 * z, [full("ONE")], [("LV", 144 * z, 144 * z + 144)])
+    iota("Q4", [[1, 32], [0, 4]])
+    sel(T.PM[:], one, [[0, 32], [-1, 2], [0, 2]], A.is_equal, 0, [full("ONE")], [full("PM")], -1.0, 0)
     for a in range(4):
-        op("g", sel(T.LE[:, a, :], one, [[-16, 8], [0, 4], [-1, 4]], A.is_equal, -4 * a, 1), [full("ONE")], [("LE", 128 * a, 128 * a + 128)])
+        sel(T.SV[:, a, :], T.PM[:], [[-16, 8], [0, 8], [-1, 2]], A.is_equal, -4 * a, [full("PM")], [("SV", 128 * a, 128 * a + 128)])
 
-    P0 = [("PC", 0, 1)]
-    ts(T.PC[:, 3:4], T.PC[:, 0:1], 1, None, A.bitwise_and, None, P0, [("PC", 3, 4)])
-    ts(T.PC[:, 2:3], T.PC[:, 0:1], 2, 3, A.logical_shift_right, A.bitwise_and, P0, [("PC", 2, 3)])
-    ts(T.PC[:, 1:2], T.PC[:, 0:1], 3, None, A.bitwise_and, None, P0, [("PC", 1, 2)])
-    tc(T.CF[:, 3:4], T.PC[:, 3:4], [("PC", 3, 4)], [("CF", 3, 4)])
-    tc(T.CF[:, 0:1], T.PC[:, 2:3], [("PC", 2, 3)], [("CF", 0, 1)])
-    tc(T.C4[:, 11:12], T.PC[:, 1:2], [("PC", 1, 2)], [("C4", 11, 12)])
-    ts(T.CF[:, 4:5], T.CF[:, 3:4], -1.0, 1.0, A.mult, A.add, [("CF", 3, 4)], [("CF", 4, 5)])
-    ts(T.QH[:], T.RQ[:], T.CF[:, 3:4], None, A.mult, None, [full("RQ"), ("CF", 3, 4)], [full("QH")])
-    ts(T.C4[:, 0:4], T.RQ[:, 0:4], T.CF[:, 0:1], None, A.is_equal, None, [full("RQ"), ("CF", 0, 1)], [("C4", 0, 4)])
-    ts(T.C4[:, 4:8], T.RQ[:, 0:4], T.C4[:, 11:12], None, A.is_equal, None, [full("RQ"), ("C4", 11, 12)], [("C4", 4, 8)])
-    tt(T.CF[:, 1:2], T.PC[:, 2:3], T.PC[:, 1:2], A.is_ge, [("PC", 1, 3)], [("CF", 1, 2)])
-    tt(T.CK[:], T.C4[:, 0:4], T.C4[:, 4:8], A.subtract, [("C4", 0, 8)], [full("CK")])
-    ts(T.CF[:, 2:3], T.CF[:, 1:2], -0.5, None, A.add, None, [("CF", 1, 2)], [("CF", 2, 3)])
-    hold[0] = here()
+    names = ["odd", "lo", "hi", "g4", "p4", "even", "ge", "tie", "eq", "wc", "lc", "w1", "keep", "big"]
+    col = {n: T.CF[:, i:i + 1] for i, n in enumerate(names)}
+    reg = {n: ("CF", i, i + 1) for i, n in enumerate(names)}
+    step("cols")
+    for i, (sh, m) in enumerate(((0, 1), (0, 3), (2, 3), (2, 28), (0, 124))):
+        ts(T.PC[:, i + 1:i + 2], T.PC[:, 0:1], sh, m, A.logical_shift_right, A.bitwise_and, [("PC", 0, 1)], [("PC", i + 1, i + 2)])
+    copy("v", T.CF[:, 0:5], T.PC[:, 1:6], [("PC", 1, 6)], [("CF", 0, 5)])
 
-    def digits(q, out, n, reg):
-        rd = [full("LO"), ("CF", 4, 5), ("QH", n, n + 1)]
-        if q == "v":
-            ts(out, T.LO[:], T.CF[:, 4:5], T.QH[:, n:n + 1], A.mult, A.add, rd, [reg], n=128)
-        else:
-            op("s", lambda e: e.activation(out, T.LO[:], F.Identity, bias=T.QH[:, n:n + 1], scale=T.CF[:, 4:5]), rd, [reg], n=256)
+    def lin(out, x, scale, bias):
+        affine("s", col[out], col[x], scale, col.get(bias, bias), [reg[x]] + ([reg[bias]] if bias in reg else []), [reg[out]])
+
+    def cmp(out, x, s1, s2, o):
+        ts(col[out], col[x], col.get(s1, s1), s2, o, A.mult, [reg[x]] + ([reg[s1]] if s1 in reg else []), [reg[out]])
+
+    ts(T.QH[:], T.RQ[:], col["odd"], None, A.mult, None, [full("RQ"), reg["odd"]], [full("QH")])
+    cmp("eq", "hi", "lo", 4 * BIG, A.is_equal)
+    cmp("keep", "lo", 2.0, 1.0, A.is_lt)
+    cmp("ge", "hi", "lo", 1.0, A.is_ge)
+    lin("even", "odd", -1.0, 1.0)
+    lin("lc", "g4", 1.0, "lo")
+    lin("w1", "odd", 31.0, 1.0)
+    lin("wc", "eq", 1.0, -BIG)
+    lin("big", "keep", -BIG, BIG)
+    lin("tie", "ge", 1.0, -0.5)
+    step("cols2")
+    ts(T.CJ[:], T.RQ[:, 0:4], col["lo"], None, A.is_equal, None, [full("RQ"), reg["lo"]], [full("CJ")])
+    ts(T.CA[:], T.RQ[:, 0:4], col["hi"], None, A.is_equal, None, [full("RQ"), reg["hi"]], [full("CA")])
+    tt(T.CK[:], T.CA[:], T.CJ[:], A.subtract, [full("CA"), full("CJ")], [full("CK")])
+    step("lc")
+    ts(T.LC[:], T.Q4[:], col["lc"], col["wc"], A.is_equal, A.mult, [full("Q4"), reg["lc"], reg["wc"]], [full("LC")])
+    ts(T.Y1[:], T.XL[:, 13:157], col["p4"], col["w1"], A.is_equal, A.mult, [full("XL"), reg["p4"], reg["w1"]], [full("Y1")])
+    ts(T.LC[:, :, 2:4], T.LC[:, :, 2:4], -1.0, None, A.mult, None, [full("LC")], [full("LC")])
+
+    def digits(name, buf, c0, n):
+        step(name)
+        affine(WHO[name], T[buf][:, c0:c0 + 256], T.XL[:, 16:272], col["even"], T.QH[:, n:n + 1], [full("XL"), reg["even"], ("QH", n, n + 1)], [(buf, c0, c0 + 256)])
 
     for n in range(4):
-        digits("v", T.LL0[:, 256 * n:256 * n + 256], n, ("LL0", 256 * n, 256 * n + 256))
-    hold[0] = None
+        digits("lldig", "LL", 256 * n, n)
     for n in range(8):
-        digits("vs"[n > 1], T.PZ[:, 256 * n:256 * n + 256], n + 4, ("PZ", 256 * n, 256 * n + 256))
-    cp(T.IF[:], T.ID[:], [full("ID")], [full("IF")])
-    cp(T.NI[:], T.ID[:], [full("ID")], [full("NI")], scale=-1.0)
-    for a in range(4):
-        cp(T.RD[:, a, :], T.ID[:], [full("ID"), ("C4", 0, 4)], [("RD", 128 * a, 128 * a + 128)], scale=T.C4[:, a:a + 1])
-    tc(T.EU16[:], T.EUI[:], [full("EUI")], [full("EU16")], n=128)
+        digits("pz%d" % (n // 2), "PZ", 256 * n, n + 4)
+    step("ni")
+    act(T.NI[:], T.ID[:], [full("ID")], [full("NI")], scale=-1.0)
+    step("eu16")
+    copy("v", T.EU16[:], T.EUI[:], [full("EUI")], [full("EU16")])
 
-    def place_scatter(b, h0, h1):
-        ll = "LL%d" % b
-        for h in range(h0, h1):
-            src = T.PZ[:, E * b + 256 * h:E * b + 256 * h + 256]
-            dst = T[ll][:, 0:V].indirect(T.EU16[:, 32 * b + 16 * h:32 * b + 16 * h + 16])
-            op("v", lambda e, dst=dst, src=src: e.tensor_copy(dst, src), [("PZ", E * b, E * b + E), ("EU16", 0, 128)], [(ll, 0, V)], waw=True, t=0.80)
-        if h1 == 2 and b + 1 < NB:
-            dmas([("y", T["LL%d" % (b + 1)][:, 0:V], T[ll][:, 0:V])], [(ll, 0, V)], [("LL%d" % (b + 1), 0, V)])
+    def place_scatter(b, h):
+        step("scat%d" % h)
+        src = T.PZ[:, E * b + 256 * h:E * b + 256 * h + 256]
+        dst = T.LL[:, 0:V].indirect(T.EU16[:, 32 * b + 16 * h:32 * b + 16 * h + 16])
+        op("v", lambda e: e.tensor_copy(dst, src), [("PZ", E * b, E * b + E), ("EU16", 0, 128)], [("LL", 0, V)], waw=True)
 
-    def place_next(b):
-        ll = "LL%d" % b
-        gath("s", T[ll][:, V:V + E], T[ll][:, 0:V], T.EU16[:, 32 * b + 32:32 * b + 64], [(ll, 0, V), ("EU16", 0, 128)], [(ll, V, V + E)])
+    def place_next(b, name="pn"):
+        step(name)
+        copy(WHO[name], T.LL[:, V:V + E], T.LL[:, 0:V].indirect(T.EU16[:, 32 * b + 32:32 * b + 64]), [("LL", 0, V), ("EU16", 0, 128)], [("LL", V, V + E)])
 
-    def place_mm(b, part):
-        ll, lx, c0, n = "LL%d" % b, ("LX", "LN", "LX")[part], (0, V, 0)[part], (64, 32, 96)[part]
+    def place_mm(part):
+        step(None, "pm%d" % part)
+        lx, c0, n = ("LX", "DA1")[part], (0, V)[part], (64, 32)[part]
         for i in range(16):
-            mm(T[lx][:, 0:n], T.ZB[:, 15 - i:143 - i], T[ll][:, c0 + i:c0 + 16 * n:16], i == 0, i == 15, [full("ZB"), (ll, c0, c0 + 16 * n)], [(lx, 0, n)], n=n)
+            mm(T[lx][:, 0:n], T.ZB[:, 15 - i:143 - i], T.LL[:, c0 + i:c0 + 16 * n:16], i == 0, i == 15, [full("ZB"), ("LL", c0, c0 + 16 * n)], [(lx, 0, n)])
 
     def place_out(b, part):
-        o, lx, n, c0 = "LW%d" % b, ("LX", "LN", "LX")[part], (64, 32, 96)[part], (0, 64, 0)[part]
-        tc(T[o][:, c0:c0 + n], T[lx][:, 0:n], [(lx, 0, n)], [(o, c0, c0 + n)], n=n)
+        step(("po", "pnout")[part])
+        o, lx, n, c0 = "LW%d" % b, ("LX", "DA1")[part], (64, 32)[part], (0, 64)[part]
+        copy("v", T[o][:, c0:c0 + n], T[lx][:, 0:n], [(lx, 0, n)], [(o, c0, c0 + n)])
 
-    def ring_gather(b, h):
-        g0 = 256 * h
-        if b == 0:
-            gath("s", T.GR[:, g0:g0 + 256], T.RW[:, 0:V], T.EU16[:, 16 * h:16 * h + 16], [("RW", 0, V), ("EU16", 0, 128)], [("GR", g0, g0 + 256)])
-        else:
-            n, lu = V + E * b, "LW%d" % (b - 1)
-            gath("s", T.GR[:, g0:g0 + 256], T.RW[:, 0:n], T[lu][:, 64 + 16 * h:80 + 16 * h], [("RW", 0, n), (lu, 64, 96)], [("GR", g0, g0 + 256)])
-
-    def ring_sum(h):
-        cx, g0 = "CX%d" % h, 256 * h
+    def ring_list(b, h):
+        cx, of, g0 = "CX%d" % h, "OF%d" % b, 256 * h
+        lu, l0, n = ("EU16", 16 * h, V) if b == 0 else ("LW%d" % (b - 1), 64 + 16 * h, V + E * b)
+        step("rg%d" % h, "rs%d" % h)
+        act(T.GR[:, g0:g0 + 256], T.RW[:, 0:n].indirect(T[lu][:, l0:l0 + 16]), [("RW", 0, n), (lu, l0, l0 + 16), reg["big"], reg["keep"]], [("GR", g0, g0 + 256)],
+            F.Abs, bias=col["big"], scale=col["keep"])
         for a in range(4):
-            mm(T[cx][:, 0:64], T.RD[:, a, :], T.GR[:, g0 + a:g0 + 256:4], a == 0, a == 3, [("RD", 128 * a, 128 * a + 128), ("GR", g0, g0 + 256)], [(cx, 0, 64)], n=256)
+            mm(T[cx][:, 0:64], T.Y2[:, 12 - 4 * a:140 - 4 * a], T.GR[:, g0 + a:g0 + 256:4], a == 0, a == 3, [full("Y2"), ("GR", g0, g0 + 256)], [(cx, 0, 64)])
+        step("ro%d" % h)
+        copy("v", T[of][:, 64 * h:64 * h + 64], T[cx][:, 0:64], [(cx, 0, 64)], [(of, 64 * h, 64 * h + 64)])
 
-    def ring_out(b, h):
-        of, cx = "OF%d" % b, "CX%d" % h
-        tc(T[of][:, 64 * h:64 * h + 64], T[cx][:, 0:64], [(cx, 0, 64)], [(of, 64 * h, 64 * h + 64)])
+    def memory(q, b, out, src, reads, writes):
+        if q == "s":
+            act(out, src, reads, writes, F.Relu, **({"bias": 15.0, "scale": -1.0} if b else {}))
+        elif b:
+            ts(out, src, 15.0, -1.0, A.min, A.mult, reads, writes)
+        else:
+            ts(out, src, -15.0, None, A.add, None, reads, writes)
 
-    def ring_diff(b, h):
-        c0 = 128 * b + 64 * h
-        tt(T.DF[:, 64 * h:64 * h + 64], T.VW[:, c0:c0 + 64], T["CX%d" % h][:, 0:64], A.subtract, [("VW", c0, c0 + 64), ("CX%d" % h, 0, 64)], [("DF", 64 * h, 64 * h + 64)])
+    def wadd(src, h, start):
+        mm(T["W%d" % h][:, 0:256], T.ID[:], T[src][:, 256 * h:256 * h + 256], start, False, [full("ID"), full(src)], [("W%d" % h, 0, 256)])
 
     def mem_u(b):
+        step("u")
         tb, mu = "TB%d" % b, "MU%d" % (b % 2)
-        gath("s", T[mu][:], T[tb][:, own:own + V], T.EU16[:, 32 * b:32 * b + 32], [(tb, own, own + V), ("EU16", 0, 128)], [full(mu)])
+        memory("s", b, T[mu][:], T[tb][:, own:own + V].indirect(T.EU16[:, 32 * b:32 * b + 32]), [(tb, own, own + V), ("EU16", 0, 128)], [full(mu)])
+        for h in range(2):
+            step(None, "wu%d" % h)
+            wadd(mu, h, True)
 
     def mem_v(b):
+        step("v", "wv")
         tb, mv = "TB%d" % b, "MV%d" % (b % 2)
-        gath("s", T[mv][:], T[tb][:], T.EV16[:, 32 * b:32 * b + 32], [full(tb), ("EV16", 0, 128)], [full(mv)])
-        marks["mv"] = here()
-
-    def wadd(b, name, start):
-        src = name + "%d" % (b % 2)
+        memory("s", b, T[mv][:], T[tb][:].indirect(T.EV16[:, 32 * b:32 * b + 32]), [full(tb), ("EV16", 0, 128)], [full(mv)])
         for h in range(2):
-            mm(T["W%d" % h][:, 0:256], T.ID[:], T[src][:, 256 * h:256 * h + 256], start, False, [full("ID"), full(src)], [("W%d" % h, 0, 256)], n=256)
+            wadd(mv, h, False)
 
-    def block_half(b, h, dst, base):
-        n, c0 = V + E * (b + 1), base + 512 * h
-        op("s", lambda e: e.activation(T[dst][:, c0:c0 + 512], T.OB[:, 0:n].indirect(T["LW%d" % b][:, 32 * h:32 * h + 32]), F.Relu, bias=15.0, scale=-1.0),
-           [("OB", 0, n), ("LW%d" % b, 0, 64)], [(dst, c0, c0 + 512)], t=0.73)
-
-    def send_half(b, h):
+    def send(b, c0, c1, final):
         tb = "TB%d" % (b + 1)
-        c0 = own + 512 * h
-        ap = T[tb][:, c0:c0 + 512]
+        ap = T[tb][:, own + c0:own + c1]
         mask = topo.mask(core, peers[0])
         ids = []
         for p in peers:
@@ -346,255 +370,167 @@ def rank_program(g, core, T, topo):
             ids.append(DstId(rid=rid, pnc=pid))
         ne = bin(mask).count("1")
 
-        def send():
+        def call():
             g.remote_dma_fused([RemoteDMATransfer(dst_ids=ids, dma_engine_mask=mask, remote_sem=T.sem["arr%d" % b],
                                                   srcs=[ap], dsts=[ap] * len(ids))], local_sem=T.sem.sent)
             total["sent"] = total.get("sent", 0) + ne
 
         def arrive():
-            total["arr%d" % b] = 2 * ne * len(peers)
+            total["arr%d" % b] = len(SENDS) * ne * len(peers)
             for p in peers:
                 o = T.rank_of(p) * V
                 note("far", ("arr%d" % b, total["arr%d" % b], {}), [], [(tb, o, o + V)])
 
-        item(q="g", kind="send", fn=send, reads=[(tb, c0, c0 + 512)], writes=[("sends%d" % b, h, h + 1)], time=0.5, lag=0.0)
-        if h == 1:
-            item(q="far", kind="far", fn=arrive, reads=[("sends%d" % b, 0, 2)], writes=[(tb, T.rank_of(p) * V, T.rank_of(p) * V + V) for p in peers], time=0.0, lag=FAR)
+        item(q="g", kind="send", fn=call, reads=[(tb, own + c0, own + c1)], writes=[("sends%d" % b, c0, c1)])
+        if final:
+            item(q="far", kind="far", fn=arrive, reads=[("sends%d" % b, 0, V)], writes=[(tb, T.rank_of(p) * V, T.rank_of(p) * V + V) for p in peers])
 
-    place_scatter(0, 0, 1)
-    tc(T.EVF[:], T.EVI[:], [full("EVI")], [full("EVF")], n=128)
-    hold[0] = here()
-    place_scatter(0, 1, 2)
-    hold[0] = None
-    for k in range(3):
-        cp(T.CD[:, k, :], T.ID[:], [full("ID"), full("CK")], [("CD", 128 * k, 128 * k + 128)], scale=T.CK[:, k + 1:k + 2])
-    mm(T.DA0[:, 0:384], T.BO[:], T.CD[:], True, True, [full("BO"), full("CD")], [("DA0", 0, 384)], n=384)
-    for z in range(4):
-        mm(T.DA1[:, z::4], T.LV[:, z, :], T.EVF[:], True, True, [("LV", 128 * z, 128 * z + 128), full("EVF")], [full("DA1")], n=512)
-    cp(T.LD[:], T.DA0[:, 0:384], [("DA0", 0, 384)], [full("LD")], n=384)
-    hold[0] = here()
-    cp(T.VW[:], T.DA1[:], [full("DA1")], [full("VW")], n=512)
-    hold[0] = None
-    vw = here()
-    place_mm(0, 0)
-    tc(T.RW[:, 0:V], T.RI[:], [full("RI")], [("RW", 0, V)], n=V)
-    hold[0] = vw
-    ring_gather(0, 0)
-    hold[0] = None
-    ring_gather(0, 1)
-    r0 = here()
-    ring_sum(0)
-    ring_sum(1)
-    tc(T.EV16[:], T.EVI[:], [full("EVI")], [full("EV16")], n=128)
-    op("v", lambda e: e.memset(T.RS[:], 1.0), [], [full("RS")], n=512)
-    op("v", lambda e: e.memset(T.RS[:, 0::4], 0.0), [], [full("RS")], waw=True, n=128)
-    ring_out(0, 0)
-    ring_out(0, 1)
-    hold[0] = r0
-    mem_u(0)
-    hold[0] = here()
-    mem_v(0)
-    hold[0] = None
-    ts(T.OB[:, 0:V], T.TB0[:, own:own + V], -1.0, 15.0, A.mult, A.add, [("TB0", own, own + V)], [("OB", 0, V)], n=V // 2)
-    wadd(0, "MU", True)
+    def split(src, tmp, dst, n):
+        ts(T[tmp][:, 0:n], T[src][:], 31, None, A.bitwise_and, None, [full(src)], [(tmp, 0, n)])
+        ts(T[tmp][:, n:2 * n], T[src][:], 5, None, A.logical_shift_right, None, [full(src)], [(tmp, n, 2 * n)])
+        copy("v", T[dst][:], T[tmp][:], [full(tmp)], [full(dst)])
+
+    step("rdig", "rw")
+    split("RI", "RJ", "RD", 256)
     for a in range(4):
-        mm(T.LN[:, 128 * a:128 * a + 128], T.LE[:, a, :], T.IF[:], True, True, [("LE", 128 * a, 128 * a + 128), full("IF")], [full("LN")], n=512)
-    place_out(0, 0)
+        bk, c0 = "DA%d" % (a // 2), 256 * (a % 2)
+        for j in range(2):
+            mm(T[bk][:, c0:c0 + 256], T.ZA[:, a, 1 - j:129 - j], T.RD[:, 256 * j:256 * j + 256], j == 0, j == 1, [full("ZA"), full("RD")], [(bk, c0, c0 + 256)])
+    step("rws")
+    copy("s", T.RW[:, 0:512], T.DA0[:], [full("DA0")], [("RW", 0, 512)])
+    step("rwv")
+    copy(WHO["rwv"], T.RW[:, 512:V], T.DA1[:], [full("DA1")], [("RW", 512, V)])
+    step("cd")
+    for k in range(3):
+        affine(WHO["cd"], T.CD[:, k, :], T.ID[:], T.CK[:, k + 1:k + 2], 0.0, [full("ID"), full("CK")], [("CD", 128 * k, 128 * k + 128)])
+    step("ld")
+    mm(T.CX1[:, 0:384], T.BO[:], T.CD[:], True, True, [full("BO"), full("CD")], [("CX1", 0, 384)])
+    copy(WHO["ld"], T.LD[:], T.CX1[:, 0:384], [("CX1", 0, 384)], [full("LD")])
+    ring_list(0, 0)
+    ring_list(0, 1)
+    place_scatter(0, 0)
+    place_scatter(0, 1)
+    step("ev16")
+    copy("v", T.EV16[:], T.EVI[:], [full("EVI")], [full("EV16")])
+    step("vdig", "vw")
+    split("EVI", "EVJ", "EVD", 128)
+    for z in range(4):
+        for j in range(2):
+            mm(T.LN[:, z::4], T.LV[:, z, 1 - j:129 - j], T.EVD[:, 128 * j:128 * j + 128], j == 0, j == 1, [("LV", 144 * z, 144 * z + 144), full("EVD")], [full("LN")])
+    step("vw")
+    act(T.VW[:], T.LN[:], [full("LN")], [full("VW")], scale=-1.0)
+    place_next(0, "pn0")
+    place_mm(0)
+    mem_u(0)
+    step("obinit")
+    affine(WHO["obinit"], T.OB[:, 0:V], T.TB0[:, own:own + V], -1.0, 15.0, [("TB0", own, own + V)], [("OB", 0, V)])
 
     for b in range(NB):
         last = b == NB - 1
         tb, mt, mv, of = "TB%d" % b, "MT%d" % (b % 2), "MV%d" % (b % 2), "OF%d" % b
+        step(None, None, b + 1)
 
-        def slots(c, q):
+        def slots(c):
+            step("s%d" % c)
             s = 512 * c
-            gath(q, T[mt][:, s:s + 512], T[tb][:], T[of][:, 32 * c:32 * c + 32], [full(tb), (of, 32 * c, 32 * c + 32)], [(mt, s, s + 512)])
+            memory("vs"[c // 2], b, T[mt][:, s:s + 512], T[tb][:].indirect(T[of][:, 32 * c:32 * c + 32]), [full(tb), (of, 32 * c, 32 * c + 32)], [(mt, s, s + 512)])
 
-        def scan(c0, c1):
-            s = (512 * c0, 512 * c1)
-            n = s[1] - s[0]
+        def scan(c):
+            step("m%d" % c)
+            s = (512 * c, 512 * c + 512)
             x = T[mt][:, s[0]:s[1]]
-            op("v", lambda e: e.tensor_tensor_scan(T.MX[:, s[0]:s[1]], T.RS[:, 0:n], x, 0.0, A.mult, A.max),
-               [full("RS"), (mt,) + s], [("MX",) + s], n=n // 2)
-
-        def wsub(h):
-            s = (1024 * h, 1024 * h + 1024)
-            mm(T["W%d" % h][:, 0:256], T.NI[:], T.MX[:, s[0] + 3:s[1]:4], False, True, [full("NI"), ("MX",) + s], [("W%d" % h, 0, 256)], n=256)
+            op("v", lambda e: e.tensor_tensor_scan(T.MX[:, s[0]:s[1]], T.RS[:], x, 0.0, A.min, A.max), [full("RS"), (mt,) + s], [("MX",) + s])
 
         def clip(h):
-            o, w = V + E * b + 256 * h, "W%d" % h
-            op("s", lambda e: e.activation(T.OB[:, o:o + 256], T[w][:, 0:256], F.Relu, bias=15.0, scale=-1.0), [(w, 0, 256)], [("OB", o, o + 256)], n=256)
+            step("clip%d" % h, "ws%d" % h)
+            s, o, w = (1024 * h, 1024 * h + 1024), V + E * b + 256 * h, "W%d" % h
+            mm(T[w][:, 0:256], T.NI[:], T.MX[:, s[0] + 3:s[1]:4], False, True, [full("NI"), ("MX",) + s], [(w, 0, 256)])
+            act(T.OB[:, o:o + 256], T[w][:, 0:256], [(w, 0, 256)], [("OB", o, o + 256)], F.Relu, bias=(30.0, 15.0)[h], scale=-1.0)
 
         def where(h, j):
             return (("DA%d" % h, 0), ("DA%d" % h, 256), ("CX%d" % h, 256))[j]
 
         def diff(h):
+            step(None, "d%d" % h)
             s = (1024 * h, 1024 * h + 1024)
-            for j in range(3):
+            for j in (2, 0, 1):
                 bk, d = where(h, j)
                 for w, k in (("ID", j + 1), ("NI", 0)):
-                    mm(T[bk][:, d:d + 256], T[w][:], T[mt][:, s[0] + k:s[1]:4], w == "ID", w == "NI", [full(w), (mt,) + s], [(bk, d, d + 256)], n=256)
+                    mm(T[bk][:, d:d + 256], T[w][:], T[mt][:, s[0] + k:s[1]:4], w == "ID", w == "NI", [full(w), (mt,) + s], [(bk, d, d + 256)])
 
-        def prod(h, j):
-            bk, d = where(h, j)
-            p = 256 * (3 * h + j)
-            tt(T.PR[:, p:p + 256], T[bk][:, d:d + 256], T[mv][:, 256 * h:256 * h + 256], A.mult, [(bk, d, d + 256), full(mv)], [("PR", p, p + 256)], n=256)
-
-        def cdiff(h):
-            bk = "DA%d" % h
-            for j in range(3):
+        def lowest(h):
+            step("p%d" % h, "cd%d" % h)
+            for j in (2, 0, 1):
+                bk, d = where(h, j)
                 p = 256 * (3 * h + j)
-                mm(T[bk][:, 0:256], T.LD[:, j, :], T.PR[:, p:p + 256], j == 0, j == 2, [full("LD"), ("PR", p, p + 256)], [(bk, 0, 256)], n=256)
-
-        def sign(h):
-            bk = "DA%d" % h
-            op("s", lambda e: e.activation(T.SG[:, 256 * h:256 * h + 256], T[bk][:, 0:256], F.Sign, bias=T.CF[:, 2:3]),
-               [(bk, 0, 256), ("CF", 2, 3)], [("SG", 256 * h, 256 * h + 256)], n=256)
-
-        def count(h):
-            cx, s = "CX%d" % h, 256 * h
-            for a in range(4):
-                mm(T[cx][:, 0:64], T.LS[:, a, :], T.SG[:, s + a:s + 256:4], a == 0, a == 3, [full("LS"), ("SG", s, s + 256)], [(cx, 0, 64)], n=64)
-
-        def pick(h):
-            cx, c0 = "CX%d" % h, 64 * h
-            ts(T[cx][:, 64:128], T[cx][:, 0:64], 3.0, None, A.is_ge, None, [(cx, 0, 64)], [(cx, 64, 128)])
-            tt(T.ON[:, c0:c0 + 64], T[cx][:, 64:128], T.DF[:, c0:c0 + 64], A.mult, [(cx, 64, 128), ("DF", c0, c0 + 64)], [("ON", c0, c0 + 64)])
-
-        def spread(h):
-            ex, c0 = "W%d" % h, 64 * h
-            for a in range(4):
-                mm(T[ex][:, a:256:4], T.LE[:, a, :], T.ON[:, c0:c0 + 64], True, True, [("LE", 128 * a, 128 * a + 128), ("ON", c0, c0 + 64)], [(ex, 0, 256)], n=256)
+                tt(T.PR[:, p:p + 256], T[bk][:, d:d + 256], T[mv][:, 256 * h:256 * h + 256], A.mult, [(bk, d, d + 256), full(mv)], [("PR", p, p + 256)])
+            cx = "CX%d" % h
+            for i, j in enumerate((2, 0, 1)):
+                p = 256 * (3 * h + j)
+                mm(T[cx][:, 0:256], T.LD[:, j, :], T.PR[:, p:p + 256], i == 0, i == 2, [full("LD"), ("PR", p, p + 256)], [(cx, 0, 256)])
+            step("sg%d" % h)
+            act(T.SG[:, 256 * h:256 * h + 256], T[cx][:, 0:256], [(cx, 0, 256), reg["tie"]], [("SG", 256 * h, 256 * h + 256)], F.Sign, bias=col["tie"])
 
         def renew(h):
-            ex, o, g0 = "W%d" % h, V + E * b + 256 * h, 256 * h
-            tt(T.RW[:, o:o + 256], T[ex][:, 0:256], T.GR[:, g0:g0 + 256], A.add, [(ex, 0, 256), ("GR", g0, g0 + 256)], [("RW", o, o + 256)], n=256)
+            step(None, "of%d" % h)
+            w, c0, s, o = ("LN", "LX")[h], 128 * b + 64 * h, 256 * h, V + E * b + 256 * h
+            mm(T[w][:, 256:512], T.ZR[:, 0:128], T.RS[:, 0:256], True, False, [full("ZR"), full("RS")], [(w, 256, 512)])
+            for a in range(4):
+                mm(T[w][:, 256 + a:512:4], T.SV[:, a, :], T.VW[:, c0:c0 + 64], False, False, [full("SV"), full("VW")], [(w, 256, 512)])
+            step("rn%d" % h, "ct%d" % h)
+            mm(T[w][:, 256:512], T.LC[:], T.SG[:, s:s + 256], False, True, [full("LC"), ("SG", s, s + 256)], [(w, 256, 512)])
+            tt(T.RW[:, o:o + 256], T[w][:, 256:512], T.GR[:, s:s + 256], A.min, [(w, 256, 512), ("GR", s, s + 256)], [("RW", o, o + 256)])
 
-        if b:
-            hold[0] = marks["ring"]
-            mem_v(b)
-        hold[0] = marks["mv"]
-        slots(0, "v")
-        slots(1, "s")
-        slots(2, "s")
-        s2 = here()
-        slots(3, "v")
-        hold[0] = None
-        if b == 0:
-            hold[0] = s2
-            cp(T.LS[:], T.LN[:], [full("LN")], [full("LS")], n=512)
-            hold[0] = None
-        wadd(b, "MV", False)
-        if last:
-            diff(0)
-            scan(0, 2)
-            ring_diff(b, 0)
-            ring_diff(b, 1)
-            for j in (2, 0, 1):
-                prod(0, j)
-            p0 = here()
-            diff(1)
-            hold[0] = here()
-            cdiff(0)
-            c0 = here()
-            sign(0)
-            hold[0] = p0
-            for j in (2, 0, 1):
-                prod(1, j)
-            hold[0] = None
-            wsub(0)
-            count(0)
-            hold[0] = c0
-            cdiff(1)
-            hold[0] = None
-            sign(1)
-            scan(2, 4)
-            wsub(1)
-            count(1)
-            pick(0)
-            place_out(b, 0)
-            pick(1)
-            clip(0)
-            clip(1)
-            spread(0)
-            hold[0] = here()
-            spread(1)
-            hold[0] = None
-            renew(0)
-            renew(1)
-            n = V + E * NB
-            for h in range(2):
-                gath("sv"[h], T.YR[:, 512 * h:512 * h + 512], T.RW[:, 0:n], T.LW3[:, 32 * h:32 * h + 32], [("RW", 0, n), ("LW3", 0, 64)], [("YR", 512 * h, 512 * h + 512)])
-                dmas([("ys"[k % 2], T.yr[k::4, 512 * h:512 * h + 512], T.YR[k::16, 512 * h:512 * h + 512]) for k in range(4)], [("YR", 512 * h, 512 * h + 512)], [])
-            for h in range(2):
-                block_half(b, h, "YB", 0)
-                dmas([("y", T.ym[:, 512 * h:512 * h + 512], T.YB[:, 512 * h:512 * h + 512])], [("YB", 512 * h, 512 * h + 512)], [])
-            continue
-        diff(0)
-        scan(0, 2)
-        wsub(0)
-        ring_diff(b, 0)
-        ring_diff(b, 1)
-        if b:
-            place_out(b, 2)
-        scan(2, 3)
-        clip(0)
-        scan(3, 4)
-        wsub(1)
-        prod(0, 2)
-        clip(1)
-        diff(1)
-        for h in range(2):
-            block_half(b, h, "TB%d" % (b + 1), own)
-            blk = here()
-            send_half(b, h)
-        if b == 0:
-            hold[0] = blk
-            place_next(b)
-            place_mm(b, 1)
-            hold[0] = None
+        mem_v(b)
+        for c in range(4):
+            slots(c)
+            scan(c)
+        place_out(b, 0)
+        if 0 < b < NB - 1:
+            place_mm(1)
             place_out(b, 1)
-        prod(0, 0)
-        prod(0, 1)
-        hold[0] = here()
-        cdiff(0)
-        c0 = here()
-        sign(0)
-        for j in range(3):
-            prod(1, j)
-        hold[0] = None
-        p1 = here()
-        count(0)
-        hold[0] = c0
-        cdiff(1)
-        hold[0] = None
-        mem_u(b + 1)
-        sign(1)
-        count(1)
-        hold[0] = p1
-        place_scatter(b + 1, 0, 1)
-        hold[0] = None
-        pick(0)
-        spread(0)
-        hold[0] = here()
-        pick(1)
-        spread(1)
-        hold[0] = None
-        renew(0)
-        renew(1)
-        hold[0] = here()
-        place_scatter(b + 1, 1, 2)
-        hold[0] = None
-        ring_gather(b + 1, 0)
-        ring_gather(b + 1, 1)
-        marks["ring"] = here()
-        ring_sum(0)
-        ring_sum(1)
-        wadd(b + 1, "MU", True)
-        if b + 2 < NB:
-            place_next(b + 1)
-        place_mm(b + 1, 2 if b + 2 < NB else 0)
-        ring_out(b + 1, 0)
-        ring_out(b + 1, 1)
+        for h in range(2):
+            diff(h)
+            clip(h)
+        n, lw = V + E * (b + 1), "LW%d" % b
+        if not last:
+            step("blk")
+            nx = "TB%d" % (b + 1)
+            for q, c0, c1 in PIECES:
+                copy(q, T[nx][:, own + c0:own + c1], T.OB[:, 0:n].indirect(T[lw][:, c0 // 16:c1 // 16]), [("OB", 0, n), (lw, 0, 64)], [(nx, own + c0, own + c1)])
+            for c0, c1 in SENDS:
+                send(b, c0, c1, (c0, c1) == SENDS[-1])
+        for h in range(2):
+            lowest(h)
+            renew(h)
+        if b == 0:
+            place_mm(1)
+            place_out(b, 1)
+        if not last:
+            mem_u(b + 1)
+            place_scatter(b + 1, 0)
+            place_scatter(b + 1, 1)
+            for h in range(2):
+                ring_list(b + 1, h)
+            if b + 2 < NB:
+                place_next(b + 1)
+            place_mm(0)
+
+    rd = [("RW", 0, n), (lw, 0, 64)]
+    step("yg", "yr")
+    act(T.YG[:, 0:512], T.RW[:, 0:n].indirect(T[lw][:, 0:32]), rd, [("YG", 0, 512)], F.Relu)
+    ts(T.YG[:, 512:V], T.RW[:, 0:n].indirect(T[lw][:, 32:64]), 0.0, None, A.max, None, rd, [("YG", 512, V)])
+    for a in range(4):
+        mm(T.DA0[:, 0:256], T.Y1[:, 3 - a:131 - a], T.YG[:, 256 * a:256 * a + 256], a == 0, a == 3, [full("Y1"), ("YG", 256 * a, 256 * a + 256)], [("DA0", 0, 256)])
+    step("yr")
+    copy("v", T.YR[:], T.DA0[:, 0:256], [("DA0", 0, 256)], [full("YR")])
+    for h in range(2):
+        step("blk%d" % h)
+        c0 = 512 * h
+        act(T.YB[:, c0:c0 + 512], T.OB[:, 0:n].indirect(T[lw][:, 32 * h:32 * h + 32]), [("OB", 0, n), (lw, 0, 64)], [("YB", c0, c0 + 512)], F.Relu, bias=15.0, scale=-1.0)
+    outs = {"yr": (T.yr[:], T.YR[:], full("YR")), "ym0": (T.ym[:, 0:512], T.YB[:, 0:512], ("YB", 0, 512)), "ym1": (T.ym[:, 512:V], T.YB[:, 512:V], ("YB", 512, V))}
+    for name in ("ym0", "yr", "ym1"):
+        dmas([("y",) + outs[name][0:2]], [outs[name][2]], [])
     for j in plan():
         emit(prog[j])
     for s in total:

@@ -3,44 +3,54 @@ from concourse.mybir import AluOpType as A, ActivationFunctionType as F
 
 NB, V, E, R = 4, 1024, 512, 4
 BF, F32, I32, U16 = "bfloat16", "float32", "int32", "uint16"
-BIG = 128.0
-PIECES = (("s", 0, 512), ("s", 512, 1024))
-SENDS = ((0, 512), (512, 1024))
-START = {"v": "fill cols cols2 eu16 rdig scat0 scat1 ld ev16 ro0 ro1",
-         "s": "cols pz0 lldig cd ni rws rwv rg0 rg1 u",
-         "p": "rw ld rs0 rs1 pm0 wu0 wu1"}
-FIRST = {"v": "s0 s1 m0 m1 obinit m2 m3 po vdig p0 blk p1 pz1 lc scat0 rn0 rn1 pnout scat1 ro0 ro1 pz2",
-         "s": "v s2 s3 clip0 pn0 clip1 blk vw sg0 sg1 u rg0 rg1 pn",
-         "p": "wv d0 ws0 ws1 d1 vw cd0 cd1 of0 of1 ct0 ct1 pm1 wu0 rs0 wu1 rs1 pm0"}
-TURN = {"v": "s0 s1 m0 m1 m2 pnout m3 po p0 blk p1 scat0 rn0 rn1 scat1 ro0 ro1 pz3",
-        "s": "v s2 s3 clip0 clip1 blk sg0 sg1 u rg0 rg1 pn",
-        "p": "pm1 wv d0 ws0 ws1 d1 of0 cd0 cd1 of1 ct0 ct1 wu0 wu1 rs0 rs1 pm0"}
-LAST = {"v": "po s0 s1 m0 m1 m2 m3 p0 p1 rn0 rn1 yg yr",
-        "s": "v s2 s3 clip0 clip1 blk0 sg0 sg1 yg blk1",
-        "p": "of0 of1 wv d0 ws0 ws1 d1 cd0 cd1 ct0 ct1 yr"}
-WHO = {"pz0": "s", "pz1": "v", "pz2": "v", "pz3": "v", "cd": "s", "pn0": "s", "pn": "s", "obinit": "v", "lldig": "s", "rwv": "s", "ld": "v"}
+LOW, HIGH, LIFT = 256.0, 8192.0, 129
+PIECES = (("s", 0, 256), ("s", 256, 640), ("s", 640, 1024))
+SENDS = ((0, 256), (256, 640), (640, 1024))
+NEXT = (("s", 0, 256), ("v", 256, 512))
+YPIECES = (("s", 0, 640), ("s", 640, 1024))
+YORDER = (0, 2, 1, 3)
+OUTS = (("y", "ym0"), ("y", "ym1"), ("s", "yr"))
+SUB = (1, 1, 1, 0)
+START = {"v": "fill cols cols2 lldig eu16 rdig scat0 scat1 ev16 vdig ro0 ro1",
+         "s": "cols pz0 cols2 cd ni ld rws rwv rg0 rg1 u",
+         "p": "ld rw rs0 rs1 pm0 wu0 wu1",
+         "g": "rows id bo za y2 rs zb lv lc sv"}
+FIRST = {"v": "s0 m0 m1 po m2 m3 clip1 p0 p1 pn1 hb pnout scat0 rn0 rn1 scat1 ro0 ro1",
+         "s": "v s2 s3 pn0 clip0 blk0 blk1 blk2 vw sg0 sg1 u rg0 rg1",
+         "p": "wv vw d0 ws0 e0 ws1 d1 e1 cd0 cd1 pm1 pm1b of0 of1 ct0 ct1 wu0 wu1 rs0 rs1 pm0",
+         "g": "send sv3 y1"}
+TURN = {"v": "s0 po m0 m2 m3 clip1 p0 p1 pn1 scat0 pnout rn0 rn1 scat1 ro0 ro1",
+        "s": "v s2 s3 pn0 clip0 blk0 blk1 blk2 sg0 sg1 u rg0 rg1",
+        "p": "of0 wv d0 of1 ws0 e0 d1 e1 cd0 cd1 pm1 pm1b ct0 ct1 wu0 wu1 rs0 rs1 pm0",
+        "g": "send"}
+LAST = {"v": "s0 po m0 m2 m3 p0 p1 top0 rn0 rn1 yg2 yg3 top1",
+        "s": "v s2 s3 clip0 clip1 blk0 sg0 sg1 blk1 yg0 yg1 yr",
+        "p": "of0 wv d0 of1 ws0 e0 ws1 d1 e1 cd0 cd1 ct0 ct1 yr",
+        "g": ""}
+WHO = {"pz0": "s", "hb": "v", "ni": "s", "cd": "s", "lldig": "v", "rwv": "s", "ld": "s", "vw": "s",
+       "yg0": "s", "yg1": "s", "yg2": "v", "yg3": "v", "yr": "s"}
 
 SCRATCH = {
     "OB": ("sbuf", [128, V + NB * E], BF),
     "RW": ("sbuf", [128, V + NB * E], BF),
-    "RI": ("sbuf", [128, 256], I32), "RJ": ("sbuf", [128, 512], I32), "RD": ("sbuf", [128, 512], BF),
-    "EUI": ("sbuf", [128, 128], I32), "EVI": ("sbuf", [128, 128], I32), "EVJ": ("sbuf", [128, 256], I32), "EVD": ("sbuf", [128, 256], BF),
+    "RI": ("sbuf", [128, 256], I32), "RJ": ("sbuf", [128, 256], I32), "RD": ("sbuf", [128, 512], BF),
+    "EUI": ("sbuf", [128, 128], I32), "EVI": ("sbuf", [128, 128], I32), "EVJ": ("sbuf", [128, 128], I32), "EVD": ("sbuf", [128, 256], BF),
     "EU16": ("sbuf", [128, 128], U16), "EV16": ("sbuf", [128, 128], U16),
     "MX": ("sbuf", [128, 2048], BF), "PR": ("sbuf", [128, 1536], BF),
     "SG": ("sbuf", [128, 512], BF), "GR": ("sbuf", [128, 512], BF),
     "VW": ("sbuf", [128, 512], BF),
     "YB": ("sbuf", [128, V], BF), "YG": ("sbuf", [128, V], BF), "YR": ("sbuf", [128, 256], F32),
-    "ONE": ("sbuf", [128, 528], BF), "PM": ("sbuf", [128, 128], BF), "ZR": ("sbuf", [128, 144], BF),
+    "ONE": ("sbuf", [128, 528], BF), "NM": ("sbuf", [128, 128], BF), "M1": ("sbuf", [128, 256], BF), "ZR": ("sbuf", [128, 144], BF),
     "ID": ("sbuf", [128, 128], BF), "NI": ("sbuf", [128, 128], BF),
-    "ZL": ("sbuf", [128, 144], BF), "ZB": ("sbuf", [128, 144], BF), "RQ": ("sbuf", [128, 16], F32), "QH": ("sbuf", [128, 16], F32),
-    "XL": ("sbuf", [128, 272], BF), "Q4": ("sbuf", [128, 128], BF), "PZ": ("sbuf", [128, NB * E], BF),
-    "ZA": ("sbuf", [128, 4, 132], BF), "LV": ("sbuf", [128, 4, 144], BF), "YL": ("sbuf", [128, 144], BF), "Y2": ("sbuf", [128, 144], BF),
-    "Y1": ("sbuf", [128, 144], BF), "LC": ("sbuf", [128, 32, 4], BF), "SV": ("sbuf", [128, 4, 128], BF),
-    "BO": ("sbuf", [128, 128], BF), "B1": ("sbuf", [128, 128], BF),
+    "ZB": ("sbuf", [128, 144], BF), "RQ": ("sbuf", [128, 16], F32), "QH": ("sbuf", [128, 16], F32),
+    "XL": ("sbuf", [128, 256], BF), "PZ": ("sbuf", [128, E], BF), "HB": ("sbuf", [128, NB - 1, 256], BF),
+    "ZA": ("sbuf", [128, 4, 132], BF), "LV": ("sbuf", [128, 4, 144], BF), "Y2": ("sbuf", [128, 144], BF),
+    "Y1": ("sbuf", [128, 144], BF), "LC": ("sbuf", [128, 128], BF), "SV": ("sbuf", [128, 4, 128], BF),
+    "BO": ("sbuf", [128, 128], BF), "B1": ("sbuf", [128, 128], BF), "B2": ("sbuf", [128, 128], BF),
     "LD": ("sbuf", [128, 3, 128], BF), "CD": ("sbuf", [128, 3, 128], BF),
     "CA": ("sbuf", [128, 4], F32), "CJ": ("sbuf", [128, 4], F32), "CK": ("sbuf", [128, 4], F32),
-    "RS": ("sbuf", [128, 512], BF), "LL": ("sbuf", [128, V + E], BF),
-    "PC": ("sbuf", [128, 8], I32), "CF": ("sbuf", [128, 24], F32),
+    "RS": ("sbuf", [128, 1024], BF), "LL": ("sbuf", [128, V + E], BF),
+    "PC": ("sbuf", [128, 8], I32), "CF": ("sbuf", [128, 8], F32),
     "W0": ("psum", [128, 512], F32), "W1": ("psum", [128, 512], F32), "LX": ("psum", [128, 512], F32), "LN": ("psum", [128, 512], F32),
     "DA0": ("psum", [128, 512], F32), "DA1": ("psum", [128, 512], F32), "CX0": ("psum", [128, 512], F32), "CX1": ("psum", [128, 512], F32),
 }
@@ -91,7 +101,7 @@ def rank_program(g, core, T, topo):
                     same = aq == q and not dma
                     if mode == 0 and ((aw and hit) or (ps and not same)):
                         deps.append(rec)
-                    elif mode == 1 and (not same or (aw and waw)):
+                    elif mode == 1 and (not same or waw):
                         deps.append(rec)
         for rec in sorted(deps, key=lambda x: -sum(x[2].values()) - x[1]):
             wait(q, rec)
@@ -133,8 +143,9 @@ def rank_program(g, core, T, topo):
             stage[0] = turn
 
     def item(**k):
-        turn, name, k["at"] = stage[0], stage[2 if k["q"] == "p" else 1], (0, 0)
-        if k["q"] in "vsp" and k["kind"] == "op":
+        turn, name = stage[0], stage[2 if k["q"] == "p" else 1]
+        k["at"] = (turn and len(turns), 0)
+        if k["q"] in "vspg" and k["kind"] != "dma":
             while name not in turns[turn][k["q"]].split():
                 turn += 1
             k["at"] = (turn, 1 + turns[turn][k["q"]].split().index(name))
@@ -183,7 +194,7 @@ def rank_program(g, core, T, topo):
                 left[i] -= 1
                 if not left[i]:
                     line.append(i)
-        assert len(line) == n, [(prog[j]["q"], prog[j]["at"]) for j in range(n) if left[j]][:9]
+        assert len(line) == n
         return line
 
     def full(n):
@@ -234,92 +245,104 @@ def rank_program(g, core, T, topo):
 
     step("fill")
     one = T.ONE[:, 0:128]
-    op("v", lambda e: e.memset(T.ONE[:], 1.0), [], [full("ONE")])
-    op("v", lambda e: e.memset(T.ZR[:], 0.0), [], [full("ZR")])
+    for name, x in (("ONE", 1.0), ("ZR", 0.0), ("M1", -1.0)):
+        op("v", lambda e, name=name, x=x: e.memset(T[name][:], x), [], [full(name)])
+    step("rows")
     op("g", lambda e: e.iota(T.PC[:, 0:1], [[0, 1]], 0, 1), [], [("PC", 0, 1)])
     iota("RQ", [[1, 16]])
-    iota("XL", [[1, 272]], -16)
+    iota("XL", [[1, 256]])
+    step("za")
     sel(T.ZA[:], T.ONE[:], [[-1, 4], [-4, 33], [1000, 4]], A.is_equal, -1000, [full("ONE")], [full("ZA")])
+    step("id")
     sel(T.ID[:], one, [[-1, 128]], A.is_equal, 0, [full("ONE")], [full("ID")])
-    sel(T.B1[:], one, [[-16, 8], [0, 16]], A.is_ge, 0, [full("ONE")], [full("B1")])
-    sel(T.BO[:], T.B1[:], [[16, 8], [0, 16]], A.is_ge, 15, [full("B1")], [full("BO")], cm=-1)
-    sel(T.YL[:], T.ZR[:], [[-16, 9], [1000, 4], [-4, 4]], A.not_equal, -3000, [full("ZR")], [full("YL")], 1.0)
-    sel(T.Y2[:], T.YL[:], [[-16, 9], [1000, 4], [-4, 4]], A.not_equal, -3001, [full("YL")], [full("Y2")], 32.0)
-    sel(T.ZL[:], T.ZR[:], [[-16, 9], [1000, 16]], A.not_equal, -15000, [full("ZR")], [full("ZL")], 1.0)
-    sel(T.ZB[:], T.ZL[:], [[-16, 9], [1000, 16]], A.not_equal, -15001, [full("ZL")], [full("ZB")], 256.0)
-    iota("RS", [[0, 128], [32, 4]], -16)
+
+    def blocks(out, tmp, src, n):
+        sel(T[tmp][:], T[src][:, 0:128], [[-n, 128 // n], [0, n]], A.is_ge, 0, [full(src)], [full(tmp)])
+        sel(T[out][:], T[tmp][:], [[n, 128 // n], [0, n]], A.is_ge, n - 1, [full(tmp)], [full(out)], cm=-1)
+
+    def marks(name, out, pat, base, values):
+        step(name)
+        src = "ZR"
+        for j, x in enumerate(values):
+            sel(T[out][:], T[src][:], pat, A.not_equal, base - j, [full(src)], [full(out)], x)
+            src = out
+
+    step("bo")
+    blocks("BO", "B1", "ONE", 16)
+    marks("y2", "Y2", [[-16, 9], [1000, 4], [-4, 4]], -3000, (LOW, HIGH))
+    marks("zb", "ZB", [[-16, 9], [1000, 16]], -15000, (1.0, 256.0))
+    marks("y1", "Y1", [[-4, 36], [1000, 4]], -3000, (LOW, HIGH, LOW, HIGH))
+    step("rs")
+    op("g", lambda e: e.iota(T.RS[:, 0:256], [[0, 64], [32, 4]], -16, 0, allow_small_or_imprecise_dtypes=True), [], [("RS", 0, 256)])
+    dmas([("y", T.RS[:, c:c + 256], T.RS[:, 0:256]) for c in (256, 512, 768)], [("RS", 0, 256)], [("RS", 256, 1024)])
+    dmas([("y", T.OB[:, 0:V], T.TB0[:, own:own + V])], [full("TB0")], [("OB", 0, V)])
+    step("lv")
     for z in range(4):
         sel(T.LV[:, z, :], T.ONE[:, 0:144], [[-16, 9], [-1, 4], [1000, 4]], A.is_equal, -1000 - 4 * z, [full("ONE")], [("LV", 144 * z, 144 * z + 144)])
-    iota("Q4", [[1, 32], [0, 4]])
-    sel(T.PM[:], one, [[0, 32], [-1, 2], [0, 2]], A.is_equal, 0, [full("ONE")], [full("PM")], -1.0, 0)
+    step("lc")
+    sel(T.NM[:], one, [[0, 32], [1, 2], [0, 2]], A.is_equal, -1, [full("ONE")], [full("NM")], -1.0, 0)
+    blocks("LC", "B2", "NM", 4)
     for a in range(4):
-        sel(T.SV[:, a, :], T.PM[:], [[-16, 8], [0, 8], [-1, 2]], A.is_equal, -4 * a, [full("PM")], [("SV", 128 * a, 128 * a + 128)])
+        step("sv" if a < 3 else "sv3")
+        sel(T.SV[:, a, :], T.NM[:], [[-16, 8], [0, 8], [-1, 2]], A.is_equal, -4 * a, [full("NM")], [("SV", 128 * a, 128 * a + 128)])
 
-    names = ["odd", "lo", "hi", "g4", "p4", "even", "ge", "tie", "eq", "wc", "lc", "w1", "keep", "big"]
+    names = ["odd", "lo", "hi", "even", "tie", "keep", "big"]
     col = {n: T.CF[:, i:i + 1] for i, n in enumerate(names)}
     reg = {n: ("CF", i, i + 1) for i, n in enumerate(names)}
     step("cols")
-    for i, (sh, m) in enumerate(((0, 1), (0, 3), (2, 3), (2, 28), (0, 124))):
+    for i, (sh, m) in enumerate(((0, 1), (0, 3), (2, 3))):
         ts(T.PC[:, i + 1:i + 2], T.PC[:, 0:1], sh, m, A.logical_shift_right, A.bitwise_and, [("PC", 0, 1)], [("PC", i + 1, i + 2)])
-    copy("v", T.CF[:, 0:5], T.PC[:, 1:6], [("PC", 1, 6)], [("CF", 0, 5)])
-
-    def lin(out, x, scale, bias):
-        affine("s", col[out], col[x], scale, col.get(bias, bias), [reg[x]] + ([reg[bias]] if bias in reg else []), [reg[out]])
-
-    def cmp(out, x, s1, s2, o):
-        ts(col[out], col[x], col.get(s1, s1), s2, o, A.mult, [reg[x]] + ([reg[s1]] if s1 in reg else []), [reg[out]])
-
+    copy("v", T.CF[:, 0:3], T.PC[:, 1:4], [("PC", 1, 4)], [("CF", 0, 3)])
     ts(T.QH[:], T.RQ[:], col["odd"], None, A.mult, None, [full("RQ"), reg["odd"]], [full("QH")])
-    cmp("eq", "hi", "lo", 4 * BIG, A.is_equal)
-    cmp("keep", "lo", 2.0, 1.0, A.is_lt)
-    cmp("ge", "hi", "lo", 1.0, A.is_ge)
-    lin("even", "odd", -1.0, 1.0)
-    lin("lc", "g4", 1.0, "lo")
-    lin("w1", "odd", 31.0, 1.0)
-    lin("wc", "eq", 1.0, -BIG)
-    lin("big", "keep", -BIG, BIG)
-    lin("tie", "ge", 1.0, -0.5)
+    affine("s", col["even"], col["odd"], -1.0, 1.0, [reg["odd"]], [reg["even"]])
     step("cols2")
     ts(T.CJ[:], T.RQ[:, 0:4], col["lo"], None, A.is_equal, None, [full("RQ"), reg["lo"]], [full("CJ")])
     ts(T.CA[:], T.RQ[:, 0:4], col["hi"], None, A.is_equal, None, [full("RQ"), reg["hi"]], [full("CA")])
-    tt(T.CK[:], T.CA[:], T.CJ[:], A.subtract, [full("CA"), full("CJ")], [full("CK")])
-    step("lc")
-    ts(T.LC[:], T.Q4[:], col["lc"], col["wc"], A.is_equal, A.mult, [full("Q4"), reg["lc"], reg["wc"]], [full("LC")])
-    ts(T.Y1[:], T.XL[:, 13:157], col["p4"], col["w1"], A.is_equal, A.mult, [full("XL"), reg["p4"], reg["w1"]], [full("Y1")])
-    ts(T.LC[:, :, 2:4], T.LC[:, :, 2:4], -1.0, None, A.mult, None, [full("LC")], [full("LC")])
+    ts(col["keep"], col["lo"], 2.0, None, A.is_lt, None, [reg["lo"]], [reg["keep"]])
+    tt(T.CK[:], T.CJ[:], T.CA[:], A.subtract, [full("CA"), full("CJ")], [full("CK")])
+    ts(col["tie"], col["lo"], col["hi"], -0.5, A.is_ge, A.add, [reg["lo"], reg["hi"]], [reg["tie"]])
+    affine("s", col["big"], col["keep"], -1.0, 1.0, [reg["keep"]], [reg["big"]])
 
     def digits(name, buf, c0, n):
         step(name)
-        affine(WHO[name], T[buf][:, c0:c0 + 256], T.XL[:, 16:272], col["even"], T.QH[:, n:n + 1], [full("XL"), reg["even"], ("QH", n, n + 1)], [(buf, c0, c0 + 256)])
+        affine(WHO[name], T[buf][:, c0:c0 + 256], T.XL[:], col["even"], T.QH[:, n:n + 1], [full("XL"), reg["even"], ("QH", n, n + 1)], [(buf, c0, c0 + 256)])
 
     for n in range(4):
         digits("lldig", "LL", 256 * n, n)
-    for n in range(8):
-        digits("pz%d" % (n // 2), "PZ", 256 * n, n + 4)
+    for n in range(2):
+        digits("pz0", "PZ", 256 * n, n + 4)
+    step("hb")
+    for b in range(1, NB):
+        affine(WHO["hb"], T.HB[:, b - 1, :], T.ONE[:, 0:256], T.QH[:, 2 * b:2 * b + 1], 0.0, [full("ONE"), ("QH", 2 * b, 2 * b + 1)], [("HB", 256 * b - 256, 256 * b)])
     step("ni")
-    act(T.NI[:], T.ID[:], [full("ID")], [full("NI")], scale=-1.0)
+    affine(WHO["ni"], T.NI[:], T.ID[:], -1.0, 0.0, [full("ID")], [full("NI")])
     step("eu16")
     copy("v", T.EU16[:], T.EUI[:], [full("EUI")], [full("EU16")])
 
     def place_scatter(b, h):
         step("scat%d" % h)
-        src = T.PZ[:, E * b + 256 * h:E * b + 256 * h + 256]
+        src, rd = T.PZ[:, 256 * h:256 * h + 256], [full("PZ"), ("EU16", 0, 128)]
         dst = T.LL[:, 0:V].indirect(T.EU16[:, 32 * b + 16 * h:32 * b + 16 * h + 16])
-        op("v", lambda e: e.tensor_copy(dst, src), [("PZ", E * b, E * b + E), ("EU16", 0, 128)], [("LL", 0, V)], waw=True)
+        if b:
+            op("v", lambda e: e.tensor_tensor(dst, src, T.HB[:, b - 1, :], A.add), rd + [("HB", 256 * b - 256, 256 * b)], [("LL", 0, V)], waw=True)
+        else:
+            op("v", lambda e: e.tensor_copy(dst, src), rd, [("LL", 0, V)], waw=True)
 
-    def place_next(b, name="pn"):
-        step(name)
-        copy(WHO[name], T.LL[:, V:V + E], T.LL[:, 0:V].indirect(T.EU16[:, 32 * b + 32:32 * b + 64]), [("LL", 0, V), ("EU16", 0, 128)], [("LL", V, V + E)])
+    def place_next(b):
+        for i, (q, c0, c1) in enumerate(NEXT):
+            step("pn%d" % i)
+            l0 = 32 * b + 32
+            copy(q, T.LL[:, V + c0:V + c1], T.LL[:, 0:V].indirect(T.EU16[:, l0 + c0 // 16:l0 + c1 // 16]), [("LL", 0, V), ("EU16", 0, 128)], [("LL", V + c0, V + c1)])
 
-    def place_mm(part):
-        step(None, "pm%d" % part)
-        lx, c0, n = ("LX", "DA1")[part], (0, V)[part], (64, 32)[part]
+    def place_mm(part, lx):
+        c0, n = (0, V)[part], (64, 32)[part]
         for i in range(16):
+            step(None, ("pm0", "pm1b" if i >= 8 else "pm1")[part])
             mm(T[lx][:, 0:n], T.ZB[:, 15 - i:143 - i], T.LL[:, c0 + i:c0 + 16 * n:16], i == 0, i == 15, [full("ZB"), ("LL", c0, c0 + 16 * n)], [(lx, 0, n)])
 
-    def place_out(b, part):
+    def place_out(b, part, lx):
         step(("po", "pnout")[part])
-        o, lx, n, c0 = "LW%d" % b, ("LX", "DA1")[part], (64, 32)[part], (0, 64)[part]
+        o, n, c0 = "LW%d" % b, (64, 32)[part], (0, 64)[part]
         copy("v", T[o][:, c0:c0 + n], T[lx][:, 0:n], [(lx, 0, n)], [(o, c0, c0 + n)])
 
     def ring_list(b, h):
@@ -331,7 +354,7 @@ def rank_program(g, core, T, topo):
         for a in range(4):
             mm(T[cx][:, 0:64], T.Y2[:, 12 - 4 * a:140 - 4 * a], T.GR[:, g0 + a:g0 + 256:4], a == 0, a == 3, [full("Y2"), ("GR", g0, g0 + 256)], [(cx, 0, 64)])
         step("ro%d" % h)
-        copy("v", T[of][:, 64 * h:64 * h + 64], T[cx][:, 0:64], [(cx, 0, 64)], [(of, 64 * h, 64 * h + 64)])
+        ts(T[of][:, 64 * h:64 * h + 64], T[cx][:, 0:64], -32.0 * LIFT, None, A.add, None, [(cx, 0, 64)], [(of, 64 * h, 64 * h + 64)])
 
     def memory(q, b, out, src, reads, writes):
         if q == "s":
@@ -341,8 +364,8 @@ def rank_program(g, core, T, topo):
         else:
             ts(out, src, -15.0, None, A.add, None, reads, writes)
 
-    def wadd(src, h, start):
-        mm(T["W%d" % h][:, 0:256], T.ID[:], T[src][:, 256 * h:256 * h + 256], start, False, [full("ID"), full(src)], [("W%d" % h, 0, 256)])
+    def wadd(src, h, start, stop=False):
+        mm(T["W%d" % h][:, 0:256], T.ID[:], T[src][:, 256 * h:256 * h + 256], start, stop, [full("ID"), full(src)], [("W%d" % h, 0, 256)])
 
     def mem_u(b):
         step("u")
@@ -357,7 +380,7 @@ def rank_program(g, core, T, topo):
         tb, mv = "TB%d" % b, "MV%d" % (b % 2)
         memory("s", b, T[mv][:], T[tb][:].indirect(T.EV16[:, 32 * b:32 * b + 32]), [full(tb), ("EV16", 0, 128)], [full(mv)])
         for h in range(2):
-            wadd(mv, h, False)
+            wadd(mv, h, False, bool(h and SUB[b]))
 
     def send(b, c0, c1, final):
         tb = "TB%d" % (b + 1)
@@ -386,20 +409,20 @@ def rank_program(g, core, T, topo):
             item(q="far", kind="far", fn=arrive, reads=[("sends%d" % b, 0, V)], writes=[(tb, T.rank_of(p) * V, T.rank_of(p) * V + V) for p in peers])
 
     def split(src, tmp, dst, n):
-        ts(T[tmp][:, 0:n], T[src][:], 31, None, A.bitwise_and, None, [full(src)], [(tmp, 0, n)])
-        ts(T[tmp][:, n:2 * n], T[src][:], 5, None, A.logical_shift_right, None, [full(src)], [(tmp, n, 2 * n)])
-        copy("v", T[dst][:], T[tmp][:], [full(tmp)], [full(dst)])
+        ts(T[tmp][:], T[src][:], 31, None, A.bitwise_and, None, [full(src)], [full(tmp)])
+        ts(T[dst][:, n:2 * n], T[src][:], 1 / 32, LIFT - 0.5 + 1 / 64, A.mult, A.add, [full(src)], [(dst, n, 2 * n)])
+        copy("v", T[dst][:, 0:n], T[tmp][:], [full(tmp)], [(dst, 0, n)])
 
     step("rdig", "rw")
     split("RI", "RJ", "RD", 256)
     for a in range(4):
         bk, c0 = "DA%d" % (a // 2), 256 * (a % 2)
-        for j in range(2):
-            mm(T[bk][:, c0:c0 + 256], T.ZA[:, a, 1 - j:129 - j], T.RD[:, 256 * j:256 * j + 256], j == 0, j == 1, [full("ZA"), full("RD")], [(bk, c0, c0 + 256)])
+        for j in (1, 0):
+            mm(T[bk][:, c0:c0 + 256], T.ZA[:, a, 1 - j:129 - j], T.RD[:, 256 * j:256 * j + 256], j == 1, j == 0, [full("ZA"), ("RD", 256 * j, 256 * j + 256)], [(bk, c0, c0 + 256)])
     step("rws")
-    copy("s", T.RW[:, 0:512], T.DA0[:], [full("DA0")], [("RW", 0, 512)])
+    affine("s", T.RW[:, 0:512], T.DA0[:], 1 / LOW, 0.0, [full("DA0")], [("RW", 0, 512)])
     step("rwv")
-    copy(WHO["rwv"], T.RW[:, 512:V], T.DA1[:], [full("DA1")], [("RW", 512, V)])
+    affine(WHO["rwv"], T.RW[:, 512:V], T.DA1[:], 1 / LOW, 0.0, [full("DA1")], [("RW", 512, V)])
     step("cd")
     for k in range(3):
         affine(WHO["cd"], T.CD[:, k, :], T.ID[:], T.CK[:, k + 1:k + 2], 0.0, [full("ID"), full("CK")], [("CD", 128 * k, 128 * k + 128)])
@@ -418,42 +441,41 @@ def rank_program(g, core, T, topo):
         for j in range(2):
             mm(T.LN[:, z::4], T.LV[:, z, 1 - j:129 - j], T.EVD[:, 128 * j:128 * j + 128], j == 0, j == 1, [("LV", 144 * z, 144 * z + 144), full("EVD")], [full("LN")])
     step("vw")
-    act(T.VW[:], T.LN[:], [full("LN")], [full("VW")], scale=-1.0)
-    place_next(0, "pn0")
-    place_mm(0)
+    affine(WHO["vw"], T.VW[:], T.LN[:], 1 / LOW, 0.0, [full("LN")], [full("VW")])
+    place_mm(0, "DA0")
     mem_u(0)
-    step("obinit")
-    affine(WHO["obinit"], T.OB[:, 0:V], T.TB0[:, own:own + V], -1.0, 15.0, [("TB0", own, own + V)], [("OB", 0, V)])
 
     for b in range(NB):
         last = b == NB - 1
         tb, mt, mv, of = "TB%d" % b, "MT%d" % (b % 2), "MV%d" % (b % 2), "OF%d" % b
         step(None, None, b + 1)
 
-        def slots(c):
-            step("s%d" % c)
-            s = 512 * c
-            memory("vs"[c // 2], b, T[mt][:, s:s + 512], T[tb][:].indirect(T[of][:, 32 * c:32 * c + 32]), [full(tb), (of, 32 * c, 32 * c + 32)], [(mt, s, s + 512)])
+        def slots(c0, c1):
+            step("s%d" % c0)
+            memory("vs"[c0 // 2], b, T[mt][:, 512 * c0:512 * c1], T[tb][:].indirect(T[of][:, 32 * c0:32 * c1]), [full(tb), (of, 32 * c0, 32 * c1)], [(mt, 512 * c0, 512 * c1)])
 
-        def scan(c):
-            step("m%d" % c)
-            s = (512 * c, 512 * c + 512)
+        def largest(c0, c1):
+            step("m%d" % c0)
+            s = (512 * c0, 512 * c1)
             x = T[mt][:, s[0]:s[1]]
-            op("v", lambda e: e.tensor_tensor_scan(T.MX[:, s[0]:s[1]], T.RS[:], x, 0.0, A.min, A.max), [full("RS"), (mt,) + s], [("MX",) + s])
+            op("v", lambda e: e.tensor_tensor_scan(T.MX[:, s[0]:s[1]], T.RS[:, 0:s[1] - s[0]], x, 0.0, A.min, A.max), [("RS", 0, s[1] - s[0]), (mt,) + s], [("MX",) + s])
 
         def clip(h):
             step("clip%d" % h, "ws%d" % h)
             s, o, w = (1024 * h, 1024 * h + 1024), V + E * b + 256 * h, "W%d" % h
+            if h and SUB[b]:
+                tt(T.OB[:, o:o + 256], T[w][:, 0:256], T.MX[:, s[0] + 3:s[1]:4], A.subtract, [("MX",) + s, (w, 0, 256)], [("OB", o, o + 256)])
+                return
             mm(T[w][:, 0:256], T.NI[:], T.MX[:, s[0] + 3:s[1]:4], False, True, [full("NI"), ("MX",) + s], [(w, 0, 256)])
-            act(T.OB[:, o:o + 256], T[w][:, 0:256], [(w, 0, 256)], [("OB", o, o + 256)], F.Relu, bias=(30.0, 15.0)[h], scale=-1.0)
+            affine("s", T.OB[:, o:o + 256], T[w][:, 0:256], 1.0, (-15.0, 0.0)[h], [(w, 0, 256)], [("OB", o, o + 256)])
 
         def where(h, j):
             return (("DA%d" % h, 0), ("DA%d" % h, 256), ("CX%d" % h, 256))[j]
 
         def diff(h):
-            step(None, "d%d" % h)
             s = (1024 * h, 1024 * h + 1024)
             for j in (2, 0, 1):
+                step(None, "de"[j < 2] + "%d" % h)
                 bk, d = where(h, j)
                 for w, k in (("ID", j + 1), ("NI", 0)):
                     mm(T[bk][:, d:d + 256], T[w][:], T[mt][:, s[0] + k:s[1]:4], w == "ID", w == "NI", [full(w), (mt,) + s], [(bk, d, d + 256)])
@@ -474,63 +496,75 @@ def rank_program(g, core, T, topo):
         def renew(h):
             step(None, "of%d" % h)
             w, c0, s, o = ("LN", "LX")[h], 128 * b + 64 * h, 256 * h, V + E * b + 256 * h
-            mm(T[w][:, 256:512], T.ZR[:, 0:128], T.RS[:, 0:256], True, False, [full("ZR"), full("RS")], [(w, 256, 512)])
+            mm(T[w][:, 256:512], T.LC[:], T.M1[:], True, False, [full("LC"), full("M1")], [(w, 256, 512)])
             for a in range(4):
-                mm(T[w][:, 256 + a:512:4], T.SV[:, a, :], T.VW[:, c0:c0 + 64], False, False, [full("SV"), full("VW")], [(w, 256, 512)])
+                mm(T[w][:, 256 + a:512:4], T.SV[:, a, :], T.VW[:, c0:c0 + 64], False, False, [("SV", 128 * a, 128 * a + 128), full("VW")], [(w, 256, 512)])
             step("rn%d" % h, "ct%d" % h)
             mm(T[w][:, 256:512], T.LC[:], T.SG[:, s:s + 256], False, True, [full("LC"), ("SG", s, s + 256)], [(w, 256, 512)])
             tt(T.RW[:, o:o + 256], T[w][:, 256:512], T.GR[:, s:s + 256], A.min, [(w, 256, 512), ("GR", s, s + 256)], [("RW", o, o + 256)])
 
         mem_v(b)
-        for c in range(4):
-            slots(c)
-            scan(c)
-        place_out(b, 0)
-        if 0 < b < NB - 1:
-            place_mm(1)
-            place_out(b, 1)
+        for c0, c1 in ((0, 2), (2, 3), (3, 4)):
+            slots(c0, c1)
+        for c0, c1 in ((0, 2), (2, 3), (3, 4)) if b else ((0, 1), (1, 2), (2, 3), (3, 4)):
+            largest(c0, c1)
+        place_out(b, 0, "DA0")
+        if not last:
+            place_next(b)
+        if b == 0:
+            place_mm(1, "LX")
+            place_out(b, 1, "LX")
         for h in range(2):
-            diff(h)
             clip(h)
+            diff(h)
         n, lw = V + E * (b + 1), "LW%d" % b
         if not last:
-            step("blk")
             nx = "TB%d" % (b + 1)
-            for q, c0, c1 in PIECES:
-                copy(q, T[nx][:, own + c0:own + c1], T.OB[:, 0:n].indirect(T[lw][:, c0 // 16:c1 // 16]), [("OB", 0, n), (lw, 0, 64)], [(nx, own + c0, own + c1)])
+            for i, (q, c0, c1) in enumerate(PIECES):
+                step("blk%d" % i)
+                act(T[nx][:, own + c0:own + c1], T.OB[:, 0:n].indirect(T[lw][:, c0 // 16:c1 // 16]), [("OB", 0, n), (lw, 0, 64)], [(nx, own + c0, own + c1)],
+                    F.Relu, bias=15.0, scale=-1.0)
+            step("send")
             for c0, c1 in SENDS:
                 send(b, c0, c1, (c0, c1) == SENDS[-1])
         for h in range(2):
             lowest(h)
             renew(h)
-        if b == 0:
-            place_mm(1)
-            place_out(b, 1)
+        if b and not last:
+            place_mm(1, "DA1")
+            place_out(b, 1, "DA1")
         if not last:
             mem_u(b + 1)
             place_scatter(b + 1, 0)
             place_scatter(b + 1, 1)
             for h in range(2):
                 ring_list(b + 1, h)
-            if b + 2 < NB:
-                place_next(b + 1)
-            place_mm(0)
+            place_mm(0, "DA0")
 
-    rd = [("RW", 0, n), (lw, 0, 64)]
-    step("yg", "yr")
-    act(T.YG[:, 0:512], T.RW[:, 0:n].indirect(T[lw][:, 0:32]), rd, [("YG", 0, 512)], F.Relu)
-    ts(T.YG[:, 512:V], T.RW[:, 0:n].indirect(T[lw][:, 32:64]), 0.0, None, A.max, None, rd, [("YG", 512, V)])
     for a in range(4):
-        mm(T.DA0[:, 0:256], T.Y1[:, 3 - a:131 - a], T.YG[:, 256 * a:256 * a + 256], a == 0, a == 3, [full("Y1"), ("YG", 256 * a, 256 * a + 256)], [("DA0", 0, 256)])
+        step("yg%d" % a)
+        out, src, rd, wr = T.YG[:, 256 * a:256 * a + 256], T.RW[:, 0:n].indirect(T[lw][:, 16 * a:16 * a + 16]), [("RW", 0, n), (lw, 0, 64)], [("YG", 256 * a, 256 * a + 256)]
+        if WHO["yg%d" % a] == "s":
+            act(out, src, rd, wr, F.Relu)
+        else:
+            ts(out, src, 0.0, None, A.max, None, rd, wr)
     step("yr")
-    copy("v", T.YR[:], T.DA0[:, 0:256], [("DA0", 0, 256)], [full("YR")])
-    for h in range(2):
-        step("blk%d" % h)
-        c0 = 512 * h
-        act(T.YB[:, c0:c0 + 512], T.OB[:, 0:n].indirect(T[lw][:, 32 * h:32 * h + 32]), [("OB", 0, n), (lw, 0, 64)], [("YB", c0, c0 + 512)], F.Relu, bias=15.0, scale=-1.0)
-    outs = {"yr": (T.yr[:], T.YR[:], full("YR")), "ym0": (T.ym[:, 0:512], T.YB[:, 0:512], ("YB", 0, 512)), "ym1": (T.ym[:, 512:V], T.YB[:, 512:V], ("YB", 512, V))}
-    for name in ("ym0", "yr", "ym1"):
-        dmas([("y",) + outs[name][0:2]], [outs[name][2]], [])
+    for i, a in enumerate(YORDER):
+        mm(T.DA0[:, 0:256], T.Y1[:, 3 - a:131 - a], T.YG[:, 256 * a:256 * a + 256], i == 0, i == 3, [full("Y1"), ("YG", 256 * a, 256 * a + 256)], [("DA0", 0, 256)])
+    affine(WHO["yr"], T.YR[:], T.DA0[:, 0:256], 1.0, -32.0 * LIFT, [("DA0", 0, 256)], [full("YR")])
+    outs = {"yr": (T.yr[:], T.YR[:], full("YR"))}
+    for i, (q, c0, c1) in enumerate(YPIECES):
+        step("blk%d" % i)
+        out, src, rd, wr = T.YB[:, c0:c1], T.OB[:, 0:n].indirect(T[lw][:, c0 // 16:c1 // 16]), [("OB", 0, n), (lw, 0, 64)], [("YB", c0, c1)]
+        if q == "s":
+            act(out, src, rd, wr, F.Relu)
+            step("top%d" % i)
+            ts(out, out, 15.0, None, A.min, None, wr, wr)
+        else:
+            ts(out, src, 0.0, 15.0, A.max, A.min, rd, wr)
+        outs["ym%d" % i] = (T.ym[:, c0:c1], out, wr[0])
+    for q, name in OUTS:
+        dmas([(q,) + outs[name][0:2]], [outs[name][2]], [])
     for j in plan():
         emit(prog[j])
     for s in total:

@@ -3,32 +3,110 @@ from concourse.mybir import AluOpType as A, ActivationFunctionType as F
 
 NB, V, E, R = 4, 1024, 512, 4
 BF, F32, I32, U16 = "bfloat16", "float32", "int32", "uint16"
-LOW, HIGH, LIFT = 256.0, 8192.0, 129
-PIECES = (("s", 0, 256), ("s", 256, 640), ("s", 640, 1024))
-SENDS = ((0, 256), (256, 640), (640, 1024))
-NEXT = (("s", 0, 256), ("v", 256, 512))
+LOW, HIGH, LIFT = 512.0, 16384.0, 129
+PIECES = [(("s", 0, 128), ("s", 128, 768), ("s", 768, 1024))] + [(("s", 0, 320), ("s", 320, 768), ("s", 768, 1024))] * (NB - 2)
+SENDS = [tuple(x[1:] for x in p) for p in PIECES]
+NEXT = [((0, 256), (256, 512))] * NB
+JOIN = (0, 0, 0, 0)
 YPIECES = (("s", 0, 640), ("s", 640, 1024))
+YRINGS = (("s", 0, 256), ("s", 256, 512), ("v", 512, 768), ("v", 768, 1024))
 YORDER = (0, 2, 1, 3)
 OUTS = (("y", "ym0"), ("y", "ym1"), ("s", "yr"))
 SUB = (1, 1, 1, 0)
-START = {"v": "fill cols cols2 lldig eu16 rdig scat0 scat1 ev16 vdig ro0 ro1",
-         "s": "cols pz0 cols2 cd ni ld rws rwv rg0 rg1 u",
-         "p": "ld rw rs0 rs1 pm0 wu0 wu1",
-         "g": "rows id bo za y2 rs zb lv lc sv"}
-FIRST = {"v": "s0 m0 m1 po m2 m3 clip1 p0 p1 pn1 hb pnout scat0 rn0 rn1 scat1 ro0 ro1",
-         "s": "v s2 s3 pn0 clip0 blk0 blk1 blk2 vw sg0 sg1 u rg0 rg1",
-         "p": "wv vw d0 ws0 e0 ws1 d1 e1 cd0 cd1 pm1 pm1b of0 of1 ct0 ct1 wu0 wu1 rs0 rs1 pm0",
-         "g": "send sv3 y1"}
-TURN = {"v": "s0 po m0 m2 m3 clip1 p0 p1 pn1 scat0 pnout rn0 rn1 scat1 ro0 ro1",
-        "s": "v s2 s3 pn0 clip0 blk0 blk1 blk2 sg0 sg1 u rg0 rg1",
-        "p": "of0 wv d0 of1 ws0 e0 d1 e1 cd0 cd1 pm1 pm1b ct0 ct1 wu0 wu1 rs0 rs1 pm0",
-        "g": "send"}
-LAST = {"v": "s0 po m0 m2 m3 p0 p1 top0 rn0 rn1 yg2 yg3 top1",
-        "s": "v s2 s3 clip0 clip1 blk0 sg0 sg1 blk1 yg0 yg1 yr",
-        "p": "of0 wv d0 of1 ws0 e0 ws1 d1 e1 cd0 cd1 ct0 ct1 yr",
+FIRST = {"v": "one cols cj qh ck tie cwy bo y2 ceven pz0 ll1 rhi rand rlo ev16 vand eu16 rw1 zb iscat0 v iro1 iro0 iscat1 s0 m1 m0 m2 po clip1 vlo vhi ipn0 p0 p1 p2 scat0 pnout rn0 rn1 scat1 ro0 ro1",
+         "s": "cpy clift ll3 pz1 i15 ni ll2 cwz ll0 cd rw0 rw2 rw3 irg1 irg0 iu s1 s2 ld clip0 ipn1 blk0 blk1 blk2 vw sg0 sg1 u rg0 rg1",
+         "p": "rw irs1 irs0 iwu1 iwu0 ld wv ipm0 ws0 d00 d10 d11 d20 d01 d21 vw cd01 pm1 pm1b cd00 cd11 cd10 cd20 cd21 of0 ct0 of1 ct1 wu0 rs0 rs1 pm0 wu1",
+         "g": "rows bo id za rs lc lv sv0 sv1 sv2 sv3 hb1 send0 send1 send2 hb2 hb3 zr y1"}
+TURN = {"v": "v s0 po m0 m1 m2 clip1 p0 p1 p2 scat0 pnout rn0 rn1 scat1 ro0 ro1",
+        "s": "pn1 s1 s2 pn0 clip0 blk0 blk1 blk2 sg0 sg1 u rg0 rg1",
+        "p": "of1 of0 wv d20 d00 d10 ws0 d01 d11 pm1 d21 pm1b cd00 cd10 cd01 cd11 cd20 cd21 ct0 ct1 wu0 wu1 rs0 rs1 pm0",
+        "g": "send0 send1 send2"}
+LAST = {"v": "v s0 po m1 m0 m2 p0 p1 p2 p3 top0 rn0 rn1 yg2 yg3 top1",
+        "s": "s1 s2 clip0 clip1 blk0 sg0 sg1 blk1 yg0 yg1 yr",
+        "p": "of0 wv of1 d00 d10 d20 ws0 d01 ws1 d11 d21 cd00 cd01 cd10 cd11 cd20 cd21 ct0 ct1 yr",
         "g": ""}
-WHO = {"pz0": "s", "hb": "v", "ni": "s", "cd": "s", "lldig": "v", "rwv": "s", "ld": "s", "vw": "s",
-       "yg0": "s", "yg1": "s", "yg2": "v", "yg3": "v", "yr": "s"}
+WHO = {"pz0": "v", "pz1": "s", "ni": "s", "cd": "s", "ll0": "s", "ll1": "v", "ll2": "s", "ll3": "s", "ld": "s", "vw": "s",
+       "rw0": "s", "rw1": "v", "rw2": "s", "rw3": "s", "id": "g", "za": "g", "lv": "g", "y2": "v", "hb1": "g", "hb2": "g", "hb3": "g", "i15": "s", "ipn0": "v", "ipn1": "s", "pn0": "s", "pn1": "s"}
+PARTS = [((0, 256), (256, 512))] * NB
+SLOTS = [(("v", 256, 416), ("s", 0, 256), ("s", 416, 512))] + [(("v", 256, 384), ("s", 0, 256), ("s", 384, 512))] * (NB - 1)
+SIGN = ("ss", "ss", "ss", "ss")
+LATE = 0
+SCAT, HW = (256, 256, 256, 256), 320
+UV = (0, 0, 0, 0)
+DIAG = 0
+WIDE = (1, 1, 1, 2)
+ONEPM = (0, 0, 0, 0)
+RINGS = ((0, 256), (256, 512))
+
+PIECES = [(("s", 0, 64), ("s", 64, 1024))] + [(("s", 0, 256), ("s", 256, 640), ("s", 640, 1024))] * (NB - 2)
+SENDS = [tuple(x[1:] for x in p) for p in PIECES]
+NEXT = [((0, 256), (256, 512))] + [((0, 512),)] * (NB - 1)
+WIDE, DIAG = (0, 0, 0, 0), 1
+SLOTS = [(("v", 0, 256), ("s", 256, 384), ("s", 384, 512))] * NB
+FIRST = {"v": "one cols cj qh ck cwy ni ceven tie pz0 bo cd rhi rand rlo ev16 eu16 vand rw1 rw3 iscat0 y2 zb iscat1 iro0 iro1 s0 po m0 m2 m1 vhi clip1 vlo p0 p1 vw scat0 pnout rn0 rn1 scat1 ro0 ro1",
+         "s": "ll0 pz1 ll2 cwz ll1 ll3 clift cpy rw0 rw2 irg0 irg1 iu v s2 s1 ld clip0 ipn0 blk0 blk1 ipn1 sg1 sg0 u rg0 rg1",
+         "p": "rw irs0 irs1 ld iwu1 iwu0 ipm0 wv e0 ws0 d0 e1 d1 vw cd0 cd1 pm1 pm1b of0 ct0 of1 ct1 wu1 wu0 rs0 rs1 pm0",
+         "g": "rows bo id za rs lc lv sv0 sv1 sv2 sv3 hb1 send0 send1 hb2 hb3 zr y1"}
+TURN = {"v": "s0 m0 m2 m1 po clip1 p0 p1 scat0 pnout rn0 rn1 scat1 ro0 ro1",
+        "s": "v s2 s1 pn0 clip0 blk0 blk1 blk2 sg0 sg1 u rg0 rg1",
+        "p": "of0 wv of1 e0 ws0 d0 d1 e1 cd0 pm1 cd1 pm1b ct0 ct1 wu1 wu0 rs0 rs1 pm0",
+        "g": "send0 send1 send2"}
+LAST = {"v": "s0 po m0 m1 m2 p0 p1 rn0 rn1 yg2 yg3 top0 top1",
+        "s": "v s1 s2 clip0 clip1 blk0 sg0 sg1 blk1 yg0 yg1 yr",
+        "p": "of0 wv of1 e0 ws0 d0 ws1 d1 e1 cd0 cd1 ct0 ct1 yr",
+        "g": ""}
+WHO.update({"pz0": "v", "pz1": "s", "ni": "v", "cd": "v", "ll0": "s", "ll1": "s", "ll2": "s", "ll3": "s", "ld": "s", "vw": "v",
+            "rw0": "s", "rw1": "v", "rw2": "s", "rw3": "v", "ipn0": "s", "ipn1": "s", "pn0": "s"})
+
+SIGN = ("vs", "vs", "vs", "vs")
+SLOTS[1] = SLOTS[2] = (("v", 0, 256), ("s", 256, 512))
+FIRST = {"v": "one cols qh cj tie ck ll0 cwy cd bo pz1 ceven rhi rand eu16 rlo vand zb ev16 rw1 rw3 iscat0 y2 iscat1 vlo iro0 iro1 s0 vhi m0 m2 m1 po clip1 p0 p1 vw ipn0 sg0 scat0 pnout rn1 rn0 scat1 ro0 ro1",
+         "s": "clift ll1 ni pz0 ll2 cwz cpy ll3 rw0 rw2 irg1 irg0 iu v s2 s1 ld clip0 blk0 blk1 ipn1 sg1 u rg0 rg1",
+         "p": "rw ld irs0 irs1 iwu0 iwu1 ipm0 wv e0 ws0 d0 d1 e1 vw cd0 cd1 of0 of1 pm1 pm1b ct1 ct0 wu1 wu0 rs0 rs1 pm0",
+         "g": "rows bo id za rs lc lv sv0 sv1 sv2 sv3 hb1 send0 send1 hb2 hb3 zr y1"}
+TURN = {"v": "s0 po m0 m1 clip1 p0 p1 sg0 scat0 rn0 rn1 pnout scat1 ro0 ro1",
+        "s": "v s1 pn0 clip0 blk0 blk1 blk2 sg1 u rg0 rg1",
+        "p": "of0 wv e0 ws0 d0 d1 e1 cd0 of1 cd1 pm1 ct0 ct1 pm1b wu1 wu0 rs0 rs1 pm0",
+        "g": "send0 send1 send2"}
+LAST = {"v": "s0 po m0 m1 m2 p0 p1 sg0 rn0 rn1 yg2 yg3 top0 top1",
+        "s": "v s1 s2 clip0 clip1 blk0 sg1 blk1 yg0 yg1 yr",
+        "p": "of0 of1 wv e0 d0 ws0 d1 ws1 e1 cd0 cd1 ct0 ct1 yr",
+        "g": ""}
+WHO.update({"pz0": "s", "pz1": "v", "ni": "s", "cd": "v", "ll0": "v", "ll1": "s", "ll2": "s", "ll3": "s", "ld": "s", "vw": "v",
+            "rw0": "s", "rw1": "v", "rw2": "s", "rw3": "v", "ipn0": "v", "ipn1": "s", "pn0": "s"})
+
+SIGN = ("ss", "vs", "vs", "vs")
+SLOTS[0] = SLOTS[1]
+SCAT = (192, 192, 192, 192)
+FIRST = {"v": "one cols qh cj bo cwy ll2 ld3 ceven ld1 y2 le1 ld2 rhi rand eu16 rlo iscat0 vand vhi rw1 zb rw3 ev16 iscat1 iro0 iro1 s0 po m0 m1 vlo clip1 le2 ipn0 tie p0 le3 p1 scat0 pnout rn0 rn1 scat1 ro0 ro1",
+         "s": "cpy clift ll3 ll1 ll0 pz0 pz1 ni cwz rw0 rw2 iu irg0 irg1 v s1 ipn1 clip0 blk0 blk1 vw sg0 sg1 u rg0 rg1",
+         "p": "rw iwu0 irs0 irs1 ipm0 iwu1 wv e0 ws0 d0 d1 e1 vw pm1 pm1b cd0 cd1 of0 ct0 of1 ct1 rs0 rs1 wu0 pm0 wu1",
+         "g": "rows bo ld id za rs lc lv sv0 sv1 sv2 sv3 hb1 send0 send1 hb2 hb3 zr y1"}
+TURN = {"v": "s0 po m0 m1 clip1 p0 p1 sg0 scat0 rn0 pnout rn1 scat1 ro0 ro1",
+        "s": "v s1 pn0 clip0 blk0 blk1 blk2 sg1 u rg0 rg1",
+        "p": "wv of1 of0 e0 ws0 d0 e1 d1 cd0 pm1 cd1 ct0 pm1b ct1 rs0 wu1 rs1 pm0 wu0",
+        "g": "send0 send1 send2"}
+WHO.update({"pz0": "s", "pz1": "s", "ni": "s", "ll0": "s", "ll1": "s", "ll2": "v", "ll3": "s", "vw": "s",
+            "rw0": "s", "rw1": "v", "rw2": "s", "rw3": "v", "ipn0": "v", "ipn1": "s"})
+
+UV = (1, 0, 0, 0)
+FIRST = {"v": "one cols cj qh ceven ll0 cwy ld1 ld3 ld2 zb bo eu16 rhi rand le1 rlo y2 ev16 vhi iscat0 rw3 vand iscat1 iro0 iro1 iu s0 tie m0 m1 po clip1 ipn0 le3 vlo le2 p0 p1 scat0 pnout rn0 rn1 scat1 ro0 ro1",
+         "s": "cpy clift pz0 cwz ll3 ni ll2 ll1 pz1 rw0 rw1 rw2 irg0 irg1 iu v s1 ipn1 clip0 blk0 blk1 vw sg0 sg1 u rg0 rg1",
+         "p": "rw irs0 irs1 iwu0 ipm0 iwu1 wv e0 ws0 d0 d1 e1 pm1 vw cd0 pm1b cd1 of0 ct0 of1 ct1 wu1 wu0 rs0 rs1 pm0",
+         "g": "rows bo ld id za rs lc lv sv0 sv1 sv2 sv3 hb1 send0 send1 hb2 hb3 zr y1"}
+WHO.update({"pz0": "s", "pz1": "s", "ni": "s", "ll0": "v", "ll1": "s", "ll2": "s", "ll3": "s", "vw": "s",
+            "rw0": "s", "rw1": "s", "rw2": "s", "rw3": "v", "ipn0": "v", "ipn1": "s"})
+
+FIRST = {"v": "one cols cj qh hb1 ceven id cwy ld3 ld1 ld2 zb y2 bo rhi rand le1 rlo eu16 vand iscat0 rw3 vhi ev16 iscat1 iro0 iro1 iu s0 tie m0 m1 po clip1 ipn0 vlo le3 p0 le2 p1 scat0 rn0 pnout rn1 scat1 ro0 ro1",
+         "s": "cpy ll1 cwz pz0 pz1 ll3 ll0 clift ll2 ni rw0 rw1 rw2 irg0 irg1 v iu s1 ipn1 clip0 blk0 blk1 vw sg0 sg1 u rg0 rg1",
+         "p": "rw irs0 irs1 ipm0 iwu1 iwu0 wv e0 ws0 d0 d1 e1 pm1 vw pm1b cd0 cd1 of0 ct0 of1 ct1 rs0 wu1 rs1 wu0 pm0",
+         "g": "rows ld bo za rs lc lv sv0 sv1 sv2 sv3 send0 send1 hb2 hb3 zr y1"}
+WHO.update({"hb1": "v", "id": "v", "ll0": "s"})
+
+FIRST = {"v": "one cols cj qh cwy ceven y2 hb1 id ld3 ld2 ld1 bo zb rhi rand vand rlo eu16 vhi iscat0 rw3 iscat1 ev16 tie le1 iro0 iu iro1 s0 po m0 m1 clip1 ipn0 le3 vlo le2 p0 p1 pnout scat0 rn0 rn1 scat1 ro0 ro1",
+         "s": "cpy clift ll2 cwz ll3 ll1 pz0 ll0 pz1 ni rw0 rw1 rw2 irg0 irg1 iu v s1 ipn1 clip0 blk0 blk1 vw sg0 sg1 u rg0 rg1",
+         "p": "rw irs0 irs1 ipm0 iwu1 iwu0 wv e0 ws0 d1 d0 e1 pm1 vw pm1b cd0 cd1 of0 ct0 of1 ct1 wu0 rs0 rs1 pm0 wu1",
+         "g": "rows ld bo za lc rs lc1 lv lc2 sv0 sv1 sv2 sv3 send0 send1 hb2 hb3 zr y1"}
 
 SCRATCH = {
     "OB": ("sbuf", [128, V + NB * E], BF),
@@ -40,17 +118,17 @@ SCRATCH = {
     "SG": ("sbuf", [128, 512], BF), "GR": ("sbuf", [128, 512], BF),
     "VW": ("sbuf", [128, 512], BF),
     "YB": ("sbuf", [128, V], BF), "YG": ("sbuf", [128, V], BF), "YR": ("sbuf", [128, 256], F32),
-    "ONE": ("sbuf", [128, 528], BF), "NM": ("sbuf", [128, 128], BF), "M1": ("sbuf", [128, 256], BF), "ZR": ("sbuf", [128, 144], BF),
+    "ONE": ("sbuf", [128, 528], BF), "NM": ("sbuf", [128, 128], BF), "ZR": ("sbuf", [128, 144], BF),
     "ID": ("sbuf", [128, 128], BF), "NI": ("sbuf", [128, 128], BF),
     "ZB": ("sbuf", [128, 144], BF), "RQ": ("sbuf", [128, 16], F32), "QH": ("sbuf", [128, 16], F32),
-    "XL": ("sbuf", [128, 256], BF), "PZ": ("sbuf", [128, E], BF), "HB": ("sbuf", [128, NB - 1, 256], BF),
+    "XL": ("sbuf", [128, 272], BF), "PZ": ("sbuf", [128, E], BF), "HB": ("sbuf", [128, NB - 1, HW], BF),
     "ZA": ("sbuf", [128, 4, 132], BF), "LV": ("sbuf", [128, 4, 144], BF), "Y2": ("sbuf", [128, 144], BF),
     "Y1": ("sbuf", [128, 144], BF), "LC": ("sbuf", [128, 128], BF), "SV": ("sbuf", [128, 4, 128], BF),
-    "BO": ("sbuf", [128, 128], BF), "B1": ("sbuf", [128, 128], BF), "B2": ("sbuf", [128, 128], BF),
-    "LD": ("sbuf", [128, 3, 128], BF), "CD": ("sbuf", [128, 3, 128], BF),
-    "CA": ("sbuf", [128, 4], F32), "CJ": ("sbuf", [128, 4], F32), "CK": ("sbuf", [128, 4], F32),
+    "BO": ("sbuf", [128, 32], BF), "B1": ("sbuf", [128, 32], BF), "B2": ("sbuf", [128, 128], BF), "B3": ("sbuf", [128, 144], BF),
+    "LD": ("sbuf", [128, 3, 128], BF), "CJ": ("sbuf", [128, 4], F32), "CA": ("sbuf", [128, 4], F32),
     "RS": ("sbuf", [128, 1024], BF), "LL": ("sbuf", [128, V + E], BF),
-    "PC": ("sbuf", [128, 8], I32), "CF": ("sbuf", [128, 8], F32),
+    "PC": ("sbuf", [128, 8], I32), "CF": ("sbuf", [128, 24], F32),
+    "MU": ("sbuf", [128, E], BF),
     "W0": ("psum", [128, 512], F32), "W1": ("psum", [128, 512], F32), "LX": ("psum", [128, 512], F32), "LN": ("psum", [128, 512], F32),
     "DA0": ("psum", [128, 512], F32), "DA1": ("psum", [128, 512], F32), "CX0": ("psum", [128, 512], F32), "CX1": ("psum", [128, 512], F32),
 }
@@ -59,7 +137,6 @@ for _c in range(4):
     SCRATCH["OF%d" % _c] = ("sbuf", [128, 128], U16)
     SCRATCH["LW%d" % _c] = ("sbuf", [128, 96], U16)
 for _c in range(2):
-    SCRATCH["MU%d" % _c] = ("sbuf", [128, 512], BF)
     SCRATCH["MV%d" % _c] = ("sbuf", [128, 512], BF)
     SCRATCH["MT%d" % _c] = ("sbuf", [128, 2048], BF)
 NDMA = 12
@@ -77,7 +154,8 @@ def rank_program(g, core, T, topo):
     stage, prog = [0, None, None], []
     total, waited, acc, ndma, clks = {}, {}, {}, [0], {}
     psum = {n for n in SCRATCH if SCRATCH[n][0] == "psum"}
-    turns = [START, FIRST] + [TURN] * (NB - 2) + [LAST]
+    turns = [FIRST] + [TURN] * (NB - 2) + [LAST]
+    pre = ["i"]
 
     def wait(q, rec):
         sem, val, clk = rec
@@ -144,10 +222,10 @@ def rank_program(g, core, T, topo):
 
     def item(**k):
         turn, name = stage[0], stage[2 if k["q"] == "p" else 1]
-        k["at"] = (turn and len(turns), 0)
+        k["at"], k["where"] = (turn and len(turns), 0), (turn, name)
         if k["q"] in "vspg" and k["kind"] != "dma":
-            while name not in turns[turn][k["q"]].split():
-                turn += 1
+            if name not in turns[turn][k["q"]].split():
+                turn, name = turn + 1, "+" + name
             k["at"] = (turn, 1 + turns[turn][k["q"]].split().index(name))
         prog.append(k)
 
@@ -240,24 +318,88 @@ def rank_program(g, core, T, topo):
     dmas([("s", T.EUI[:], T.eu[:])], [], [full("EUI")])
     dmas([("s", T.EVI[:], T.ev[:])], [], [full("EVI")])
     dmas([("y", T.TB0[:, own:own + V], T.m0[:, own:own + V])], [], [("TB0", own, own + V)])
-    rest = [(a, b) for a, b in ((0, own), (own + V, 4 * V)) if a < b]
-    dmas([("y", T.TB0[:, a:b], T.m0[:, a:b]) for a, b in rest], [], [("TB0", a, b) for a, b in rest])
 
-    step("fill")
     one = T.ONE[:, 0:128]
-    for name, x in (("ONE", 1.0), ("ZR", 0.0), ("M1", -1.0)):
-        op("v", lambda e, name=name, x=x: e.memset(T[name][:], x), [], [full(name)])
+    wide = 528 if WHO["za"] == "g" else 256
+    step("one")
+    op("v", lambda e: e.memset(T.ONE[:, 0:wide], 1.0), [], [full("ONE")])
     step("rows")
     op("g", lambda e: e.iota(T.PC[:, 0:1], [[0, 1]], 0, 1), [], [("PC", 0, 1)])
     iota("RQ", [[1, 16]])
-    iota("XL", [[1, 256]])
+    iota("XL", [[1, 272]], -16)
+
+    names = ["p", "odd", "lo", "hi", "g16", "p4", "even", "tie", "wy", "wz", "py", "pv", "lift"]
+    col = {n: T.CF[:, i:i + 1] for i, n in enumerate(names)}
+    reg = {n: ("CF", i, i + 1) for i, n in enumerate(names)}
+
+    def column(name, src, scale, bias, rd=None):
+        step("c" + name)
+        x, rd = (col[src], reg[src]) if rd is None else (src, rd)
+        named = isinstance(bias, str)
+        affine(WHO.get("c" + name, "s"), col[name], x, scale, col[bias] if named else bias, [rd] + [reg[bias]] * named if named else [rd], [reg[name]])
+
+    step("cols")
+    bits = ((0, 1), (0, 3), (2, 3), (0, 112), (0, 124))[:5 if WHO["za"] == "v" else 4]
+    for i, (sh, m) in enumerate(bits):
+        ts(T.PC[:, i + 1:i + 2], T.PC[:, 0:1], sh, m, A.logical_shift_right, A.bitwise_and, [("PC", 0, 1)], [("PC", i + 1, i + 2)])
+    copy("v", T.CF[:, 0:len(bits) + 1], T.PC[:, 0:len(bits) + 1], [("PC", 0, 8)], [("CF", 0, 6)])
+    rest = [(a, b) for a, b in ((0, own), (own + V, 4 * V)) if a < b]
+    dmas([("y", T.TB0[:, a:b], T.m0[:, a:b]) for a, b in rest], [("PC", 4, 5)] * LATE, [("TB0", a, b) for a, b in rest])
+    step("qh")
+    ts(T.QH[:], T.RQ[:], col["odd"], -1.0, A.mult, A.mult, [full("RQ"), reg["odd"]], [full("QH")])
+    step("cj")
+    ts(T.CJ[:], T.RQ[:, 0:4], col["lo"], None, A.is_equal, None, [full("RQ"), reg["lo"]], [full("CJ")])
+    step("tie")
+    ts(col["tie"], col["lo"], col["hi"], -0.5, A.is_lt, A.add, [reg["lo"], reg["hi"]], [reg["tie"]])
+    step("ceven")
+    ts(col["even"], T.CJ[:, 0:1], T.CJ[:, 2:3], 0.25, A.subtract, A.mult, [full("CJ")], [reg["even"]])
+    column("wz", "odd", -32.0, "even")
+    if WHO["y2"] == "v":
+        column("py", "hi", 1.0, "g16")
+        step("cwy")
+        ts(col["wy"], T.CJ[:, 1:2], HIGH / LOW, T.CJ[:, 0:1], A.mult, A.add, [full("CJ")], [reg["wy"]])
+    if WHO["lv"] == "v":
+        column("pv", "lo", 4.0, "g16")
+        step("ca")
+        ts(T.CA[:], T.RQ[:, 0:4], col["hi"], None, A.is_equal, None, [full("RQ"), reg["hi"]], [full("CA")])
+    column("lift", T.CJ[:, 1:2], LIFT / LOW, 0.0, full("CJ"))
+
+    def match(out, wr, shift, n, at, w=None, rw=()):
+        rd = [full("XL"), reg[at]] + list(rw)
+        ts(out, T.XL[:, 16 - shift:16 - shift + n], col[at], w, A.is_equal, None if w is None else A.mult, rd, [wr])
+
     step("za")
-    sel(T.ZA[:], T.ONE[:], [[-1, 4], [-4, 33], [1000, 4]], A.is_equal, -1000, [full("ONE")], [full("ZA")])
+    if WHO["za"] == "g":
+        sel(T.ZA[:], T.ONE[:], [[-1, 4], [-4, 33], [1000, 4]], A.is_equal, -1000, [full("ONE")], [full("ZA")])
+    else:
+        for a in range(4):
+            match(T.ZA[:, a, :], ("ZA", 132 * a, 132 * a + 132), 1, 132, "p4", T.CJ[:, a:a + 1], [full("CJ")])
     step("id")
-    sel(T.ID[:], one, [[-1, 128]], A.is_equal, 0, [full("ONE")], [full("ID")])
+    if WHO["id"] == "g":
+        sel(T.ID[:], one, [[-1, 128]], A.is_equal, 0, [full("ONE")], [full("ID")])
+    else:
+        match(T.ID[:], full("ID"), 0, 128, "p")
+    step("y2")
+    if WHO["y2"] == "v":
+        match(T.Y2[:], full("Y2"), 12, 144, "py", col["wy"], [reg["wy"]])
+    step("zb")
+    match(T.ZB[:], full("ZB"), 15, 144, "g16", col["wz"], [reg["wz"]])
+    step("bo")
+    iota("B1", [[16, 8], [0, 4]])
+    ts(T.BO[:], T.B1[:], col["g16"], None, A.is_equal, None, [full("B1"), reg["g16"]], [full("BO")])
+    step("ld")
+    iota("B3", [[16, 9], [1000, 4], [0, 4]], -3000)
+    for j in range(1, 4):
+        step("ld%d" % j)
+        r = ("LD", 128 * j - 128, 128 * j)
+        ts(T.LD[:, j - 1, :], T.B3[:, 12 - 4 * j:140 - 4 * j], col["g16"], None, A.is_equal, None, [full("B3"), reg["g16"]], [r])
+        step("le%d" % j)
+        tt(T.LD[:, j - 1, j::4], T.LD[:, j - 1, j::4], T.BO[:], A.subtract, [r, full("BO")], [r])
 
     def blocks(out, tmp, src, n):
+        step("lc1")
         sel(T[tmp][:], T[src][:, 0:128], [[-n, 128 // n], [0, n]], A.is_ge, 0, [full(src)], [full(tmp)])
+        step("lc2")
         sel(T[out][:], T[tmp][:], [[n, 128 // n], [0, n]], A.is_ge, n - 1, [full(tmp)], [full(out)], cm=-1)
 
     def marks(name, out, pat, base, values):
@@ -267,94 +409,94 @@ def rank_program(g, core, T, topo):
             sel(T[out][:], T[src][:], pat, A.not_equal, base - j, [full(src)], [full(out)], x)
             src = out
 
-    step("bo")
-    blocks("BO", "B1", "ONE", 16)
-    marks("y2", "Y2", [[-16, 9], [1000, 4], [-4, 4]], -3000, (LOW, HIGH))
-    marks("zb", "ZB", [[-16, 9], [1000, 16]], -15000, (1.0, 256.0))
-    marks("y1", "Y1", [[-4, 36], [1000, 4]], -3000, (LOW, HIGH, LOW, HIGH))
+    step("zr")
+    iota("ZR", [[0, 144]])
+    if WHO["y2"] == "g":
+        marks("y2", "Y2", [[-16, 9], [1000, 4], [-4, 4]], -3000, (1.0, HIGH / LOW))
+    marks("y1", "Y1", [[-4, 36], [1000, 4]], -3000, (LOW, HIGH))
     step("rs")
     op("g", lambda e: e.iota(T.RS[:, 0:256], [[0, 64], [32, 4]], -16, 0, allow_small_or_imprecise_dtypes=True), [], [("RS", 0, 256)])
     dmas([("y", T.RS[:, c:c + 256], T.RS[:, 0:256]) for c in (256, 512, 768)], [("RS", 0, 256)], [("RS", 256, 1024)])
-    dmas([("y", T.OB[:, 0:V], T.TB0[:, own:own + V])], [full("TB0")], [("OB", 0, V)])
     step("lv")
     for z in range(4):
-        sel(T.LV[:, z, :], T.ONE[:, 0:144], [[-16, 9], [-1, 4], [1000, 4]], A.is_equal, -1000 - 4 * z, [full("ONE")], [("LV", 144 * z, 144 * z + 144)])
+        if WHO["lv"] == "g":
+            sel(T.LV[:, z, :], T.ONE[:, 0:144], [[-16, 9], [-1, 4], [1000, 4]], A.is_equal, -1000 - 4 * z, [full("ONE")], [("LV", 144 * z, 144 * z + 144)])
+        else:
+            match(T.LV[:, z, :], ("LV", 144 * z, 144 * z + 144), 1, 144, "pv", T.CA[:, z:z + 1], [full("CA")])
     step("lc")
-    sel(T.NM[:], one, [[0, 32], [1, 2], [0, 2]], A.is_equal, -1, [full("ONE")], [full("NM")], -1.0, 0)
+    iota("NM", [[0, 32], [-1, 2], [0, 2]], 1)
     blocks("LC", "B2", "NM", 4)
-    for a in range(4):
-        step("sv" if a < 3 else "sv3")
-        sel(T.SV[:, a, :], T.NM[:], [[-16, 8], [0, 8], [-1, 2]], A.is_equal, -4 * a, [full("NM")], [("SV", 128 * a, 128 * a + 128)])
 
-    names = ["odd", "lo", "hi", "even", "tie", "keep", "big"]
-    col = {n: T.CF[:, i:i + 1] for i, n in enumerate(names)}
-    reg = {n: ("CF", i, i + 1) for i, n in enumerate(names)}
-    step("cols")
-    for i, (sh, m) in enumerate(((0, 1), (0, 3), (2, 3))):
-        ts(T.PC[:, i + 1:i + 2], T.PC[:, 0:1], sh, m, A.logical_shift_right, A.bitwise_and, [("PC", 0, 1)], [("PC", i + 1, i + 2)])
-    copy("v", T.CF[:, 0:3], T.PC[:, 1:4], [("PC", 1, 4)], [("CF", 0, 3)])
-    ts(T.QH[:], T.RQ[:], col["odd"], None, A.mult, None, [full("RQ"), reg["odd"]], [full("QH")])
-    affine("s", col["even"], col["odd"], -1.0, 1.0, [reg["odd"]], [reg["even"]])
-    step("cols2")
-    ts(T.CJ[:], T.RQ[:, 0:4], col["lo"], None, A.is_equal, None, [full("RQ"), reg["lo"]], [full("CJ")])
-    ts(T.CA[:], T.RQ[:, 0:4], col["hi"], None, A.is_equal, None, [full("RQ"), reg["hi"]], [full("CA")])
-    ts(col["keep"], col["lo"], 2.0, None, A.is_lt, None, [reg["lo"]], [reg["keep"]])
-    tt(T.CK[:], T.CJ[:], T.CA[:], A.subtract, [full("CA"), full("CJ")], [full("CK")])
-    ts(col["tie"], col["lo"], col["hi"], -0.5, A.is_ge, A.add, [reg["lo"], reg["hi"]], [reg["tie"]])
-    affine("s", col["big"], col["keep"], -1.0, 1.0, [reg["keep"]], [reg["big"]])
+    for a in range(4):
+        step("sv%d" % a)
+        sel(T.SV[:, a, :], T.NM[:], [[-16, 8], [0, 8], [-1, 2]], A.is_equal, -4 * a, [full("NM")], [("SV", 128 * a, 128 * a + 128)])
 
     def digits(name, buf, c0, n):
         step(name)
-        affine(WHO[name], T[buf][:, c0:c0 + 256], T.XL[:], col["even"], T.QH[:, n:n + 1], [full("XL"), reg["even"], ("QH", n, n + 1)], [(buf, c0, c0 + 256)])
+        affine(WHO[name], T[buf][:, c0:c0 + 256], T.XL[:, 16:272], T.CJ[:, 0:1], T.QH[:, n:n + 1], [full("XL"), full("CJ"), ("QH", n, n + 1)], [(buf, c0, c0 + 256)])
 
     for n in range(4):
-        digits("lldig", "LL", 256 * n, n)
+        digits("ll%d" % n, "LL", 256 * n, n)
     for n in range(2):
-        digits("pz0", "PZ", 256 * n, n + 4)
-    step("hb")
+        digits("pz%d" % n, "PZ", 256 * n, n + 4)
     for b in range(1, NB):
-        affine(WHO["hb"], T.HB[:, b - 1, :], T.ONE[:, 0:256], T.QH[:, 2 * b:2 * b + 1], 0.0, [full("ONE"), ("QH", 2 * b, 2 * b + 1)], [("HB", 256 * b - 256, 256 * b)])
+        step("hb%d" % b)
+        if WHO["hb%d" % b] == "v":
+            op("v", lambda e, b=b: e.memset(T.HB[:, b - 1, :], -2.0 * b), [], [("HB", HW * b - HW, HW * b)])
+        else:
+            op("g", lambda e, b=b: e.iota(T.HB[:, b - 1, :], [[0, HW]], -2 * b, 0, allow_small_or_imprecise_dtypes=True), [], [("HB", HW * b - HW, HW * b)])
     step("ni")
-    affine(WHO["ni"], T.NI[:], T.ID[:], -1.0, 0.0, [full("ID")], [full("NI")])
+    if WHO["ni"] == "v":
+        match(T.NI[:], full("NI"), 0, 128, "p", -1.0)
+    else:
+        affine(WHO["ni"], T.NI[:], T.ID[:], -1.0, 0.0, [full("ID")], [full("NI")])
     step("eu16")
     copy("v", T.EU16[:], T.EUI[:], [full("EUI")], [full("EU16")])
 
     def place_scatter(b, h):
-        step("scat%d" % h)
-        src, rd = T.PZ[:, 256 * h:256 * h + 256], [full("PZ"), ("EU16", 0, 128)]
-        dst = T.LL[:, 0:V].indirect(T.EU16[:, 32 * b + 16 * h:32 * b + 16 * h + 16])
+        step(pre[0] + "scat%d" % h)
+        e0, e1 = ((0, SCAT[b]), (SCAT[b], E))[h]
+        if e0 == e1:
+            return
+        src, rd = T.PZ[:, e0:e1], [("PZ", e0, e1), ("EU16", 0, 128)]
+        dst = T.LL[:, 0:V].indirect(T.EU16[:, 32 * b + e0 // 16:32 * b + e1 // 16])
         if b:
-            op("v", lambda e: e.tensor_tensor(dst, src, T.HB[:, b - 1, :], A.add), rd + [("HB", 256 * b - 256, 256 * b)], [("LL", 0, V)], waw=True)
+            op("v", lambda e: e.tensor_tensor(dst, src, T.HB[:, b - 1, 0:e1 - e0], A.add), rd + [("HB", HW * b - HW, HW * b)], [("LL", 0, V)], waw=True)
         else:
             op("v", lambda e: e.tensor_copy(dst, src), rd, [("LL", 0, V)], waw=True)
 
     def place_next(b):
-        for i, (q, c0, c1) in enumerate(NEXT):
-            step("pn%d" % i)
+        for i, (c0, c1) in enumerate(NEXT[b]):
+            name = ("pn%d" if b else "ipn%d") % i
+            step(name)
+            q = WHO[name]
             l0 = 32 * b + 32
             copy(q, T.LL[:, V + c0:V + c1], T.LL[:, 0:V].indirect(T.EU16[:, l0 + c0 // 16:l0 + c1 // 16]), [("LL", 0, V), ("EU16", 0, 128)], [("LL", V + c0, V + c1)])
 
     def place_mm(part, lx):
-        c0, n = (0, V)[part], (64, 32)[part]
+        c0, n = (0, V, 0)[part], (64, 32, 96)[part]
         for i in range(16):
-            step(None, ("pm0", "pm1b" if i >= 8 else "pm1")[part])
+            step(None, "pm1b" if part and i >= 8 else "pm1" if part else pre[0] + "pm0")
             mm(T[lx][:, 0:n], T.ZB[:, 15 - i:143 - i], T.LL[:, c0 + i:c0 + 16 * n:16], i == 0, i == 15, [full("ZB"), ("LL", c0, c0 + 16 * n)], [(lx, 0, n)])
 
     def place_out(b, part, lx):
-        step(("po", "pnout")[part])
-        o, n, c0 = "LW%d" % b, (64, 32)[part], (0, 64)[part]
+        step(("po", "pnout", "po")[part])
+        o, n, c0 = "LW%d" % b, (64, 32, 96)[part], (0, 64, 0)[part]
         copy("v", T[o][:, c0:c0 + n], T[lx][:, 0:n], [(lx, 0, n)], [(o, c0, c0 + n)])
 
     def ring_list(b, h):
-        cx, of, g0 = "CX%d" % h, "OF%d" % b, 256 * h
-        lu, l0, n = ("EU16", 16 * h, V) if b == 0 else ("LW%d" % (b - 1), 64 + 16 * h, V + E * b)
-        step("rg%d" % h, "rs%d" % h)
-        act(T.GR[:, g0:g0 + 256], T.RW[:, 0:n].indirect(T[lu][:, l0:l0 + 16]), [("RW", 0, n), (lu, l0, l0 + 16), reg["big"], reg["keep"]], [("GR", g0, g0 + 256)],
-            F.Abs, bias=col["big"], scale=col["keep"])
+        cx, of, (e0, e1) = "CX%d" % (0 if JOIN[b] else h), "OF%d" % b, RINGS[h]
+        lu, l0, n = ("EU16", 0, V) if b == 0 else ("LW%d" % (b - 1), 64, V + E * b)
+        l0, l1 = l0 + e0 // 16, l0 + e1 // 16
+        step(pre[0] + "rg%d" % h, pre[0] + "rs%d" % h)
+        act(T.GR[:, e0:e1], T.RW[:, 0:n].indirect(T[lu][:, l0:l1]), [("RW", 0, n), (lu, l0, l1)], [("GR", e0, e1)], F.Abs)
         for a in range(4):
-            mm(T[cx][:, 0:64], T.Y2[:, 12 - 4 * a:140 - 4 * a], T.GR[:, g0 + a:g0 + 256:4], a == 0, a == 3, [full("Y2"), ("GR", g0, g0 + 256)], [(cx, 0, 64)])
-        step("ro%d" % h)
-        ts(T[of][:, 64 * h:64 * h + 64], T[cx][:, 0:64], -32.0 * LIFT, None, A.add, None, [(cx, 0, 64)], [(of, 64 * h, 64 * h + 64)])
+            mm(T[cx][:, e0 // 4:e1 // 4], T.Y2[:, 12 - 4 * a:140 - 4 * a], T.GR[:, e0 + a:e1:4], a == 0, a == 3, [full("Y2"), ("GR", e0, e1)], [(cx, e0 // 4, e1 // 4)])
+        if JOIN[b] and not h:
+            return
+        c0, c1 = 0 if JOIN[b] else e0 // 4, e1 // 4
+        step(pre[0] + "ro%d" % h)
+        ts(T[of][:, c0:c1], T[cx][:, c0:c1], LOW, None, A.mult, None, [(cx, c0, c1)], [(of, c0, c1)])
 
     def memory(q, b, out, src, reads, writes):
         if q == "s":
@@ -364,23 +506,29 @@ def rank_program(g, core, T, topo):
         else:
             ts(out, src, -15.0, None, A.add, None, reads, writes)
 
-    def wadd(src, h, start, stop=False):
-        mm(T["W%d" % h][:, 0:256], T.ID[:], T[src][:, 256 * h:256 * h + 256], start, stop, [full("ID"), full(src)], [("W%d" % h, 0, 256)])
+    def part(b, h):
+        e = SLOTS[b][0][2]
+        return ((0, e), (e, E))[h]
+
+    def wadd(b, w, src, h, start, stop=False):
+        e0, e1 = part(b, h)
+        mm(T["W%d" % h][:, 0:e1 - e0], T[w][:], T[src][:, e0:e1], start, stop, [full(w), (src, e0, e1)], [("W%d" % h, 0, e1 - e0)])
 
     def mem_u(b):
-        step("u")
-        tb, mu = "TB%d" % b, "MU%d" % (b % 2)
-        memory("s", b, T[mu][:], T[tb][:, own:own + V].indirect(T.EU16[:, 32 * b:32 * b + 32]), [(tb, own, own + V), ("EU16", 0, 128)], [full(mu)])
+        step(pre[0] + "u")
+        tb = "TB%d" % b
+        for q, (e0, e1) in (("s", part(b, 1)), ("v", part(b, 0))) if UV[b] else (("s", (0, E)),):
+            memory(q, b, T.MU[:, e0:e1], T[tb][:, own:own + V].indirect(T.EU16[:, 32 * b + e0 // 16:32 * b + e1 // 16]), [(tb, own, own + V), ("EU16", 0, 128)], [("MU", e0, e1)])
         for h in range(2):
-            step(None, "wu%d" % h)
-            wadd(mu, h, True)
+            step(None, pre[0] + "wu%d" % h)
+            wadd(b, "ID", "MU", h, True)
 
     def mem_v(b):
         step("v", "wv")
         tb, mv = "TB%d" % b, "MV%d" % (b % 2)
         memory("s", b, T[mv][:], T[tb][:].indirect(T.EV16[:, 32 * b:32 * b + 32]), [full(tb), ("EV16", 0, 128)], [full(mv)])
         for h in range(2):
-            wadd(mv, h, False, bool(h and SUB[b]))
+            wadd(b, "ID", mv, h, False, bool(h and SUB[b]))
 
     def send(b, c0, c1, final):
         tb = "TB%d" % (b + 1)
@@ -399,7 +547,7 @@ def rank_program(g, core, T, topo):
             total["sent"] = total.get("sent", 0) + ne
 
         def arrive():
-            total["arr%d" % b] = len(SENDS) * ne * len(peers)
+            total["arr%d" % b] = len(SENDS[b]) * ne * len(peers)
             for p in peers:
                 o = T.rank_of(p) * V
                 note("far", ("arr%d" % b, total["arr%d" % b], {}), [], [(tb, o, o + V)])
@@ -408,66 +556,67 @@ def rank_program(g, core, T, topo):
         if final:
             item(q="far", kind="far", fn=arrive, reads=[("sends%d" % b, 0, V)], writes=[(tb, T.rank_of(p) * V, T.rank_of(p) * V + V) for p in peers])
 
-    def split(src, tmp, dst, n):
+    def split(name, src, tmp, dst, n):
+        step(name + "and")
         ts(T[tmp][:], T[src][:], 31, None, A.bitwise_and, None, [full(src)], [full(tmp)])
-        ts(T[dst][:, n:2 * n], T[src][:], 1 / 32, LIFT - 0.5 + 1 / 64, A.mult, A.add, [full(src)], [(dst, n, 2 * n)])
-        copy("v", T[dst][:, 0:n], T[tmp][:], [full(tmp)], [(dst, 0, n)])
+        step(name + "hi")
+        ts(T[dst][:, n:2 * n], T[src][:], 1 / HIGH, (LIFT - 0.5 + 1 / 64) / LOW, A.mult, A.add, [full(src)], [(dst, n, 2 * n)])
+        step(name + "lo")
+        ts(T[dst][:, 0:n], T[tmp][:], 1 / LOW, None, A.mult, None, [full(tmp)], [(dst, 0, n)])
 
-    step("rdig", "rw")
-    split("RI", "RJ", "RD", 256)
-    for a in range(4):
-        bk, c0 = "DA%d" % (a // 2), 256 * (a % 2)
-        for j in (1, 0):
-            mm(T[bk][:, c0:c0 + 256], T.ZA[:, a, 1 - j:129 - j], T.RD[:, 256 * j:256 * j + 256], j == 1, j == 0, [full("ZA"), ("RD", 256 * j, 256 * j + 256)], [(bk, c0, c0 + 256)])
-    step("rws")
-    affine("s", T.RW[:, 0:512], T.DA0[:], 1 / LOW, 0.0, [full("DA0")], [("RW", 0, 512)])
-    step("rwv")
-    affine(WHO["rwv"], T.RW[:, 512:V], T.DA1[:], 1 / LOW, 0.0, [full("DA1")], [("RW", 512, V)])
-    step("cd")
-    for k in range(3):
-        affine(WHO["cd"], T.CD[:, k, :], T.ID[:], T.CK[:, k + 1:k + 2], 0.0, [full("ID"), full("CK")], [("CD", 128 * k, 128 * k + 128)])
-    step("ld")
-    mm(T.CX1[:, 0:384], T.BO[:], T.CD[:], True, True, [full("BO"), full("CD")], [("CX1", 0, 384)])
-    copy(WHO["ld"], T.LD[:], T.CX1[:, 0:384], [("CX1", 0, 384)], [full("LD")])
+    split("r", "RI", "RJ", "RD", 256)
+    dmas([("y", T.OB[:, 0:V], T.m0[:, own:own + V])], [full("RD")], [("OB", 0, V)])
+    step(None, "rw")
+    four = ("DA0", "DA1", "LX", "LN")
+    for j in (1, 0):
+        for a, bk in enumerate(four):
+            mm(T[bk][:, 0:256], T.ZA[:, a, 1 - j:129 - j], T.RD[:, 256 * j:256 * j + 256], j == 1, j == 0, [full("ZA"), ("RD", 256 * j, 256 * j + 256)], [(bk, 0, 256)])
+    for a, bk in enumerate(four):
+        step("rw%d" % a)
+        affine(WHO["rw%d" % a], T.RW[:, 256 * a:256 * a + 256], T[bk][:, 0:256], -1.0, col["lift"], [(bk, 0, 256), reg["lift"]], [("RW", 256 * a, 256 * a + 256)])
     ring_list(0, 0)
     ring_list(0, 1)
     place_scatter(0, 0)
     place_scatter(0, 1)
     step("ev16")
     copy("v", T.EV16[:], T.EVI[:], [full("EVI")], [full("EV16")])
-    step("vdig", "vw")
-    split("EVI", "EVJ", "EVD", 128)
+    split("v", "EVI", "EVJ", "EVD", 128)
+    step("vw")
     for z in range(4):
         for j in range(2):
             mm(T.LN[:, z::4], T.LV[:, z, 1 - j:129 - j], T.EVD[:, 128 * j:128 * j + 128], j == 0, j == 1, [("LV", 144 * z, 144 * z + 144), full("EVD")], [full("LN")])
     step("vw")
-    affine(WHO["vw"], T.VW[:], T.LN[:], 1 / LOW, 0.0, [full("LN")], [full("VW")])
-    place_mm(0, "DA0")
+    affine(WHO["vw"], T.VW[:], T.LN[:], -1.0, col["lift"], [full("LN"), reg["lift"]], [full("VW")])
+    if not ONEPM[0]:
+        place_mm(0, "DA1")
     mem_u(0)
+    pre[0] = ""
 
     for b in range(NB):
         last = b == NB - 1
         tb, mt, mv, of = "TB%d" % b, "MT%d" % (b % 2), "MV%d" % (b % 2), "OF%d" % b
-        step(None, None, b + 1)
+        step(None, None, b)
 
-        def slots(c0, c1):
-            step("s%d" % c0)
-            memory("vs"[c0 // 2], b, T[mt][:, 512 * c0:512 * c1], T[tb][:].indirect(T[of][:, 32 * c0:32 * c1]), [full(tb), (of, 32 * c0, 32 * c1)], [(mt, 512 * c0, 512 * c1)])
+        def slots(i, q, e0, e1):
+            step("s%d" % i)
+            memory(q, b, T[mt][:, 4 * e0:4 * e1], T[tb][:].indirect(T[of][:, e0 // 4:e1 // 4]), [full(tb), (of, e0 // 4, e1 // 4)], [(mt, 4 * e0, 4 * e1)])
 
-        def largest(c0, c1):
-            step("m%d" % c0)
-            s = (512 * c0, 512 * c1)
-            x = T[mt][:, s[0]:s[1]]
-            op("v", lambda e: e.tensor_tensor_scan(T.MX[:, s[0]:s[1]], T.RS[:, 0:s[1] - s[0]], x, 0.0, A.min, A.max), [("RS", 0, s[1] - s[0]), (mt,) + s], [("MX",) + s])
+        def largest(i, e0, e1):
+            step("m%d" % i)
+            for e in range(e0, e1, 256):
+                s = (4 * e, 4 * min(e + 256, e1))
+                op("v", lambda q, s=s, mt=mt: q.tensor_tensor_scan(T.MX[:, s[0]:s[1]], T.RS[:, 0:s[1] - s[0]], T[mt][:, s[0]:s[1]], 0.0, A.min, A.max),
+                   [("RS", 0, s[1] - s[0]), (mt,) + s], [("MX",) + s])
 
         def clip(h):
             step("clip%d" % h, "ws%d" % h)
-            s, o, w = (1024 * h, 1024 * h + 1024), V + E * b + 256 * h, "W%d" % h
+            e0, e1 = part(b, h)
+            s, o, w, n = (4 * e0, 4 * e1), V + E * b + e0, "W%d" % h, e1 - e0
             if h and SUB[b]:
-                tt(T.OB[:, o:o + 256], T[w][:, 0:256], T.MX[:, s[0] + 3:s[1]:4], A.subtract, [("MX",) + s, (w, 0, 256)], [("OB", o, o + 256)])
+                tt(T.OB[:, o:o + n], T[w][:, 0:n], T.MX[:, s[0] + 3:s[1]:4], A.subtract, [("MX",) + s, (w, 0, n)], [("OB", o, o + n)])
                 return
-            mm(T[w][:, 0:256], T.NI[:], T.MX[:, s[0] + 3:s[1]:4], False, True, [full("NI"), ("MX",) + s], [(w, 0, 256)])
-            affine("s", T.OB[:, o:o + 256], T[w][:, 0:256], 1.0, (-15.0, 0.0)[h], [(w, 0, 256)], [("OB", o, o + 256)])
+            mm(T[w][:, 0:n], T.NI[:], T.MX[:, s[0] + 3:s[1]:4], False, True, [full("NI"), ("MX",) + s], [(w, 0, n)])
+            affine("s", T.OB[:, o:o + n], T[w][:, 0:n], 1.0, 0.0 if h or UV[b] else -15.0, [(w, 0, n)], [("OB", o, o + n)])
 
         def where(h, j):
             return (("DA%d" % h, 0), ("DA%d" % h, 256), ("CX%d" % h, 256))[j]
@@ -490,68 +639,95 @@ def rank_program(g, core, T, topo):
             for i, j in enumerate((2, 0, 1)):
                 p = 256 * (3 * h + j)
                 mm(T[cx][:, 0:256], T.LD[:, j, :], T.PR[:, p:p + 256], i == 0, i == 2, [full("LD"), ("PR", p, p + 256)], [(cx, 0, 256)])
+            sign(h, cx)
+
+        def wide_diff(h):
+            for j, bk in enumerate(("DA0", "CX0", "DA1")):
+                step(None, "d%d%d" % (j, h))
+                for w, k in (("ID", j + 1), ("NI", 0)):
+                    mm(T[bk][:, 256 * h:256 * h + 256], T[w][:], T[mt][:, 1024 * h + k:1024 * h + 1024:4], w == "ID", w == "NI",
+                       [full(w), (mt, 1024 * h, 1024 * h + 1024)], [(bk, 256 * h, 256 * h + 256)])
+
+        def wide_lowest():
+            for j, bk in enumerate(("DA0", "CX0", "DA1")):
+                for i, (e0, e1) in enumerate(((0, 256), (256, E)) if j == 2 and WIDE[b] == 2 else ((0, E),)):
+                    step("p%d" % (j + i))
+                    tt(T.PR[:, E * j + e0:E * j + e1], T[bk][:, e0:e1], T[mv][:, e0:e1], A.mult, [(bk, e0, e1), full(mv)], [("PR", E * j + e0, E * j + e1)])
+                for h, cx in enumerate(("CX1", "W1")):
+                    step(None, "cd%d%d" % (j, h))
+                    p = E * j + 256 * h
+                    mm(T[cx][:, 0:256], T.LD[:, j, :], T.PR[:, p:p + 256], j == 0, j == 2, [full("LD"), ("PR", p, p + 256)], [(cx, 0, 256)])
+            for h, cx in enumerate(("CX1", "W1")):
+                sign(h, cx)
+
+        def sign(h, cx):
             step("sg%d" % h)
-            act(T.SG[:, 256 * h:256 * h + 256], T[cx][:, 0:256], [(cx, 0, 256), reg["tie"]], [("SG", 256 * h, 256 * h + 256)], F.Sign, bias=col["tie"])
+            rd, wr = [(cx, 0, 256), reg["tie"]], [("SG", 256 * h, 256 * h + 256)]
+            if SIGN[b][h] == "s":
+                act(T.SG[:, 256 * h:256 * h + 256], T[cx][:, 0:256], rd, wr, F.Relu, bias=col["tie"])
+            else:
+                ts(T.SG[:, 256 * h:256 * h + 256], T[cx][:, 0:256], col["tie"], 0.0, A.add, A.is_gt, rd, wr)
 
         def renew(h):
             step(None, "of%d" % h)
             w, c0, s, o = ("LN", "LX")[h], 128 * b + 64 * h, 256 * h, V + E * b + 256 * h
-            mm(T[w][:, 256:512], T.LC[:], T.M1[:], True, False, [full("LC"), full("M1")], [(w, 256, 512)])
             for a in range(4):
-                mm(T[w][:, 256 + a:512:4], T.SV[:, a, :], T.VW[:, c0:c0 + 64], False, False, [("SV", 128 * a, 128 * a + 128), full("VW")], [(w, 256, 512)])
+                mm(T[w][:, 256 + a:512:4], T.SV[:, a, :], T.VW[:, c0:c0 + 64], a == 0, False, [("SV", 128 * a, 128 * a + 128), full("VW")], [(w, 256, 512)])
             step("rn%d" % h, "ct%d" % h)
             mm(T[w][:, 256:512], T.LC[:], T.SG[:, s:s + 256], False, True, [full("LC"), ("SG", s, s + 256)], [(w, 256, 512)])
             tt(T.RW[:, o:o + 256], T[w][:, 256:512], T.GR[:, s:s + 256], A.min, [(w, 256, 512), ("GR", s, s + 256)], [("RW", o, o + 256)])
 
         mem_v(b)
-        for c0, c1 in ((0, 2), (2, 3), (3, 4)):
-            slots(c0, c1)
-        for c0, c1 in ((0, 2), (2, 3), (3, 4)) if b else ((0, 1), (1, 2), (2, 3), (3, 4)):
-            largest(c0, c1)
-        place_out(b, 0, "DA0")
-        if not last:
+        for i, (q, e0, e1) in enumerate(SLOTS[b]):
+            slots(i, q, e0, e1)
+        for i, (q, e0, e1) in enumerate(SLOTS[b]):
+            largest(i, e0, e1)
+        if ONEPM[b]:
             place_next(b)
-        if b == 0:
-            place_mm(1, "LX")
-            place_out(b, 1, "LX")
+            place_mm(2, "DA1")
+            place_out(b, 2, "DA1")
+        else:
+            place_out(b, 0, "DA1")
+            if not last:
+                place_next(b)
         for h in range(2):
             clip(h)
-            diff(h)
+            (wide_diff if WIDE[b] else diff)(h)
+        if not last and not ONEPM[b]:
+            place_mm(1, "W0")
+            place_out(b, 1, "W0")
         n, lw = V + E * (b + 1), "LW%d" % b
         if not last:
             nx = "TB%d" % (b + 1)
-            for i, (q, c0, c1) in enumerate(PIECES):
+            for i, (q, c0, c1) in enumerate(PIECES[b]):
                 step("blk%d" % i)
-                act(T[nx][:, own + c0:own + c1], T.OB[:, 0:n].indirect(T[lw][:, c0 // 16:c1 // 16]), [("OB", 0, n), (lw, 0, 64)], [(nx, own + c0, own + c1)],
-                    F.Relu, bias=15.0, scale=-1.0)
-            step("send")
-            for c0, c1 in SENDS:
-                send(b, c0, c1, (c0, c1) == SENDS[-1])
+                out, src, rd, wr = T[nx][:, own + c0:own + c1], T.OB[:, 0:n].indirect(T[lw][:, c0 // 16:c1 // 16]), [("OB", 0, n), (lw, 0, 64)], [(nx, own + c0, own + c1)]
+                act(out, src, rd, wr, F.Relu, bias=15.0, scale=-1.0)
+            for i, (c0, c1) in enumerate(SENDS[b]):
+                step("send%d" % i)
+                send(b, c0, c1, (c0, c1) == SENDS[b][-1])
+        if WIDE[b]:
+            wide_lowest()
         for h in range(2):
-            lowest(h)
+            if not WIDE[b]:
+                lowest(h)
             renew(h)
-        if b and not last:
-            place_mm(1, "DA1")
-            place_out(b, 1, "DA1")
         if not last:
             mem_u(b + 1)
             place_scatter(b + 1, 0)
             place_scatter(b + 1, 1)
             for h in range(2):
                 ring_list(b + 1, h)
-            place_mm(0, "DA0")
+            if not ONEPM[b + 1]:
+                place_mm(0, "DA1")
 
-    for a in range(4):
-        step("yg%d" % a)
-        out, src, rd, wr = T.YG[:, 256 * a:256 * a + 256], T.RW[:, 0:n].indirect(T[lw][:, 16 * a:16 * a + 16]), [("RW", 0, n), (lw, 0, 64)], [("YG", 256 * a, 256 * a + 256)]
-        if WHO["yg%d" % a] == "s":
-            act(out, src, rd, wr, F.Relu)
-        else:
-            ts(out, src, 0.0, None, A.max, None, rd, wr)
+    for i, (q, c0, c1) in enumerate(YRINGS):
+        step("yg%d" % i)
+        copy(q, T.YG[:, c0:c1], T.RW[:, 0:n].indirect(T[lw][:, c0 // 16:c1 // 16]), [("RW", 0, n), (lw, 0, 64)], [("YG", c0, c1)])
     step("yr")
     for i, a in enumerate(YORDER):
         mm(T.DA0[:, 0:256], T.Y1[:, 3 - a:131 - a], T.YG[:, 256 * a:256 * a + 256], i == 0, i == 3, [full("Y1"), ("YG", 256 * a, 256 * a + 256)], [("DA0", 0, 256)])
-    affine(WHO["yr"], T.YR[:], T.DA0[:, 0:256], 1.0, -32.0 * LIFT, [("DA0", 0, 256)], [full("YR")])
+    act(T.YR[:], T.DA0[:, 0:256], [("DA0", 0, 256)], [full("YR")], F.Abs)
     outs = {"yr": (T.yr[:], T.YR[:], full("YR"))}
     for i, (q, c0, c1) in enumerate(YPIECES):
         step("blk%d" % i)

from concourse.bass import DstId, RemoteDMATransfer
from concourse.mybir import AluOpType as A, ActivationFunctionType as F

NB, V, E, R = 4, 1024, 512, 4
BF, F32, I32, U16 = "bfloat16", "float32", "int32", "uint16"
LOW, HIGH, LIFT = 512.0, 16384.0, 129
PIECES = [(("s", 0, 128), ("s", 128, 768), ("s", 768, 1024))] + [(("s", 0, 320), ("s", 320, 768), ("s", 768, 1024))] * (NB - 2)
SENDS = [tuple(x[1:] for x in p) for p in PIECES]
NEXT = [((0, 256), (256, 512))] * NB
JOIN = (0, 0, 0, 0)
YPIECES = (("s", 0, 640), ("s", 640, 1024))
YRINGS = (("s", 0, 256), ("s", 256, 512), ("v", 512, 768), ("v", 768, 1024))
YORDER = (0, 2, 1, 3)
OUTS = (("y", "ym0"), ("y", "ym1"), ("s", "yr"))
SUB = (1, 1, 1, 0)
FIRST = {"v": "one cols cj qh ck tie cwy bo y2 ceven pz0 ll1 rhi rand rlo ev16 vand eu16 rw1 zb iscat0 v iro1 iro0 iscat1 s0 m1 m0 m2 po clip1 vlo vhi ipn0 p0 p1 p2 scat0 pnout rn0 rn1 scat1 ro0 ro1",
         "s": "cpy clift ll3 pz1 i15 ni ll2 cwz ll0 cd rw0 rw2 rw3 irg1 irg0 iu s1 s2 ld clip0 ipn1 blk0 blk1 blk2 vw sg0 sg1 u rg0 rg1",
         "p": "rw irs1 irs0 iwu1 iwu0 ld wv ipm0 ws0 d00 d10 d11 d20 d01 d21 vw cd01 pm1 pm1b cd00 cd11 cd10 cd20 cd21 of0 ct0 of1 ct1 wu0 rs0 rs1 pm0 wu1",
         "g": "rows bo id za rs lc lv sv0 sv1 sv2 sv3 hb1 send0 send1 send2 hb2 hb3 zr y1"}
TURN = {"v": "v s0 po m0 m1 m2 clip1 p0 p1 p2 scat0 pnout rn0 rn1 scat1 ro0 ro1",
        "s": "pn1 s1 s2 pn0 clip0 blk0 blk1 blk2 sg0 sg1 u rg0 rg1",
        "p": "of1 of0 wv d20 d00 d10 ws0 d01 d11 pm1 d21 pm1b cd00 cd10 cd01 cd11 cd20 cd21 ct0 ct1 wu0 wu1 rs0 rs1 pm0",
        "g": "send0 send1 send2"}
LAST = {"v": "v s0 po m1 m0 m2 p0 p1 p2 p3 top0 rn0 rn1 yg2 yg3 top1",
        "s": "s1 s2 clip0 clip1 blk0 sg0 sg1 blk1 yg0 yg1 yr",
        "p": "of0 wv of1 d00 d10 d20 ws0 d01 ws1 d11 d21 cd00 cd01 cd10 cd11 cd20 cd21 ct0 ct1 yr",
        "g": ""}
WHO = {"pz0": "v", "pz1": "s", "ni": "s", "cd": "s", "ll0": "s", "ll1": "v", "ll2": "s", "ll3": "s", "ld": "s", "vw": "s",
       "rw0": "s", "rw1": "v", "rw2": "s", "rw3": "s", "id": "g", "za": "g", "lv": "g", "y2": "v", "hb1": "g", "hb2": "g", "hb3": "g", "i15": "s", "ipn0": "v", "ipn1": "s", "pn0": "s", "pn1": "s"}
PARTS = [((0, 256), (256, 512))] * NB
SLOTS = [(("v", 256, 416), ("s", 0, 256), ("s", 416, 512))] + [(("v", 256, 384), ("s", 0, 256), ("s", 384, 512))] * (NB - 1)
SIGN = ("ss", "ss", "ss", "ss")
LATE = 0
SCAT, HW = (256, 256, 256, 256), 320
UV = (0, 0, 0, 0)
DIAG = 0
WIDE = (1, 1, 1, 2)
ONEPM = (0, 0, 0, 0)
RINGS = ((0, 256), (256, 512))

PIECES = [(("s", 0, 64), ("s", 64, 1024))] + [(("s", 0, 256), ("s", 256, 640), ("s", 640, 1024))] * (NB - 2)
SENDS = [tuple(x[1:] for x in p) for p in PIECES]
NEXT = [((0, 256), (256, 512))] + [((0, 512),)] * (NB - 1)
WIDE, DIAG = (0, 0, 0, 0), 1
SLOTS = [(("v", 0, 256), ("s", 256, 384), ("s", 384, 512))] * NB
FIRST = {"v": "one cols cj qh ck cwy ni ceven tie pz0 bo cd rhi rand rlo ev16 eu16 vand rw1 rw3 iscat0 y2 zb iscat1 iro0 iro1 s0 po m0 m2 m1 vhi clip1 vlo p0 p1 vw scat0 pnout rn0 rn1 scat1 ro0 ro1",
         "s": "ll0 pz1 ll2 cwz ll1 ll3 clift cpy rw0 rw2 irg0 irg1 iu v s2 s1 ld clip0 ipn0 blk0 blk1 ipn1 sg1 sg0 u rg0 rg1",
         "p": "rw irs0 irs1 ld iwu1 iwu0 ipm0 wv e0 ws0 d0 e1 d1 vw cd0 cd1 pm1 pm1b of0 ct0 of1 ct1 wu1 wu0 rs0 rs1 pm0",
         "g": "rows bo id za rs lc lv sv0 sv1 sv2 sv3 hb1 send0 send1 hb2 hb3 zr y1"}
TURN = {"v": "s0 m0 m2 m1 po clip1 p0 p1 scat0 pnout rn0 rn1 scat1 ro0 ro1",
        "s": "v s2 s1 pn0 clip0 blk0 blk1 blk2 sg0 sg1 u rg0 rg1",
        "p": "of0 wv of1 e0 ws0 d0 d1 e1 cd0 pm1 cd1 pm1b ct0 ct1 wu1 wu0 rs0 rs1 pm0",
        "g": "send0 send1 send2"}
LAST = {"v": "s0 po m0 m1 m2 p0 p1 rn0 rn1 yg2 yg3 top0 top1",
        "s": "v s1 s2 clip0 clip1 blk0 sg0 sg1 blk1 yg0 yg1 yr",
        "p": "of0 wv of1 e0 ws0 d0 ws1 d1 e1 cd0 cd1 ct0 ct1 yr",
        "g": ""}
WHO.update({"pz0": "v", "pz1": "s", "ni": "v", "cd": "v", "ll0": "s", "ll1": "s", "ll2": "s", "ll3": "s", "ld": "s", "vw": "v",
            "rw0": "s", "rw1": "v", "rw2": "s", "rw3": "v", "ipn0": "s", "ipn1": "s", "pn0": "s"})

SIGN = ("vs", "vs", "vs", "vs")
SLOTS[1] = SLOTS[2] = (("v", 0, 256), ("s", 256, 512))
FIRST = {"v": "one cols qh cj tie ck ll0 cwy cd bo pz1 ceven rhi rand eu16 rlo vand zb ev16 rw1 rw3 iscat0 y2 iscat1 vlo iro0 iro1 s0 vhi m0 m2 m1 po clip1 p0 p1 vw ipn0 sg0 scat0 pnout rn1 rn0 scat1 ro0 ro1",
         "s": "clift ll1 ni pz0 ll2 cwz cpy ll3 rw0 rw2 irg1 irg0 iu v s2 s1 ld clip0 blk0 blk1 ipn1 sg1 u rg0 rg1",
         "p": "rw ld irs0 irs1 iwu0 iwu1 ipm0 wv e0 ws0 d0 d1 e1 vw cd0 cd1 of0 of1 pm1 pm1b ct1 ct0 wu1 wu0 rs0 rs1 pm0",
         "g": "rows bo id za rs lc lv sv0 sv1 sv2 sv3 hb1 send0 send1 hb2 hb3 zr y1"}
TURN = {"v": "s0 po m0 m1 clip1 p0 p1 sg0 scat0 rn0 rn1 pnout scat1 ro0 ro1",
        "s": "v s1 pn0 clip0 blk0 blk1 blk2 sg1 u rg0 rg1",
        "p": "of0 wv e0 ws0 d0 d1 e1 cd0 of1 cd1 pm1 ct0 ct1 pm1b wu1 wu0 rs0 rs1 pm0",
        "g": "send0 send1 send2"}
LAST = {"v": "s0 po m0 m1 m2 p0 p1 sg0 rn0 rn1 yg2 yg3 top0 top1",
        "s": "v s1 s2 clip0 clip1 blk0 sg1 blk1 yg0 yg1 yr",
        "p": "of0 of1 wv e0 d0 ws0 d1 ws1 e1 cd0 cd1 ct0 ct1 yr",
        "g": ""}
WHO.update({"pz0": "s", "pz1": "v", "ni": "s", "cd": "v", "ll0": "v", "ll1": "s", "ll2": "s", "ll3": "s", "ld": "s", "vw": "v",
            "rw0": "s", "rw1": "v", "rw2": "s", "rw3": "v", "ipn0": "v", "ipn1": "s", "pn0": "s"})

SIGN = ("ss", "vs", "vs", "vs")
SLOTS[0] = SLOTS[1]
SCAT = (192, 192, 192, 192)
FIRST = {"v": "one cols qh cj bo cwy ll2 ld3 ceven ld1 y2 le1 ld2 rhi rand eu16 rlo iscat0 vand vhi rw1 zb rw3 ev16 iscat1 iro0 iro1 s0 po m0 m1 vlo clip1 le2 ipn0 tie p0 le3 p1 scat0 pnout rn0 rn1 scat1 ro0 ro1",
         "s": "cpy clift ll3 ll1 ll0 pz0 pz1 ni cwz rw0 rw2 iu irg0 irg1 v s1 ipn1 clip0 blk0 blk1 vw sg0 sg1 u rg0 rg1",
         "p": "rw iwu0 irs0 irs1 ipm0 iwu1 wv e0 ws0 d0 d1 e1 vw pm1 pm1b cd0 cd1 of0 ct0 of1 ct1 rs0 rs1 wu0 pm0 wu1",
         "g": "rows bo ld id za rs lc lv sv0 sv1 sv2 sv3 hb1 send0 send1 hb2 hb3 zr y1"}
TURN = {"v": "s0 po m0 m1 clip1 p0 p1 sg0 scat0 rn0 pnout rn1 scat1 ro0 ro1",
        "s": "v s1 pn0 clip0 blk0 blk1 blk2 sg1 u rg0 rg1",
        "p": "wv of1 of0 e0 ws0 d0 e1 d1 cd0 pm1 cd1 ct0 pm1b ct1 rs0 wu1 rs1 pm0 wu0",
        "g": "send0 send1 send2"}
WHO.update({"pz0": "s", "pz1": "s", "ni": "s", "ll0": "s", "ll1": "s", "ll2": "v", "ll3": "s", "vw": "s",
            "rw0": "s", "rw1": "v", "rw2": "s", "rw3": "v", "ipn0": "v", "ipn1": "s"})

UV = (1, 0, 0, 0)
FIRST = {"v": "one cols cj qh ceven ll0 cwy ld1 ld3 ld2 zb bo eu16 rhi rand le1 rlo y2 ev16 vhi iscat0 rw3 vand iscat1 iro0 iro1 iu s0 tie m0 m1 po clip1 ipn0 le3 vlo le2 p0 p1 scat0 pnout rn0 rn1 scat1 ro0 ro1",
         "s": "cpy clift pz0 cwz ll3 ni ll2 ll1 pz1 rw0 rw1 rw2 irg0 irg1 iu v s1 ipn1 clip0 blk0 blk1 vw sg0 sg1 u rg0 rg1",
         "p": "rw irs0 irs1 iwu0 ipm0 iwu1 wv e0 ws0 d0 d1 e1 pm1 vw cd0 pm1b cd1 of0 ct0 of1 ct1 wu1 wu0 rs0 rs1 pm0",
         "g": "rows bo ld id za rs lc lv sv0 sv1 sv2 sv3 hb1 send0 send1 hb2 hb3 zr y1"}
WHO.update({"pz0": "s", "pz1": "s", "ni": "s", "ll0": "v", "ll1": "s", "ll2": "s", "ll3": "s", "vw": "s",
            "rw0": "s", "rw1": "s", "rw2": "s", "rw3": "v", "ipn0": "v", "ipn1": "s"})

FIRST = {"v": "one cols cj qh hb1 ceven id cwy ld3 ld1 ld2 zb y2 bo rhi rand le1 rlo eu16 vand iscat0 rw3 vhi ev16 iscat1 iro0 iro1 iu s0 tie m0 m1 po clip1 ipn0 vlo le3 p0 le2 p1 scat0 rn0 pnout rn1 scat1 ro0 ro1",
         "s": "cpy ll1 cwz pz0 pz1 ll3 ll0 clift ll2 ni rw0 rw1 rw2 irg0 irg1 v iu s1 ipn1 clip0 blk0 blk1 vw sg0 sg1 u rg0 rg1",
         "p": "rw irs0 irs1 ipm0 iwu1 iwu0 wv e0 ws0 d0 d1 e1 pm1 vw pm1b cd0 cd1 of0 ct0 of1 ct1 rs0 wu1 rs1 wu0 pm0",
         "g": "rows ld bo za rs lc lv sv0 sv1 sv2 sv3 send0 send1 hb2 hb3 zr y1"}
WHO.update({"hb1": "v", "id": "v", "ll0": "s"})

FIRST = {"v": "one cols cj qh cwy ceven y2 hb1 id ld3 ld2 ld1 bo zb rhi rand vand rlo eu16 vhi iscat0 rw3 iscat1 ev16 tie le1 iro0 iu iro1 s0 po m0 m1 clip1 ipn0 le3 vlo le2 p0 p1 pnout scat0 rn0 rn1 scat1 ro0 ro1",
         "s": "cpy clift ll2 cwz ll3 ll1 pz0 ll0 pz1 ni rw0 rw1 rw2 irg0 irg1 iu v s1 ipn1 clip0 blk0 blk1 vw sg0 sg1 u rg0 rg1",
         "p": "rw irs0 irs1 ipm0 iwu1 iwu0 wv e0 ws0 d1 d0 e1 pm1 vw pm1b cd0 cd1 of0 ct0 of1 ct1 wu0 rs0 rs1 pm0 wu1",
         "g": "rows ld bo za lc rs lc1 lv lc2 sv0 sv1 sv2 sv3 send0 send1 hb2 hb3 zr y1"}

SCRATCH = {
    "OB": ("sbuf", [128, V + NB * E], BF),
    "RW": ("sbuf", [128, V + NB * E], BF),
    "RI": ("sbuf", [128, 256], I32), "RJ": ("sbuf", [128, 256], I32), "RD": ("sbuf", [128, 512], BF),
    "EUI": ("sbuf", [128, 128], I32), "EVI": ("sbuf", [128, 128], I32), "EVJ": ("sbuf", [128, 128], I32), "EVD": ("sbuf", [128, 256], BF),
    "EU16": ("sbuf", [128, 128], U16), "EV16": ("sbuf", [128, 128], U16),
    "MX": ("sbuf", [128, 2048], BF), "PR": ("sbuf", [128, 1536], BF),
    "SG": ("sbuf", [128, 512], BF), "GR": ("sbuf", [128, 512], BF),
    "VW": ("sbuf", [128, 512], BF),
    "YB": ("sbuf", [128, V], BF), "YG": ("sbuf", [128, V], BF), "YR": ("sbuf", [128, 256], F32),
    "ONE": ("sbuf", [128, 528], BF), "NM": ("sbuf", [128, 128], BF), "ZR": ("sbuf", [128, 144], BF),
    "ID": ("sbuf", [128, 128], BF), "NI": ("sbuf", [128, 128], BF),
    "ZB": ("sbuf", [128, 144], BF), "RQ": ("sbuf", [128, 16], F32), "QH": ("sbuf", [128, 16], F32),
    "XL": ("sbuf", [128, 272], BF), "PZ": ("sbuf", [128, E], BF), "HB": ("sbuf", [128, NB - 1, HW], BF),
    "ZA": ("sbuf", [128, 4, 132], BF), "LV": ("sbuf", [128, 4, 144], BF), "Y2": ("sbuf", [128, 144], BF),
    "Y1": ("sbuf", [128, 144], BF), "LC": ("sbuf", [128, 128], BF), "SV": ("sbuf", [128, 4, 128], BF),
    "BO": ("sbuf", [128, 32], BF), "B1": ("sbuf", [128, 32], BF), "B2": ("sbuf", [128, 128], BF), "B3": ("sbuf", [128, 144], BF),
    "LD": ("sbuf", [128, 3, 128], BF), "CJ": ("sbuf", [128, 4], F32), "CA": ("sbuf", [128, 4], F32),
    "RS": ("sbuf", [128, 1024], BF), "LL": ("sbuf", [128, V + E], BF),
    "PC": ("sbuf", [128, 8], I32), "CF": ("sbuf", [128, 24], F32),
    "MU": ("sbuf", [128, E], BF),
    "W0": ("psum", [128, 512], F32), "W1": ("psum", [128, 512], F32), "LX": ("psum", [128, 512], F32), "LN": ("psum", [128, 512], F32),
    "DA0": ("psum", [128, 512], F32), "DA1": ("psum", [128, 512], F32), "CX0": ("psum", [128, 512], F32), "CX1": ("psum", [128, 512], F32),
}
for _c in range(4):
    SCRATCH["TB%d" % _c] = ("sbuf", [128, 4 * V], BF)
    SCRATCH["OF%d" % _c] = ("sbuf", [128, 128], U16)
    SCRATCH["LW%d" % _c] = ("sbuf", [128, 96], U16)
for _c in range(2):
    SCRATCH["MV%d" % _c] = ("sbuf", [128, 512], BF)
    SCRATCH["MT%d" % _c] = ("sbuf", [128, 2048], BF)
NDMA = 12
SEMAPHORES = ["cv", "cs", "cp", "cg", "sent"] + ["arr%d" % b for b in range(NB)] + ["d%d" % i for i in range(NDMA)]


def rank_program(g, core, T, topo):
    rank = T.rank_of(core)
    if rank is None:
        return
    peers = [c for c in T.cores if c != core]
    own = rank * V
    QU = {"v": g.vector, "s": g.scalar, "p": g.tensor, "g": g, "y": g.sync}
    known = {q: {} for q in QU}
    stage, prog = [0, None, None], []
    total, waited, acc, ndma, clks = {}, {}, {}, [0], {}
    psum = {n for n in SCRATCH if SCRATCH[n][0] == "psum"}
    turns = [FIRST] + [TURN] * (NB - 2) + [LAST]
    pre = ["i"]

    def wait(q, rec):
        sem, val, clk = rec
        if known[q].get(sem, 0) >= val:
            return
        QU[q].wait_ge(T.sem[sem], val)
        waited[sem] = max(waited.get(sem, 0), val)
        for s, x in clk.items():
            known[q][s] = max(known[q].get(s, 0), x)
        known[q][sem] = max(known[q].get(sem, 0), val)

    def order(q, reads, writes, dma=False, waw=False):
        deps = []
        for mode, regs in ((0, reads), (1, writes)):
            for (b, c0, c1) in regs:
                for (aq, aw, a0, a1, rec) in acc.get(b, []):
                    ps = b in psum
                    hit = a1 > c0 and c1 > a0
                    if not ps and not hit:
                        continue
                    same = aq == q and not dma
                    if mode == 0 and ((aw and hit) or (ps and not same)):
                        deps.append(rec)
                    elif mode == 1 and (not same or waw):
                        deps.append(rec)
        for rec in sorted(deps, key=lambda x: -sum(x[2].values()) - x[1]):
            wait(q, rec)

    def note(q, rec, reads, writes):
        for w, regs in ((False, reads), (True, writes)):
            for (b, c0, c1) in regs:
                lst = acc.setdefault(b, [])
                if w and b not in psum:
                    lst[:] = [x for x in lst if not (c0 <= x[2] and x[3] <= c1)]
                lst.append((q, w, c0, c1, rec))

    def emit(k):
        q, reads, writes = k["q"], k["reads"], k["writes"]
        if k["kind"] == "op":
            order(q, reads, writes, waw=k["waw"])
            sem = "c" + q
            k["fn"](QU[q]).then_inc(T.sem[sem], 1)
            total[sem] = total.get(sem, 0) + 1
            note(q, (sem, total[sem], dict(known[q])), reads, writes)
        elif k["kind"] == "dma":
            order(q, reads, writes, dma=True)
            QU[q].dma_start(*k["fn"]).then_inc(T.sem[k["sem"]], 16)
            total[k["sem"]] = 16 * k["n"]
            clk = clks.setdefault(k["sem"], [0, {}])
            for s, x in known[q].items():
                clk[1][s] = max(clk[1].get(s, 0), x)
            clk[0] += 1
            if clk[0] == k["n"]:
                note("dma" + k["sem"], (k["sem"], total[k["sem"]], clk[1]), reads, writes)
        else:
            if k["kind"] == "send":
                order("g", reads, [])
            k["fn"]()

    def step(name, p=None, turn=None):
        stage[1:] = [name, p or name]
        if turn is not None:
            stage[0] = turn

    def item(**k):
        turn, name = stage[0], stage[2 if k["q"] == "p" else 1]
        k["at"], k["where"] = (turn and len(turns), 0), (turn, name)
        if k["q"] in "vspg" and k["kind"] != "dma":
            if name not in turns[turn][k["q"]].split():
                turn, name = turn + 1, "+" + name
            k["at"] = (turn, 1 + turns[turn][k["q"]].split().index(name))
        prog.append(k)

    def op(q, fn, reads, writes, waw=False):
        item(q=q, kind="op", fn=fn, reads=reads, writes=writes, waw=waw)

    def dmas(parts, reads, writes):
        sem = "d%d" % ndma[0]
        ndma[0] += 1
        for q, out, in_ in parts:
            item(q=q, kind="dma", fn=(out, in_), reads=reads, writes=writes, sem=sem, n=len(parts))

    def plan():
        n = len(prog)
        after, then = [set() for _ in range(n)], [[] for _ in range(n)]
        seen, bank = {}, {}
        for q in QU:
            mine = sorted((j for j in range(n) if prog[j]["q"] == q), key=lambda j: (prog[j]["at"], j))
            for i, j in zip(mine, mine[1:]):
                after[j].add(i)
        for j, k in enumerate(prog):
            regs = [(0,) + r for r in k["reads"]] + [(1,) + r for r in k["writes"]]
            for w, b, c0, c1 in regs:
                if b in psum:
                    if bank.get(b, j) != j:
                        after[j].add(bank[b])
                    continue
                for (i, w2, a0, a1) in seen.get(b, []):
                    together = k["kind"] == prog[i]["kind"] == "dma" and k["sem"] == prog[i]["sem"]
                    if i != j and (w or w2) and a1 > c0 and c1 > a0 and not together:
                        after[j].add(i)
            for w, b, c0, c1 in regs:
                if b in psum:
                    bank[b] = j
                else:
                    seen.setdefault(b, []).append((j, w, c0, c1))
        for j in range(n):
            for i in after[j]:
                then[i].append(j)
        left = [len(after[j]) for j in range(n)]
        line = [j for j in range(n) if not left[j]]
        for j in line:
            for i in then[j]:
                left[i] -= 1
                if not left[i]:
                    line.append(i)
        assert len(line) == n
        return line

    def full(n):
        c = 1
        for d in SCRATCH[n][1][1:]:
            c *= d
        return (n, 0, c)

    def mm(out, lhsT, rhs, start, stop, reads, writes):
        op("p", lambda e: e.matmul(out, lhsT, rhs, start, stop), reads, writes)

    def act(out, in_, reads, writes, f=F.Copy, **k):
        op("s", lambda e: e.activation(out, in_, f, **k), reads, writes)

    def sel(out, in_, pat, cmp, base, reads, writes, fill=0.0, cm=1):
        op("g", lambda e: e.affine_select(out, in_, pat, cmp, fill, base, cm), reads, writes)

    def iota(name, pat, base=0):
        op("g", lambda e: e.iota(T[name][:], pat, base, 0, allow_small_or_imprecise_dtypes=True), [], [full(name)])

    def ts(out, in_, s1, s2, o0, o1, reads, writes):
        if o1 is None:
            op("v", lambda e: e.tensor_scalar(out, in_, s1, None, o0), reads, writes)
        else:
            op("v", lambda e: e.tensor_scalar(out, in_, s1, s2, o0, o1), reads, writes)

    def tt(out, x, y, o, reads, writes):
        op("v", lambda e: e.tensor_tensor(out, x, y, o), reads, writes)

    def copy(q, out, in_, reads, writes):
        if q == "v":
            op("v", lambda e: e.tensor_copy(out, in_), reads, writes)
        else:
            act(out, in_, reads, writes)

    def affine(q, out, in_, scale, bias, reads, writes):
        if q == "v":
            ts(out, in_, scale, bias, A.mult, A.add, reads, writes)
        else:
            act(out, in_, reads, writes, F.Identity, scale=scale, bias=bias)

    dmas([("y", T.RI[:], T.ring0[:])], [], [full("RI")])
    dmas([("s", T.EUI[:], T.eu[:])], [], [full("EUI")])
    dmas([("s", T.EVI[:], T.ev[:])], [], [full("EVI")])
    dmas([("y", T.TB0[:, own:own + V], T.m0[:, own:own + V])], [], [("TB0", own, own + V)])

    one = T.ONE[:, 0:128]
    wide = 528 if WHO["za"] == "g" else 256
    step("one")
    op("v", lambda e: e.memset(T.ONE[:, 0:wide], 1.0), [], [full("ONE")])
    step("rows")
    op("g", lambda e: e.iota(T.PC[:, 0:1], [[0, 1]], 0, 1), [], [("PC", 0, 1)])
    iota("RQ", [[1, 16]])
    iota("XL", [[1, 272]], -16)

    names = ["p", "odd", "lo", "hi", "g16", "p4", "even", "tie", "wy", "wz", "py", "pv", "lift"]
    col = {n: T.CF[:, i:i + 1] for i, n in enumerate(names)}
    reg = {n: ("CF", i, i + 1) for i, n in enumerate(names)}

    def column(name, src, scale, bias, rd=None):
        step("c" + name)
        x, rd = (col[src], reg[src]) if rd is None else (src, rd)
        named = isinstance(bias, str)
        affine(WHO.get("c" + name, "s"), col[name], x, scale, col[bias] if named else bias, [rd] + [reg[bias]] * named if named else [rd], [reg[name]])

    step("cols")
    bits = ((0, 1), (0, 3), (2, 3), (0, 112), (0, 124))[:5 if WHO["za"] == "v" else 4]
    for i, (sh, m) in enumerate(bits):
        ts(T.PC[:, i + 1:i + 2], T.PC[:, 0:1], sh, m, A.logical_shift_right, A.bitwise_and, [("PC", 0, 1)], [("PC", i + 1, i + 2)])
    copy("v", T.CF[:, 0:len(bits) + 1], T.PC[:, 0:len(bits) + 1], [("PC", 0, 8)], [("CF", 0, 6)])
    rest = [(a, b) for a, b in ((0, own), (own + V, 4 * V)) if a < b]
    dmas([("y", T.TB0[:, a:b], T.m0[:, a:b]) for a, b in rest], [("PC", 4, 5)] * LATE, [("TB0", a, b) for a, b in rest])
    step("qh")
    ts(T.QH[:], T.RQ[:], col["odd"], -1.0, A.mult, A.mult, [full("RQ"), reg["odd"]], [full("QH")])
    step("cj")
    ts(T.CJ[:], T.RQ[:, 0:4], col["lo"], None, A.is_equal, None, [full("RQ"), reg["lo"]], [full("CJ")])
    step("tie")
    ts(col["tie"], col["lo"], col["hi"], -0.5, A.is_lt, A.add, [reg["lo"], reg["hi"]], [reg["tie"]])
    step("ceven")
    ts(col["even"], T.CJ[:, 0:1], T.CJ[:, 2:3], 0.25, A.subtract, A.mult, [full("CJ")], [reg["even"]])
    column("wz", "odd", -32.0, "even")
    if WHO["y2"] == "v":
        column("py", "hi", 1.0, "g16")
        step("cwy")
        ts(col["wy"], T.CJ[:, 1:2], HIGH / LOW, T.CJ[:, 0:1], A.mult, A.add, [full("CJ")], [reg["wy"]])
    if WHO["lv"] == "v":
        column("pv", "lo", 4.0, "g16")
        step("ca")
        ts(T.CA[:], T.RQ[:, 0:4], col["hi"], None, A.is_equal, None, [full("RQ"), reg["hi"]], [full("CA")])
    column("lift", T.CJ[:, 1:2], LIFT / LOW, 0.0, full("CJ"))

    def match(out, wr, shift, n, at, w=None, rw=()):
        rd = [full("XL"), reg[at]] + list(rw)
        ts(out, T.XL[:, 16 - shift:16 - shift + n], col[at], w, A.is_equal, None if w is None else A.mult, rd, [wr])

    step("za")
    if WHO["za"] == "g":
        sel(T.ZA[:], T.ONE[:], [[-1, 4], [-4, 33], [1000, 4]], A.is_equal, -1000, [full("ONE")], [full("ZA")])
    else:
        for a in range(4):
            match(T.ZA[:, a, :], ("ZA", 132 * a, 132 * a + 132), 1, 132, "p4", T.CJ[:, a:a + 1], [full("CJ")])
    step("id")
    if WHO["id"] == "g":
        sel(T.ID[:], one, [[-1, 128]], A.is_equal, 0, [full("ONE")], [full("ID")])
    else:
        match(T.ID[:], full("ID"), 0, 128, "p")
    step("y2")
    if WHO["y2"] == "v":
        match(T.Y2[:], full("Y2"), 12, 144, "py", col["wy"], [reg["wy"]])
    step("zb")
    match(T.ZB[:], full("ZB"), 15, 144, "g16", col["wz"], [reg["wz"]])
    step("bo")
    iota("B1", [[16, 8], [0, 4]])
    ts(T.BO[:], T.B1[:], col["g16"], None, A.is_equal, None, [full("B1"), reg["g16"]], [full("BO")])
    step("ld")
    iota("B3", [[16, 9], [1000, 4], [0, 4]], -3000)
    for j in range(1, 4):
        step("ld%d" % j)
        r = ("LD", 128 * j - 128, 128 * j)
        ts(T.LD[:, j - 1, :], T.B3[:, 12 - 4 * j:140 - 4 * j], col["g16"], None, A.is_equal, None, [full("B3"), reg["g16"]], [r])
        step("le%d" % j)
        tt(T.LD[:, j - 1, j::4], T.LD[:, j - 1, j::4], T.BO[:], A.subtract, [r, full("BO")], [r])

    def blocks(out, tmp, src, n):
        step("lc1")
        sel(T[tmp][:], T[src][:, 0:128], [[-n, 128 // n], [0, n]], A.is_ge, 0, [full(src)], [full(tmp)])
        step("lc2")
        sel(T[out][:], T[tmp][:], [[n, 128 // n], [0, n]], A.is_ge, n - 1, [full(tmp)], [full(out)], cm=-1)

    def marks(name, out, pat, base, values):
        step(name)
        src = "ZR"
        for j, x in enumerate(values):
            sel(T[out][:], T[src][:], pat, A.not_equal, base - j, [full(src)], [full(out)], x)
            src = out

    step("zr")
    iota("ZR", [[0, 144]])
    if WHO["y2"] == "g":
        marks("y2", "Y2", [[-16, 9], [1000, 4], [-4, 4]], -3000, (1.0, HIGH / LOW))
    marks("y1", "Y1", [[-4, 36], [1000, 4]], -3000, (LOW, HIGH))
    step("rs")
    op("g", lambda e: e.iota(T.RS[:, 0:256], [[0, 64], [32, 4]], -16, 0, allow_small_or_imprecise_dtypes=True), [], [("RS", 0, 256)])
    dmas([("y", T.RS[:, c:c + 256], T.RS[:, 0:256]) for c in (256, 512, 768)], [("RS", 0, 256)], [("RS", 256, 1024)])
    step("lv")
    for z in range(4):
        if WHO["lv"] == "g":
            sel(T.LV[:, z, :], T.ONE[:, 0:144], [[-16, 9], [-1, 4], [1000, 4]], A.is_equal, -1000 - 4 * z, [full("ONE")], [("LV", 144 * z, 144 * z + 144)])
        else:
            match(T.LV[:, z, :], ("LV", 144 * z, 144 * z + 144), 1, 144, "pv", T.CA[:, z:z + 1], [full("CA")])
    step("lc")
    iota("NM", [[0, 32], [-1, 2], [0, 2]], 1)
    blocks("LC", "B2", "NM", 4)

    for a in range(4):
        step("sv%d" % a)
        sel(T.SV[:, a, :], T.NM[:], [[-16, 8], [0, 8], [-1, 2]], A.is_equal, -4 * a, [full("NM")], [("SV", 128 * a, 128 * a + 128)])

    def digits(name, buf, c0, n):
        step(name)
        affine(WHO[name], T[buf][:, c0:c0 + 256], T.XL[:, 16:272], T.CJ[:, 0:1], T.QH[:, n:n + 1], [full("XL"), full("CJ"), ("QH", n, n + 1)], [(buf, c0, c0 + 256)])

    for n in range(4):
        digits("ll%d" % n, "LL", 256 * n, n)
    for n in range(2):
        digits("pz%d" % n, "PZ", 256 * n, n + 4)
    for b in range(1, NB):
        step("hb%d" % b)
        if WHO["hb%d" % b] == "v":
            op("v", lambda e, b=b: e.memset(T.HB[:, b - 1, :], -2.0 * b), [], [("HB", HW * b - HW, HW * b)])
        else:
            op("g", lambda e, b=b: e.iota(T.HB[:, b - 1, :], [[0, HW]], -2 * b, 0, allow_small_or_imprecise_dtypes=True), [], [("HB", HW * b - HW, HW * b)])
    step("ni")
    if WHO["ni"] == "v":
        match(T.NI[:], full("NI"), 0, 128, "p", -1.0)
    else:
        affine(WHO["ni"], T.NI[:], T.ID[:], -1.0, 0.0, [full("ID")], [full("NI")])
    step("eu16")
    copy("v", T.EU16[:], T.EUI[:], [full("EUI")], [full("EU16")])

    def place_scatter(b, h):
        step(pre[0] + "scat%d" % h)
        e0, e1 = ((0, SCAT[b]), (SCAT[b], E))[h]
        if e0 == e1:
            return
        src, rd = T.PZ[:, e0:e1], [("PZ", e0, e1), ("EU16", 0, 128)]
        dst = T.LL[:, 0:V].indirect(T.EU16[:, 32 * b + e0 // 16:32 * b + e1 // 16])
        if b:
            op("v", lambda e: e.tensor_tensor(dst, src, T.HB[:, b - 1, 0:e1 - e0], A.add), rd + [("HB", HW * b - HW, HW * b)], [("LL", 0, V)], waw=True)
        else:
            op("v", lambda e: e.tensor_copy(dst, src), rd, [("LL", 0, V)], waw=True)

    def place_next(b):
        for i, (c0, c1) in enumerate(NEXT[b]):
            name = ("pn%d" if b else "ipn%d") % i
            step(name)
            q = WHO[name]
            l0 = 32 * b + 32
            copy(q, T.LL[:, V + c0:V + c1], T.LL[:, 0:V].indirect(T.EU16[:, l0 + c0 // 16:l0 + c1 // 16]), [("LL", 0, V), ("EU16", 0, 128)], [("LL", V + c0, V + c1)])

    def place_mm(part, lx):
        c0, n = (0, V, 0)[part], (64, 32, 96)[part]
        for i in range(16):
            step(None, "pm1b" if part and i >= 8 else "pm1" if part else pre[0] + "pm0")
            mm(T[lx][:, 0:n], T.ZB[:, 15 - i:143 - i], T.LL[:, c0 + i:c0 + 16 * n:16], i == 0, i == 15, [full("ZB"), ("LL", c0, c0 + 16 * n)], [(lx, 0, n)])

    def place_out(b, part, lx):
        step(("po", "pnout", "po")[part])
        o, n, c0 = "LW%d" % b, (64, 32, 96)[part], (0, 64, 0)[part]
        copy("v", T[o][:, c0:c0 + n], T[lx][:, 0:n], [(lx, 0, n)], [(o, c0, c0 + n)])

    def ring_list(b, h):
        cx, of, (e0, e1) = "CX%d" % (0 if JOIN[b] else h), "OF%d" % b, RINGS[h]
        lu, l0, n = ("EU16", 0, V) if b == 0 else ("LW%d" % (b - 1), 64, V + E * b)
        l0, l1 = l0 + e0 // 16, l0 + e1 // 16
        step(pre[0] + "rg%d" % h, pre[0] + "rs%d" % h)
        act(T.GR[:, e0:e1], T.RW[:, 0:n].indirect(T[lu][:, l0:l1]), [("RW", 0, n), (lu, l0, l1)], [("GR", e0, e1)], F.Abs)
        for a in range(4):
            mm(T[cx][:, e0 // 4:e1 // 4], T.Y2[:, 12 - 4 * a:140 - 4 * a], T.GR[:, e0 + a:e1:4], a == 0, a == 3, [full("Y2"), ("GR", e0, e1)], [(cx, e0 // 4, e1 // 4)])
        if JOIN[b] and not h:
            return
        c0, c1 = 0 if JOIN[b] else e0 // 4, e1 // 4
        step(pre[0] + "ro%d" % h)
        ts(T[of][:, c0:c1], T[cx][:, c0:c1], LOW, None, A.mult, None, [(cx, c0, c1)], [(of, c0, c1)])

    def memory(q, b, out, src, reads, writes):
        if q == "s":
            act(out, src, reads, writes, F.Relu, **({"bias": 15.0, "scale": -1.0} if b else {}))
        elif b:
            ts(out, src, 15.0, -1.0, A.min, A.mult, reads, writes)
        else:
            ts(out, src, -15.0, None, A.add, None, reads, writes)

    def part(b, h):
        e = SLOTS[b][0][2]
        return ((0, e), (e, E))[h]

    def wadd(b, w, src, h, start, stop=False):
        e0, e1 = part(b, h)
        mm(T["W%d" % h][:, 0:e1 - e0], T[w][:], T[src][:, e0:e1], start, stop, [full(w), (src, e0, e1)], [("W%d" % h, 0, e1 - e0)])

    def mem_u(b):
        step(pre[0] + "u")
        tb = "TB%d" % b
        for q, (e0, e1) in (("s", part(b, 1)), ("v", part(b, 0))) if UV[b] else (("s", (0, E)),):
            memory(q, b, T.MU[:, e0:e1], T[tb][:, own:own + V].indirect(T.EU16[:, 32 * b + e0 // 16:32 * b + e1 // 16]), [(tb, own, own + V), ("EU16", 0, 128)], [("MU", e0, e1)])
        for h in range(2):
            step(None, pre[0] + "wu%d" % h)
            wadd(b, "ID", "MU", h, True)

    def mem_v(b):
        step("v", "wv")
        tb, mv = "TB%d" % b, "MV%d" % (b % 2)
        memory("s", b, T[mv][:], T[tb][:].indirect(T.EV16[:, 32 * b:32 * b + 32]), [full(tb), ("EV16", 0, 128)], [full(mv)])
        for h in range(2):
            wadd(b, "ID", mv, h, False, bool(h and SUB[b]))

    def send(b, c0, c1, final):
        tb = "TB%d" % (b + 1)
        ap = T[tb][:, own + c0:own + c1]
        mask = topo.mask(core, peers[0])
        ids = []
        for p in peers:
            rid, pid, _ = topo.addr(p)
            mask &= topo.mask(core, p)
            ids.append(DstId(rid=rid, pnc=pid))
        ne = bin(mask).count("1")

        def call():
            g.remote_dma_fused([RemoteDMATransfer(dst_ids=ids, dma_engine_mask=mask, remote_sem=T.sem["arr%d" % b],
                                                  srcs=[ap], dsts=[ap] * len(ids))], local_sem=T.sem.sent)
            total["sent"] = total.get("sent", 0) + ne

        def arrive():
            total["arr%d" % b] = len(SENDS[b]) * ne * len(peers)
            for p in peers:
                o = T.rank_of(p) * V
                note("far", ("arr%d" % b, total["arr%d" % b], {}), [], [(tb, o, o + V)])

        item(q="g", kind="send", fn=call, reads=[(tb, own + c0, own + c1)], writes=[("sends%d" % b, c0, c1)])
        if final:
            item(q="far", kind="far", fn=arrive, reads=[("sends%d" % b, 0, V)], writes=[(tb, T.rank_of(p) * V, T.rank_of(p) * V + V) for p in peers])

    def split(name, src, tmp, dst, n):
        step(name + "and")
        ts(T[tmp][:], T[src][:], 31, None, A.bitwise_and, None, [full(src)], [full(tmp)])
        step(name + "hi")
        ts(T[dst][:, n:2 * n], T[src][:], 1 / HIGH, (LIFT - 0.5 + 1 / 64) / LOW, A.mult, A.add, [full(src)], [(dst, n, 2 * n)])
        step(name + "lo")
        ts(T[dst][:, 0:n], T[tmp][:], 1 / LOW, None, A.mult, None, [full(tmp)], [(dst, 0, n)])

    split("r", "RI", "RJ", "RD", 256)
    dmas([("y", T.OB[:, 0:V], T.m0[:, own:own + V])], [full("RD")], [("OB", 0, V)])
    step(None, "rw")
    four = ("DA0", "DA1", "LX", "LN")
    for j in (1, 0):
        for a, bk in enumerate(four):
            mm(T[bk][:, 0:256], T.ZA[:, a, 1 - j:129 - j], T.RD[:, 256 * j:256 * j + 256], j == 1, j == 0, [full("ZA"), ("RD", 256 * j, 256 * j + 256)], [(bk, 0, 256)])
    for a, bk in enumerate(four):
        step("rw%d" % a)
        affine(WHO["rw%d" % a], T.RW[:, 256 * a:256 * a + 256], T[bk][:, 0:256], -1.0, col["lift"], [(bk, 0, 256), reg["lift"]], [("RW", 256 * a, 256 * a + 256)])
    ring_list(0, 0)
    ring_list(0, 1)
    place_scatter(0, 0)
    place_scatter(0, 1)
    step("ev16")
    copy("v", T.EV16[:], T.EVI[:], [full("EVI")], [full("EV16")])
    split("v", "EVI", "EVJ", "EVD", 128)
    step("vw")
    for z in range(4):
        for j in range(2):
            mm(T.LN[:, z::4], T.LV[:, z, 1 - j:129 - j], T.EVD[:, 128 * j:128 * j + 128], j == 0, j == 1, [("LV", 144 * z, 144 * z + 144), full("EVD")], [full("LN")])
    step("vw")
    affine(WHO["vw"], T.VW[:], T.LN[:], -1.0, col["lift"], [full("LN"), reg["lift"]], [full("VW")])
    if not ONEPM[0]:
        place_mm(0, "DA1")
    mem_u(0)
    pre[0] = ""

    for b in range(NB):
        last = b == NB - 1
        tb, mt, mv, of = "TB%d" % b, "MT%d" % (b % 2), "MV%d" % (b % 2), "OF%d" % b
        step(None, None, b)

        def slots(i, q, e0, e1):
            step("s%d" % i)
            memory(q, b, T[mt][:, 4 * e0:4 * e1], T[tb][:].indirect(T[of][:, e0 // 4:e1 // 4]), [full(tb), (of, e0 // 4, e1 // 4)], [(mt, 4 * e0, 4 * e1)])

        def largest(i, e0, e1):
            step("m%d" % i)
            for e in range(e0, e1, 256):
                s = (4 * e, 4 * min(e + 256, e1))
                op("v", lambda q, s=s, mt=mt: q.tensor_tensor_scan(T.MX[:, s[0]:s[1]], T.RS[:, 0:s[1] - s[0]], T[mt][:, s[0]:s[1]], 0.0, A.min, A.max),
                   [("RS", 0, s[1] - s[0]), (mt,) + s], [("MX",) + s])

        def clip(h):
            step("clip%d" % h, "ws%d" % h)
            e0, e1 = part(b, h)
            s, o, w, n = (4 * e0, 4 * e1), V + E * b + e0, "W%d" % h, e1 - e0
            if h and SUB[b]:
                tt(T.OB[:, o:o + n], T[w][:, 0:n], T.MX[:, s[0] + 3:s[1]:4], A.subtract, [("MX",) + s, (w, 0, n)], [("OB", o, o + n)])
                return
            mm(T[w][:, 0:n], T.NI[:], T.MX[:, s[0] + 3:s[1]:4], False, True, [full("NI"), ("MX",) + s], [(w, 0, n)])
            affine("s", T.OB[:, o:o + n], T[w][:, 0:n], 1.0, 0.0 if h or UV[b] else -15.0, [(w, 0, n)], [("OB", o, o + n)])

        def where(h, j):
            return (("DA%d" % h, 0), ("DA%d" % h, 256), ("CX%d" % h, 256))[j]

        def diff(h):
            s = (1024 * h, 1024 * h + 1024)
            for j in (2, 0, 1):
                step(None, "de"[j < 2] + "%d" % h)
                bk, d = where(h, j)
                for w, k in (("ID", j + 1), ("NI", 0)):
                    mm(T[bk][:, d:d + 256], T[w][:], T[mt][:, s[0] + k:s[1]:4], w == "ID", w == "NI", [full(w), (mt,) + s], [(bk, d, d + 256)])

        def lowest(h):
            step("p%d" % h, "cd%d" % h)
            for j in (2, 0, 1):
                bk, d = where(h, j)
                p = 256 * (3 * h + j)
                tt(T.PR[:, p:p + 256], T[bk][:, d:d + 256], T[mv][:, 256 * h:256 * h + 256], A.mult, [(bk, d, d + 256), full(mv)], [("PR", p, p + 256)])
            cx = "CX%d" % h
            for i, j in enumerate((2, 0, 1)):
                p = 256 * (3 * h + j)
                mm(T[cx][:, 0:256], T.LD[:, j, :], T.PR[:, p:p + 256], i == 0, i == 2, [full("LD"), ("PR", p, p + 256)], [(cx, 0, 256)])
            sign(h, cx)

        def wide_diff(h):
            for j, bk in enumerate(("DA0", "CX0", "DA1")):
                step(None, "d%d%d" % (j, h))
                for w, k in (("ID", j + 1), ("NI", 0)):
                    mm(T[bk][:, 256 * h:256 * h + 256], T[w][:], T[mt][:, 1024 * h + k:1024 * h + 1024:4], w == "ID", w == "NI",
                       [full(w), (mt, 1024 * h, 1024 * h + 1024)], [(bk, 256 * h, 256 * h + 256)])

        def wide_lowest():
            for j, bk in enumerate(("DA0", "CX0", "DA1")):
                for i, (e0, e1) in enumerate(((0, 256), (256, E)) if j == 2 and WIDE[b] == 2 else ((0, E),)):
                    step("p%d" % (j + i))
                    tt(T.PR[:, E * j + e0:E * j + e1], T[bk][:, e0:e1], T[mv][:, e0:e1], A.mult, [(bk, e0, e1), full(mv)], [("PR", E * j + e0, E * j + e1)])
                for h, cx in enumerate(("CX1", "W1")):
                    step(None, "cd%d%d" % (j, h))
                    p = E * j + 256 * h
                    mm(T[cx][:, 0:256], T.LD[:, j, :], T.PR[:, p:p + 256], j == 0, j == 2, [full("LD"), ("PR", p, p + 256)], [(cx, 0, 256)])
            for h, cx in enumerate(("CX1", "W1")):
                sign(h, cx)

        def sign(h, cx):
            step("sg%d" % h)
            rd, wr = [(cx, 0, 256), reg["tie"]], [("SG", 256 * h, 256 * h + 256)]
            if SIGN[b][h] == "s":
                act(T.SG[:, 256 * h:256 * h + 256], T[cx][:, 0:256], rd, wr, F.Relu, bias=col["tie"])
            else:
                ts(T.SG[:, 256 * h:256 * h + 256], T[cx][:, 0:256], col["tie"], 0.0, A.add, A.is_gt, rd, wr)

        def renew(h):
            step(None, "of%d" % h)
            w, c0, s, o = ("LN", "LX")[h], 128 * b + 64 * h, 256 * h, V + E * b + 256 * h
            for a in range(4):
                mm(T[w][:, 256 + a:512:4], T.SV[:, a, :], T.VW[:, c0:c0 + 64], a == 0, False, [("SV", 128 * a, 128 * a + 128), full("VW")], [(w, 256, 512)])
            step("rn%d" % h, "ct%d" % h)
            mm(T[w][:, 256:512], T.LC[:], T.SG[:, s:s + 256], False, True, [full("LC"), ("SG", s, s + 256)], [(w, 256, 512)])
            tt(T.RW[:, o:o + 256], T[w][:, 256:512], T.GR[:, s:s + 256], A.min, [(w, 256, 512), ("GR", s, s + 256)], [("RW", o, o + 256)])

        mem_v(b)
        for i, (q, e0, e1) in enumerate(SLOTS[b]):
            slots(i, q, e0, e1)
        for i, (q, e0, e1) in enumerate(SLOTS[b]):
            largest(i, e0, e1)
        if ONEPM[b]:
            place_next(b)
            place_mm(2, "DA1")
            place_out(b, 2, "DA1")
        else:
            place_out(b, 0, "DA1")
            if not last:
                place_next(b)
        for h in range(2):
            clip(h)
            (wide_diff if WIDE[b] else diff)(h)
        if not last and not ONEPM[b]:
            place_mm(1, "W0")
            place_out(b, 1, "W0")
        n, lw = V + E * (b + 1), "LW%d" % b
        if not last:
            nx = "TB%d" % (b + 1)
            for i, (q, c0, c1) in enumerate(PIECES[b]):
                step("blk%d" % i)
                out, src, rd, wr = T[nx][:, own + c0:own + c1], T.OB[:, 0:n].indirect(T[lw][:, c0 // 16:c1 // 16]), [("OB", 0, n), (lw, 0, 64)], [(nx, own + c0, own + c1)]
                act(out, src, rd, wr, F.Relu, bias=15.0, scale=-1.0)
            for i, (c0, c1) in enumerate(SENDS[b]):
                step("send%d" % i)
                send(b, c0, c1, (c0, c1) == SENDS[b][-1])
        if WIDE[b]:
            wide_lowest()
        for h in range(2):
            if not WIDE[b]:
                lowest(h)
            renew(h)
        if not last:
            mem_u(b + 1)
            place_scatter(b + 1, 0)
            place_scatter(b + 1, 1)
            for h in range(2):
                ring_list(b + 1, h)
            if not ONEPM[b + 1]:
                place_mm(0, "DA1")

    for i, (q, c0, c1) in enumerate(YRINGS):
        step("yg%d" % i)
        copy(q, T.YG[:, c0:c1], T.RW[:, 0:n].indirect(T[lw][:, c0 // 16:c1 // 16]), [("RW", 0, n), (lw, 0, 64)], [("YG", c0, c1)])
    step("yr")
    for i, a in enumerate(YORDER):
        mm(T.DA0[:, 0:256], T.Y1[:, 3 - a:131 - a], T.YG[:, 256 * a:256 * a + 256], i == 0, i == 3, [full("Y1"), ("YG", 256 * a, 256 * a + 256)], [("DA0", 0, 256)])
    act(T.YR[:], T.DA0[:, 0:256], [("DA0", 0, 256)], [full("YR")], F.Abs)
    outs = {"yr": (T.yr[:], T.YR[:], full("YR"))}
    for i, (q, c0, c1) in enumerate(YPIECES):
        step("blk%d" % i)
        out, src, rd, wr = T.YB[:, c0:c1], T.OB[:, 0:n].indirect(T[lw][:, c0 // 16:c1 // 16]), [("OB", 0, n), (lw, 0, 64)], [("YB", c0, c1)]
        if q == "s":
            act(out, src, rd, wr, F.Relu)
            step("top%d" % i)
            ts(out, out, 15.0, None, A.min, None, wr, wr)
        else:
            ts(out, src, 0.0, 15.0, A.max, A.min, rd, wr)
        outs["ym%d" % i] = (T.ym[:, c0:c1], out, wr[0])
    for q, name in OUTS:
        dmas([(q,) + outs[name][0:2]], [outs[name][2]], [])
    for j in plan():
        emit(prog[j])
    for s in total:
        if waited.get(s, 0) < total[s]:
            g.wait_ge(T.sem[s], total[s])
